import numpy as np
import ml_dtypes


def mxq(x, axis, fmt="e4m3"):
    dtype, down = {"e4m3": (ml_dtypes.float8_e4m3fn, 7), "e5m2": (ml_dtypes.float8_e5m2, 14)}[fmt]
    v = np.moveaxis(np.asarray(x, np.float32).astype(ml_dtypes.bfloat16).astype(np.float64), axis, -1)
    blocks = v.reshape(v.shape[:-1] + (-1, 32))
    amax = np.abs(blocks).max(-1, keepdims=True)
    byte = np.maximum(np.where(amax > 0, np.frexp(amax)[1] - 1 + 127, 0) - down, 1)
    scale = np.exp2(byte - 127.0)
    codes = (blocks / scale).astype(np.float32).astype(dtype).astype(np.float64)
    return np.moveaxis((codes * scale).reshape(v.shape), -1, axis)


WIDE = False


def mx_kscale(k):
    if not WIDE:
        return np.ones(k)
    levels = np.array([10, -10, 5, -5, 0])
    if k % 512:
        return np.exp2(np.random.permutation(np.resize(levels, k // 32))).repeat(32)
    a = np.empty((k // 512, 16))
    for p in range(k // 512):
        a[p, :8] = np.random.permutation(np.resize(levels, 8))
        for g in range(8):
            far = levels[np.abs(levels - a[p, g]) >= 10]
            a[p, g + 8] = far[np.random.randint(len(far))]
    return np.exp2(a.ravel()).repeat(32)


def f64(x):
    return np.asarray(x).astype(np.float64)


def striped(idx):
    return np.tile(idx.reshape(-1, 16).T, (8, 1)).astype(np.uint16)


def unstriped(offs):
    return offs[:16].T.reshape(-1).astype(np.int64)


E2M1 = np.array([0.0, 0.5, 1.0, 1.5, 2.0, 3.0, 4.0, 6.0, -0.0, -0.5, -1.0, -1.5, -2.0, -3.0, -4.0, -6.0])


def pack_weight(w, fmt):
    k, n = w.shape
    w = f64(np.asarray(w, np.float32).astype(ml_dtypes.bfloat16)).reshape(k // 32, 32, n)
    amax = np.abs(w).max(1)
    if fmt == "e4m3":
        byte = np.frexp(amax)[1] - 1 + 127 - 7
    else:
        mant, ex = np.frexp(amax / 6.0)
        byte = np.where(mant > 0.5, ex, ex - 1) + 127
    byte = np.clip(np.where(amax > 0, byte, 1), 1, 254)
    scaled = (w * np.exp2(127.0 - byte)[:, None, :]).reshape(k, n).astype(np.float32)
    by_word = np.ascontiguousarray(scaled.reshape(k // 512, 128, 4, n).transpose(0, 1, 3, 2))
    if fmt == "e4m3":
        words = by_word.astype(ml_dtypes.float8_e4m3fn).view(np.uint8)
    else:
        c = by_word.astype(ml_dtypes.float4_e2m1fn).view(np.uint8) & 0xF
        words = (c[..., 0::2] | (c[..., 1::2] << 4)).reshape(k // 512, 128, 2 * n)
    return np.ascontiguousarray(words), np.ascontiguousarray(byte.astype(np.uint8).reshape(k // 512, 16, n))


def unpack_weight(words, scales, fmt):
    g, _, n = scales.shape
    words = np.ascontiguousarray(words).reshape(g, 128, n, -1)
    if fmt == "e4m3":
        vals = words.view(ml_dtypes.float8_e4m3fn).astype(np.float64)
    else:
        nib = np.empty((g, 128, n, 4), np.uint8)
        nib[..., 0::2] = words & 0xF
        nib[..., 1::2] = words >> 4
        vals = E2M1[nib]
    vals = vals * np.repeat(np.exp2(scales.astype(np.float64) - 127.0), 8, axis=1)[..., None]
    return vals.transpose(0, 1, 3, 2).reshape(g * 512, n)


def gelu(v):
    return 0.5 * v * (1.0 + np.tanh(np.sqrt(2.0 / np.pi) * (v + 0.044715 * v**3)))


K, H, N, T, S, P = 1024, 1024, 384, 4096, 1024, 512

def setup_inputs():
    n = np.random.standard_normal
    s = mx_kscale(K)[:, None]
    u = mx_kscale(H)[:, None]
    tab_words, tab_scales = pack_weight(n((K, T)) * s, "e4m3")
    w1_words, w1_scales = pack_weight(n((K, H)) / np.sqrt(K) / s, "e2m1")
    w2 = (n((K, H)) / np.sqrt(K) / s * u.T).astype(np.float32)
    w3_words, w3_scales = pack_weight(n((H, N)) / np.sqrt(H) / u, "e4m3")
    return {
        "tab_words": tab_words, "tab_scales": tab_scales,
        "offs": striped(np.random.permutation(T)[:S]),
        "pos1": striped(np.random.permutation(S)[:P]),
        "pos2": striped(np.random.permutation(S)[:P]),
        "pos3": striped(np.random.permutation(S)[:P]),
        "w1_words": w1_words, "w1_scales": w1_scales,
        "w2": w2,
        "w3_words": w3_words, "w3_scales": w3_scales,
        "period": n(N).astype(np.float32),
    }

def reference(tab_words, tab_scales, offs, pos1, pos2, pos3, w1_words, w1_scales, w2, w3_words, w3_scales, period):
    v = unpack_weight(tab_words, tab_scales, "e4m3")[:, unstriped(offs)]
    w1 = unpack_weight(w1_words, w1_scales, "e2m1")
    w3 = unpack_weight(w3_words, w3_scales, "e4m3")
    x1 = w1.T @ v
    x2 = mxq(f64(w2), 0, "e4m3").T @ v
    anc = np.tanh(x1[:, unstriped(pos1)])
    dau = x2[:, unstriped(pos2)]
    loan = x2[:, unstriped(pos3)]
    z = anc * dau + loan
    y = w3.T @ mxq(z, 0, "e4m3")
    return y + f64(period)[:, None]

@@ -1,0 +1,240 @@
+from contextlib import ExitStack
+
+import concourse.mybir as mybir
+
+K, H, N, T, S, M = 1024, 1024, 384, 4096, 1024, 512
+FLOPS = 2 * (2 * K * H * S + H * N * M)
+
+F32 = mybir.dt.float32
+BF16 = mybir.dt.bfloat16
+I32 = mybir.dt.int32
+U32 = mybir.dt.uint32
+U16 = mybir.dt.uint16
+U8 = mybir.dt.uint8
+FP8X4 = mybir.dt.float8_e4m3fn_x4
+FP4X4 = mybir.dt.float4_e2m1fn_x4
+ACT = mybir.ActivationFunctionType
+ALU = mybir.AluOpType
+
+P = 128
+PACK = 4
+PASS = 512
+BANK = 512
+HALF = M // 2
+AFFINE_ON_SCALAR = ()
+
+
+def tile_list_sound_change_dating_kernel(
+    tc, tab_words, tab_scales, offs, pos1, pos2, pos3, w1_words, w1_scales, w2, w3_words, w3_scales, period, out
+):
+    nc = tc.nc
+    with ExitStack() as ctx:
+        keep = ctx.enter_context(tc.tile_pool(name="keep", bufs=1))
+        ring = ctx.enter_context(tc.tile_pool(name="ring", bufs=1))
+        psum = ctx.enter_context(tc.psum_pool(name="psum", bufs=4))
+
+        def held(shape, dtype, name):
+            return keep.tile(shape, dtype, name=name, align_bytes=64)
+
+        def bank(tag):
+            return psum.tile([P, BANK], F32, name=tag)
+
+        idx = keep.tile([P, S // 16], U16, name="idx")
+        p1 = keep.tile([P, M // 16], U16, name="p1")
+        p2 = keep.tile([P, M // 16], U16, name="p2")
+        p3 = keep.tile([P, M // 16], U16, name="p3")
+
+        tab_s = held([P, T], U8, "tab_s")
+        w1_s_raw = held([P, H], U8, "w1_s_raw")
+        planes = [held([P, S + H + N], U8, f"plane{a}") for a in range(2)]
+        v_cols, w1_cols, w3_cols = slice(0, S), slice(S, S + H), slice(S + H, S + H + N)
+        for rows in (slice(32, 64), slice(64, P)):
+            nc.vector.memset(w1_s_raw[rows, :].bitcast(I32), 0)
+            nc.vector.memset(tab_s[rows, :].bitcast(I32), 0)
+            nc.vector.memset(planes[0][rows, w3_cols].bitcast(I32), 0)
+        nc.vector.memset(planes[1][:].bitcast(I32), 0)
+        warm = held([P, 2], F32, "warm")
+        nc.vector.memset(warm[:, 0:1], 0.0)
+        nc.scalar.activation(warm[:, 1:2], warm[:, 0:1], ACT.Sigmoid)
+
+        nc.sync.dma_start(idx[:], offs)
+        for dst, src in ((tab_s[:32, :], tab_scales), (w1_s_raw[:32, :], w1_scales), (planes[0][:32, w3_cols], w3_scales)):
+            nc.sync.dma_start(dst.bitcast(I32), src.rearrange("a q c -> (a q) c").bitcast(I32))
+        w1_raw = held([P, 2, 2 * H], U8, "w1_raw")
+        nc.sync.dma_start(w1_raw[:].bitcast(I32), w1_words.rearrange("a p c -> p a c").bitcast(I32))
+        tab_w = []
+        for a in range(2):
+            words = held([P, T], I32, f"tab_w{a}")
+            nc.sync.dma_start(words[:], tab_words[a].rearrange("p t i -> p (t i)").bitcast(I32))
+            tab_w.append(words)
+
+        w2_pieces = [(0, 0, 0, PASS), (0, 1, 0, PASS // 2), (0, 1, PASS // 2, PASS), (1, 0, 0, PASS), (1, 1, 0, PASS)]
+        w2_raw = {}
+        for b, a, c0, c1 in w2_pieces:
+            raw = held([P, PACK, c1 - c0], F32, f"w2_raw{b}{a}{c0}")
+            rows = w2[PASS * a : PASS * (a + 1), PASS * b + c0 : PASS * b + c1]
+            nc.sync.dma_start(raw[:], rows.rearrange("(p j) c -> p j c", j=PACK))
+            w2_raw[b, a, c0] = raw
+            if (b, a) == (0, 0):
+                nc.sync.dma_start(p1[:], pos1)
+                nc.sync.dma_start(p2[:], pos2)
+                nc.sync.dma_start(p3[:], pos3)
+
+        w3_w = held([P, 2, N], I32, "w3_w")
+        nc.sync.dma_start(w3_w[:], w3_words.rearrange("a p c i -> p a (c i)").bitcast(I32))
+        prior = held([P, N // P], F32, "prior")
+        with nc.allow_non_contiguous_dma(reason="one value of period to a partition"):
+            nc.sync.dma_start(prior[:], period.rearrange("(c p) -> p c", p=P))
+
+        nc.vector.tensor_copy(
+            planes[0][:, w1_cols].rearrange("p (b t m) -> p b t m", b=2, t=PACK),
+            w1_s_raw[:].rearrange("p (b m t) -> p b t m", b=2, t=PACK),
+        )
+        v_s_raw = held([P, S], U8, "v_s_raw")
+        nc.vector.tensor_copy(v_s_raw[:], tab_s[:].indirect(idx[:]))
+        nc.vector.tensor_copy(planes[0][:, v_cols].bitcast(I32), v_s_raw[:].bitcast(I32))
+        for a in range(2):
+            for q in range(4):
+                if (a, q) != (0, 0):
+                    row = 16 * a + 4 * q
+                    nc.gpsimd.dma_start(
+                        planes[a][32 * q : 32 * q + 4, :].bitcast(I32), planes[0][row : row + 4, :].bitcast(I32)
+                    )
+
+        w1_w = []
+        for b in range(2):
+            words = held([P, 2, PACK, 2 * P], U8, f"w1_w{b}")
+            src = w1_raw[:].bitcast(U16)[:, :, PASS * b : PASS * (b + 1)]
+            nc.vector.tensor_copy(words[:].bitcast(U16), src.rearrange("p a (m t) -> p a t m", t=PACK))
+            w1_w.append(words)
+
+        v_w = {}
+        for a in range(2):
+            for h in range(2):
+                words = held([P, BANK], I32, f"v_w{a}{h}")
+                nc.vector.tensor_copy(
+                    words[:].bitcast(U32), tab_w[a][:].bitcast(U32).indirect(idx[:, 32 * h : 32 * (h + 1)])
+                )
+                v_w[a, h] = words
+
+        w2_bf = {(b, a): held([P, PACK, P, PACK], BF16, f"w2_bf{b}{a}") for b in range(2) for a in range(2)}
+        w2_w = {(b, a): held([P, PASS], I32, f"w2_w{b}{a}") for b in range(2) for a in range(2)}
+        w2_s = {(b, a): held([P, PASS], U8, f"w2_s{b}{a}") for b in range(2) for a in range(2)}
+
+        def round_w2(b, a, c0, c1):
+            dst = w2_bf[b, a][:, :, c0 // PACK : c1 // PACK, :].rearrange("p t m j -> p m j t")
+            copy = nc.scalar.copy if (b, a) in ((1, 1),) else nc.vector.tensor_copy
+            copy(dst, w2_raw[b, a, c0][:].rearrange("p j (m t) -> p m j t", t=PACK))
+
+        def quantize_w2(b, a, t0, t1):
+            cols = slice(P * t0, P * t1)
+            nc.vector.quantize_mx(
+                w2_w[b, a][:, cols].bitcast(FP8X4),
+                w2_s[b, a][:, cols],
+                w2_bf[b, a][:, t0:t1].rearrange("p t m j -> p (t m j)"),
+            )
+
+        def first_stage(tag, weights, evacuate):
+            x = ring.tile([P, S], F32, name=tag, bufs=4)
+            for h in range(2):
+                cols = slice(BANK * h, BANK * (h + 1))
+                acc = bank(tag + "_bank")
+                for a in range(2):
+                    w, s = weights(a)
+                    nc.tensor.matmul_mx(
+                        acc[:], lhsT=w, lhsT_scale=s, rhs=v_w[a, h][:].bitcast(FP8X4), rhs_scale=planes[a][:, cols],
+                        start=a == 0, stop=a == 1,
+                    )
+                evacuate(x[:, cols], acc[:])
+            return x
+
+        def ancestor(b, t):
+            first = S + PASS * b + P * t
+            x1 = first_stage(
+                "x1", lambda a: (w1_w[b][:, a, t, :].bitcast(FP4X4), planes[a][:, first : first + P]), nc.scalar.copy
+            )
+            sig = ring.tile([P, M], F32, name="sig", bufs=2)
+            nc.scalar.activation(sig[:], x1[:].indirect(p1[:]), ACT.Sigmoid, scale=2.0)
+            if b == 0 and t < 2:
+                anc = held([P, M], F32, f"w2_raw01{PASS // 2 * t}")
+            else:
+                anc = ring.tile([P, M], F32, name="anc", bufs=3)
+            if PACK * b + t in AFFINE_ON_SCALAR:
+                nc.scalar.activation(anc[:], sig[:], ACT.Copy, scale=2.0, bias=-1.0)
+            else:
+                nc.vector.tensor_scalar(anc[:], sig[:], 2.0, -1.0, ALU.mult, ALU.add)
+            return anc
+
+        def reflexes(b, t):
+            cols = slice(P * t, P * (t + 1))
+            evacuate = nc.vector.tensor_copy if (b, t) == (0, 0) else nc.scalar.copy
+            return first_stage("x2", lambda a: (w2_w[b, a][:, cols].bitcast(FP8X4), w2_s[b, a][:, cols]), evacuate)
+
+        z_parts = {0: [(0, M)], 1: [(0, HALF), (HALF, M)]}
+        z = {(b, m0): held([P, PACK, m1 - m0], F32, f"z{b}{m0}") for b in range(2) for m0, m1 in z_parts[b]}
+        z_w, z_s = {}, {}
+
+        def combine(b, t, anc, x2):
+            weighed = ring.tile([P, M], F32, name="weighed", bufs=2)
+            for n0, n1 in z_parts[1] if (b, t) == (1, PACK - 1) else z_parts[0]:
+                nc.vector.tensor_tensor(
+                    weighed[:, n0:n1], x2[:].indirect(p2[:, n0 // 16 : n1 // 16]), anc[:, n0:n1], ALU.mult
+                )
+                for m0, m1 in z_parts[b]:
+                    if n0 <= m0 < n1:
+                        nc.vector.tensor_tensor(
+                            z[b, m0][:, t, :], x2[:].indirect(p3[:, m0 // 16 : m1 // 16]), weighed[:, m0:m1], ALU.add
+                        )
+
+        def quantize_z(b, m0, m1, copy):
+            z_bf = held([P, m1 - m0, PACK], BF16, f"z_bf{b}{m0}")
+            copy(z_bf[:].rearrange("p (c i) t -> p c t i", i=4), z[b, m0][:].rearrange("p t (c i) -> p c t i", i=4))
+            words = held([P, m1 - m0], I32, f"z_w{b}{m0}")
+            plane = held([P, m1 - m0], U8, f"z_s{b}{m0}")
+            nc.vector.quantize_mx(words[:].bitcast(FP8X4), plane[:], z_bf[:].rearrange("p m t -> p (m t)"))
+            for h in range(m0 // HALF, m1 // HALF):
+                cols = slice(HALF * h - m0, HALF * (h + 1) - m0)
+                z_w[b, h], z_s[b, h] = words[:, cols], plane[:, cols]
+
+        def score(h):
+            y = held([P, N // P, HALF], F32, f"y{h}")
+            for c in range(N // P):
+                cols = slice(P * c, P * (c + 1))
+                acc = bank(("x1_bank", "x2_bank")[h])
+                for b in range(2):
+                    nc.tensor.matmul_mx(
+                        acc[:, :HALF], lhsT=w3_w[:, b, cols].bitcast(FP8X4), lhsT_scale=planes[b][:, S + H + P * c : S + H + P * (c + 1)],
+                        rhs=z_w[b, h].bitcast(FP8X4), rhs_scale=z_s[b, h], start=b == 0, stop=b == 1,
+                    )
+                if h == 1 and c == 1:
+                    nc.vector.tensor_scalar(y[:, c, :], acc[:, :HALF], prior[:, c : c + 1], None, ALU.add)
+                else:
+                    nc.scalar.activation(y[:, c, :], acc[:, :HALF], ACT.Identity, bias=prior[:, c : c + 1])
+                nc.sync.dma_start(out[cols, HALF * h : HALF * (h + 1)], y[:, c, :])
+
+        anc = {}
+        anc[0, 0] = ancestor(0, 0)
+        round_w2(0, 0, 0, PASS)
+        anc[0, 1] = ancestor(0, 1)
+        quantize_w2(0, 0, 0, PACK)
+        round_w2(0, 1, 0, PASS // 2)
+        round_w2(0, 1, PASS // 2, PASS)
+        quantize_w2(0, 1, 0, 1)
+        quantize_w2(0, 1, 1, 2)
+        quantize_w2(0, 1, 2, PACK)
+        order = [(b, t) for b in range(2) for t in range(PACK)]
+        for i, (b, t) in enumerate(order):
+            x2 = reflexes(b, t)
+            if i + 2 < len(order):
+                anc[order[i + 2]] = ancestor(*order[i + 2])
+            combine(b, t, anc[b, t], x2)
+            if b == 0 and t < 2:
+                round_w2(1, t, 0, PASS)
+            if b == 0 and 1 <= t < 3:
+                quantize_w2(1, t - 1, 0, PACK)
+            if (b, t) == (1, 0):
+                quantize_z(0, 0, M, nc.scalar.copy)
+        quantize_z(1, 0, HALF, nc.scalar.copy)
+        quantize_z(1, HALF, M, nc.vector.tensor_copy)
+        score(0)
+        score(1)

@@ -46,45 +46,57 @@ def tile_list_sound_change_dating_kernel(
 
         tab_s = held([P, T], U8, "tab_s")
         w1_s_raw = held([P, H], U8, "w1_s_raw")
-        planes = [held([P, S + H + N], U8, f"plane{a}") for a in range(2)]
-        v_cols, w1_cols, w3_cols = slice(0, S), slice(S, S + H), slice(S + H, S + H + N)
+        planes = [held([P, S + H], U8, f"plane{a}") for a in range(2)]
+        w3_s = held([P, 2, N], U8, "w3_s")
+        v_cols, w1_cols = slice(0, S), slice(S, S + H)
+        nc.vector.memset(w3_s[:].bitcast(I32), 0)
         for rows in (slice(32, 64), slice(64, P)):
             nc.vector.memset(w1_s_raw[rows, :].bitcast(I32), 0)
             nc.vector.memset(tab_s[rows, :].bitcast(I32), 0)
-            nc.vector.memset(planes[0][rows, w3_cols].bitcast(I32), 0)
         nc.vector.memset(planes[1][:].bitcast(I32), 0)
         warm = held([P, 2], F32, "warm")
         nc.vector.memset(warm[:, 0:1], 0.0)
         nc.scalar.activation(warm[:, 1:2], warm[:, 0:1], ACT.Sigmoid)
 
         nc.sync.dma_start(idx[:], offs)
-        for dst, src in ((tab_s[:32, :], tab_scales), (w1_s_raw[:32, :], w1_scales), (planes[0][:32, w3_cols], w3_scales)):
+        for dst, src in ((tab_s[:32, :], tab_scales), (w1_s_raw[:32, :], w1_scales)):
             nc.sync.dma_start(dst.bitcast(I32), src.rearrange("a q c -> (a q) c").bitcast(I32))
-        w1_raw = held([P, 2, 2 * H], U8, "w1_raw")
-        nc.sync.dma_start(w1_raw[:].bitcast(I32), w1_words.rearrange("a p c -> p a c").bitcast(I32))
-        tab_w = []
-        for a in range(2):
-            words = held([P, T], I32, f"tab_w{a}")
-            nc.sync.dma_start(words[:], tab_words[a].rearrange("p t i -> p (t i)").bitcast(I32))
+        nc.sync.dma_start(p1[:], pos1)
+        nc.sync.dma_start(p2[:], pos2)
+        nc.sync.dma_start(p3[:], pos3)
+        w1_raw, tab_w = [], []
+        for i in range(2):
+            half = held([P, 2, 2 * PASS], U8, f"w1_raw{i}")
+            src = w1_words[:, :, 2 * PASS * i : 2 * PASS * (i + 1)]
+            nc.sync.dma_start(half[:].bitcast(I32), src.rearrange("a p c -> p a c").bitcast(I32))
+            w1_raw.append(half)
+            words = held([P, T], I32, f"tab_w{i}")
+            nc.sync.dma_start(words[:], tab_words[i].rearrange("p t i -> p (t i)").bitcast(I32))
             tab_w.append(words)
 
-        w2_pieces = [(0, 0, 0, PASS), (0, 1, 0, PASS // 2), (0, 1, PASS // 2, PASS), (1, 0, 0, PASS), (1, 1, 0, PASS)]
+        w2_pieces = [
+            (0, 0, 0, PASS, "w1_raw0"),
+            (0, 1, 0, PASS // 2, "tab_w0"),
+            (0, 1, PASS // 2, PASS, "w1_raw1"),
+            (1, 0, 0, PASS, "tab_w1"),
+            (1, 1, 0, PASS, "w1_raw0"),
+        ]
         w2_raw = {}
-        for b, a, c0, c1 in w2_pieces:
-            raw = held([P, PACK, c1 - c0], F32, f"w2_raw{b}{a}{c0}")
+
+        def load_w2(b, a, c0, c1, space):
+            raw = held([P, PACK, c1 - c0], F32, space)
             rows = w2[PASS * a : PASS * (a + 1), PASS * b + c0 : PASS * b + c1]
             nc.sync.dma_start(raw[:], rows.rearrange("(p j) c -> p j c", j=PACK))
             w2_raw[b, a, c0] = raw
-            if (b, a) == (0, 0):
-                nc.sync.dma_start(p1[:], pos1)
-                nc.sync.dma_start(p2[:], pos2)
-                nc.sync.dma_start(p3[:], pos3)
 
-        w3_w = held([P, 2, N], I32, "w3_w")
-        nc.sync.dma_start(w3_w[:], w3_words.rearrange("a p c i -> p a (c i)").bitcast(I32))
+        for q in range(4):
+            nc.gpsimd.dma_start(
+                w3_s[32 * q : 32 * q + 4].bitcast(I32),
+                w3_scales[:, 4 * q : 4 * q + 4, :].rearrange("a r c -> r a c").bitcast(I32),
+            )
         prior = held([P, N // P], F32, "prior")
         with nc.allow_non_contiguous_dma(reason="one value of period to a partition"):
-            nc.sync.dma_start(prior[:], period.rearrange("(c p) -> p c", p=P))
+            nc.gpsimd.dma_start(prior[:], period.rearrange("(c p) -> p c", p=P))
 
         nc.vector.tensor_copy(
             planes[0][:, w1_cols].rearrange("p (b t m) -> p b t m", b=2, t=PACK),
@@ -97,14 +109,15 @@ def tile_list_sound_change_dating_kernel(
             for q in range(4):
                 if (a, q) != (0, 0):
                     row = 16 * a + 4 * q
-                    nc.gpsimd.dma_start(
+                    queue = nc.gpsimd if (a, q) == (1, 3) else nc.scalar
+                    queue.dma_start(
                         planes[a][32 * q : 32 * q + 4, :].bitcast(I32), planes[0][row : row + 4, :].bitcast(I32)
                     )
 
         w1_w = []
         for b in range(2):
             words = held([P, 2, PACK, 2 * P], U8, f"w1_w{b}")
-            src = w1_raw[:].bitcast(U16)[:, :, PASS * b : PASS * (b + 1)]
+            src = w1_raw[b][:].bitcast(U16)
             nc.vector.tensor_copy(words[:].bitcast(U16), src.rearrange("p a (m t) -> p a t m", t=PACK))
             w1_w.append(words)
 
@@ -116,6 +129,9 @@ def tile_list_sound_change_dating_kernel(
                     words[:].bitcast(U32), tab_w[a][:].bitcast(U32).indirect(idx[:, 32 * h : 32 * (h + 1)])
                 )
                 v_w[a, h] = words
+
+        for piece in w2_pieces[:4]:
+            load_w2(*piece)
 
         w2_bf = {(b, a): held([P, PACK, P, PACK], BF16, f"w2_bf{b}{a}") for b in range(2) for a in range(2)}
         w2_w = {(b, a): held([P, PASS], I32, f"w2_w{b}{a}") for b in range(2) for a in range(2)}
@@ -156,7 +172,7 @@ def tile_list_sound_change_dating_kernel(
             sig = ring.tile([P, M], F32, name="sig", bufs=2)
             nc.scalar.activation(sig[:], x1[:].indirect(p1[:]), ACT.Sigmoid, scale=2.0)
             if b == 0 and t < 2:
-                anc = held([P, M], F32, f"w2_raw01{PASS // 2 * t}")
+                anc = held([P, M], F32, ("tab_w0", "w1_raw1")[t])
             else:
                 anc = ring.tile([P, M], F32, name="anc", bufs=3)
             if PACK * b + t in AFFINE_ON_SCALAR:
@@ -170,31 +186,28 @@ def tile_list_sound_change_dating_kernel(
             evacuate = nc.vector.tensor_copy if (b, t) == (0, 0) else nc.scalar.copy
             return first_stage("x2", lambda a: (w2_w[b, a][:, cols].bitcast(FP8X4), w2_s[b, a][:, cols]), evacuate)
 
-        z_parts = {0: [(0, M)], 1: [(0, HALF), (HALF, M)]}
-        z = {(b, m0): held([P, PACK, m1 - m0], F32, f"z{b}{m0}") for b in range(2) for m0, m1 in z_parts[b]}
+        z = {(b, h): held([P, PACK, HALF], F32, f"z{b}{h}") for b in range(2) for h in range(2)}
         z_w, z_s = {}, {}
 
         def combine(b, t, anc, x2):
             weighed = ring.tile([P, M], F32, name="weighed", bufs=2)
-            for n0, n1 in z_parts[1] if (b, t) == (1, PACK - 1) else z_parts[0]:
+            for h in range(2):
+                cols = slice(HALF * h, HALF * (h + 1))
                 nc.vector.tensor_tensor(
-                    weighed[:, n0:n1], x2[:].indirect(p2[:, n0 // 16 : n1 // 16]), anc[:, n0:n1], ALU.mult
+                    weighed[:, cols], x2[:].indirect(p2[:, 16 * h : 16 * (h + 1)]), anc[:, cols], ALU.mult
                 )
-                for m0, m1 in z_parts[b]:
-                    if n0 <= m0 < n1:
-                        nc.vector.tensor_tensor(
-                            z[b, m0][:, t, :], x2[:].indirect(p3[:, m0 // 16 : m1 // 16]), weighed[:, m0:m1], ALU.add
-                        )
+            for h in range(2):
+                cols = slice(HALF * h, HALF * (h + 1))
+                nc.vector.tensor_tensor(
+                    z[b, h][:, t, :], x2[:].indirect(p3[:, 16 * h : 16 * (h + 1)]), weighed[:, cols], ALU.add
+                )
 
-        def quantize_z(b, m0, m1, copy):
-            z_bf = held([P, m1 - m0, PACK], BF16, f"z_bf{b}{m0}")
-            copy(z_bf[:].rearrange("p (c i) t -> p c t i", i=4), z[b, m0][:].rearrange("p t (c i) -> p c t i", i=4))
-            words = held([P, m1 - m0], I32, f"z_w{b}{m0}")
-            plane = held([P, m1 - m0], U8, f"z_s{b}{m0}")
-            nc.vector.quantize_mx(words[:].bitcast(FP8X4), plane[:], z_bf[:].rearrange("p m t -> p (m t)"))
-            for h in range(m0 // HALF, m1 // HALF):
-                cols = slice(HALF * h - m0, HALF * (h + 1) - m0)
-                z_w[b, h], z_s[b, h] = words[:, cols], plane[:, cols]
+        def quantize_z(b, h, copy):
+            z_bf = held([P, HALF, PACK], BF16, f"z_bf{b}{h}")
+            copy(z_bf[:].rearrange("p (c i) t -> p c t i", i=4), z[b, h][:].rearrange("p t (c i) -> p c t i", i=4))
+            z_w[b, h] = held([P, HALF], I32, f"z_w{b}{h}")[:]
+            z_s[b, h] = held([P, HALF], U8, f"z_s{b}{h}")[:]
+            nc.vector.quantize_mx(z_w[b, h].bitcast(FP8X4), z_s[b, h], z_bf[:].rearrange("p m t -> p (m t)"))
 
         def score(h):
             y = held([P, N // P, HALF], F32, f"y{h}")
@@ -203,7 +216,7 @@ def tile_list_sound_change_dating_kernel(
                 acc = bank(("x1_bank", "x2_bank")[h])
                 for b in range(2):
                     nc.tensor.matmul_mx(
-                        acc[:, :HALF], lhsT=w3_w[:, b, cols].bitcast(FP8X4), lhsT_scale=planes[b][:, S + H + P * c : S + H + P * (c + 1)],
+                        acc[:, :HALF], lhsT=w3_w[:, b, cols].bitcast(FP8X4), lhsT_scale=w3_s[:, b, cols],
                         rhs=z_w[b, h].bitcast(FP8X4), rhs_scale=z_s[b, h], start=b == 0, stop=b == 1,
                     )
                 if h == 1 and c == 1:
@@ -212,14 +225,15 @@ def tile_list_sound_change_dating_kernel(
                     nc.scalar.activation(y[:, c, :], acc[:, :HALF], ACT.Identity, bias=prior[:, c : c + 1])
                 nc.sync.dma_start(out[cols, HALF * h : HALF * (h + 1)], y[:, c, :])
 
-        anc = {}
-        anc[0, 0] = ancestor(0, 0)
         round_w2(0, 0, 0, PASS)
-        anc[0, 1] = ancestor(0, 1)
+        load_w2(*w2_pieces[4])
         quantize_w2(0, 0, 0, PACK)
         round_w2(0, 1, 0, PASS // 2)
         round_w2(0, 1, PASS // 2, PASS)
         quantize_w2(0, 1, 0, 1)
+        anc = {}
+        anc[0, 0] = ancestor(0, 0)
+        anc[0, 1] = ancestor(0, 1)
         quantize_w2(0, 1, 1, 2)
         quantize_w2(0, 1, 2, PACK)
         order = [(b, t) for b in range(2) for t in range(PACK)]
@@ -230,11 +244,14 @@ def tile_list_sound_change_dating_kernel(
             combine(b, t, anc[b, t], x2)
             if b == 0 and t < 2:
                 round_w2(1, t, 0, PASS)
+            if (b, t) == (0, 0):
+                w3_w = held([P, 2, N], I32, "tab_w1")
+                nc.sync.dma_start(w3_w[:], w3_words.rearrange("a p c i -> p a (c i)").bitcast(I32))
             if b == 0 and 1 <= t < 3:
                 quantize_w2(1, t - 1, 0, PACK)
-            if (b, t) == (1, 0):
-                quantize_z(0, 0, M, nc.scalar.copy)
-        quantize_z(1, 0, HALF, nc.scalar.copy)
-        quantize_z(1, HALF, M, nc.vector.tensor_copy)
+        quantize_z(0, 0, nc.scalar.copy)
+        quantize_z(0, 1, nc.scalar.copy)
+        quantize_z(1, 0, nc.scalar.copy)
+        quantize_z(1, 1, nc.vector.tensor_copy)
         score(0)
         score(1)

@@ -31,13 +31,20 @@ def tile_list_sound_change_dating_kernel(
     with ExitStack() as ctx:
         keep = ctx.enter_context(tc.tile_pool(name="keep", bufs=1))
         ring = ctx.enter_context(tc.tile_pool(name="ring", bufs=1))
-        psum = ctx.enter_context(tc.psum_pool(name="psum", bufs=4))
+        reuse = ctx.enter_context(tc.tile_pool(name="reuse", bufs=1))
+        psum = ctx.enter_context(tc.psum_pool(name="psum", bufs=1))
 
         def held(shape, dtype, name):
             return keep.tile(shape, dtype, name=name, align_bytes=64)
 
-        def bank(tag):
-            return psum.tile([P, BANK], F32, name=tag)
+        def reused(shape, dtype, name, offset):
+            return reuse.tile(shape, dtype, name=name, offset=offset, align_bytes=64)
+
+        taken = []
+
+        def bank():
+            taken.append(psum.tile([P, BANK], F32, name=f"bank{len(taken) % 8}"))
+            return taken[-1]
 
         idx = keep.tile([P, S // 16], U16, name="idx")
         p1 = keep.tile([P, M // 16], U16, name="p1")
@@ -47,13 +54,11 @@ def tile_list_sound_change_dating_kernel(
         tab_s = held([P, T], U8, "tab_s")
         w1_s_raw = held([P, H], U8, "w1_s_raw")
         planes = [held([P, S + H], U8, f"plane{a}") for a in range(2)]
-        w3_s = held([P, 2, N], U8, "w3_s")
         v_cols, w1_cols = slice(0, S), slice(S, S + H)
-        nc.vector.memset(w3_s[:].bitcast(I32), 0)
-        for rows in (slice(32, 64), slice(64, P)):
-            nc.vector.memset(w1_s_raw[rows, :].bitcast(I32), 0)
-            nc.vector.memset(tab_s[rows, :].bitcast(I32), 0)
-        nc.vector.memset(planes[1][:].bitcast(I32), 0)
+        for raw in (tab_s, w1_s_raw):
+            for rows in (slice(32, 64), slice(64, P)):
+                nc.gpsimd.memset(raw[rows, :].bitcast(I32), 0)
+        nc.gpsimd.memset(planes[1][:].bitcast(I32), 0)
         warm = held([P, 2], F32, "warm")
         nc.vector.memset(warm[:, 0:1], 0.0)
         nc.scalar.activation(warm[:, 1:2], warm[:, 0:1], ACT.Sigmoid)
@@ -64,62 +69,60 @@ def tile_list_sound_change_dating_kernel(
         nc.sync.dma_start(p1[:], pos1)
         nc.sync.dma_start(p2[:], pos2)
         nc.sync.dma_start(p3[:], pos3)
-        w1_raw, tab_w = [], []
-        for i in range(2):
-            half = held([P, 2, 2 * PASS], U8, f"w1_raw{i}")
-            src = w1_words[:, :, 2 * PASS * i : 2 * PASS * (i + 1)]
-            nc.sync.dma_start(half[:].bitcast(I32), src.rearrange("a p c -> p a c").bitcast(I32))
-            w1_raw.append(half)
-            words = held([P, T], I32, f"tab_w{i}")
-            nc.sync.dma_start(words[:], tab_words[i].rearrange("p t i -> p (t i)").bitcast(I32))
+        w1_raw = reused([P, 2, 2 * H], U8, "w1_raw", 32768)
+        nc.sync.dma_start(w1_raw[:].bitcast(I32), w1_words.rearrange("a p c -> p a c").bitcast(I32))
+        tab_w = []
+        for a in range(2):
+            words = reused([P, T], I32, f"tab_w{a}", 16384 * a)
+            nc.sync.dma_start(words[:], tab_words[a].rearrange("p t i -> p (t i)").bitcast(I32))
             tab_w.append(words)
 
         w2_pieces = [
-            (0, 0, 0, PASS, "w1_raw0"),
-            (0, 1, 0, PASS // 2, "tab_w0"),
-            (0, 1, PASS // 2, PASS, "w1_raw1"),
-            (1, 0, 0, PASS, "tab_w1"),
-            (1, 1, 0, PASS, "w1_raw0"),
+            (0, 0, 0, PASS, 32768),
+            (0, 1, 0, PASS // 2, 0),
+            (0, 1, PASS // 2, PASS, 4096),
+            (1, 0, 0, PASS, 16384 + 4096),
+            (1, 1, 0, PASS, 32768),
         ]
         w2_raw = {}
 
         def load_w2(b, a, c0, c1, space):
-            raw = held([P, PACK, c1 - c0], F32, space)
+            raw = reused([P, PACK, c1 - c0], F32, f"w2_raw{b}{a}{c0}", space)
             rows = w2[PASS * a : PASS * (a + 1), PASS * b + c0 : PASS * b + c1]
             nc.sync.dma_start(raw[:], rows.rearrange("(p j) c -> p j c", j=PACK))
             w2_raw[b, a, c0] = raw
 
-        for q in range(4):
-            nc.gpsimd.dma_start(
-                w3_s[32 * q : 32 * q + 4].bitcast(I32),
-                w3_scales[:, 4 * q : 4 * q + 4, :].rearrange("a r c -> r a c").bitcast(I32),
-            )
-        prior = held([P, N // P], F32, "prior")
-        with nc.allow_non_contiguous_dma(reason="one value of period to a partition"):
-            nc.gpsimd.dma_start(prior[:], period.rearrange("(c p) -> p c", p=P))
-
+        v_s_raw = held([P, S], U8, "v_s_raw")
+        nc.vector.tensor_copy(v_s_raw[:], tab_s[:].indirect(idx[:]))
         nc.vector.tensor_copy(
             planes[0][:, w1_cols].rearrange("p (b t m) -> p b t m", b=2, t=PACK),
             w1_s_raw[:].rearrange("p (b m t) -> p b t m", b=2, t=PACK),
         )
-        v_s_raw = held([P, S], U8, "v_s_raw")
-        nc.vector.tensor_copy(v_s_raw[:], tab_s[:].indirect(idx[:]))
         nc.vector.tensor_copy(planes[0][:, v_cols].bitcast(I32), v_s_raw[:].bitcast(I32))
         for a in range(2):
             for q in range(4):
                 if (a, q) != (0, 0):
                     row = 16 * a + 4 * q
-                    queue = nc.gpsimd if (a, q) == (1, 3) else nc.scalar
+                    queue = nc.gpsimd if a == 1 and q >= 2 else nc.scalar
                     queue.dma_start(
                         planes[a][32 * q : 32 * q + 4, :].bitcast(I32), planes[0][row : row + 4, :].bitcast(I32)
                     )
 
-        w1_w = []
-        for b in range(2):
-            words = held([P, 2, PACK, 2 * P], U8, f"w1_w{b}")
-            src = w1_raw[b][:].bitcast(U16)
-            nc.vector.tensor_copy(words[:].bitcast(U16), src.rearrange("p a (m t) -> p a t m", t=PACK))
-            w1_w.append(words)
+        w3_s = held([P, 2, N], U8, "w1_s_raw")
+        nc.gpsimd.memset(w3_s[:].bitcast(I32), 0)
+        for q in range(4):
+            nc.gpsimd.dma_start(
+                w3_s[32 * q : 32 * q + 4].bitcast(I32),
+                w3_scales[:, 4 * q : 4 * q + 4, :].rearrange("a r c -> r a c").bitcast(I32),
+            )
+        prior = held([P, N // P], F32, "v_s_raw")
+        with nc.allow_non_contiguous_dma(reason="one value of period to a partition"):
+            nc.gpsimd.dma_start(prior[:], period.rearrange("(c p) -> p c", p=P))
+
+        w1_w = held([P, 2, 2, PACK, 2 * P], U8, "w1_w")
+        nc.vector.tensor_copy(
+            w1_w[:].bitcast(U16), w1_raw[:].bitcast(U16).rearrange("p a (b m t) -> p a b t m", b=2, t=PACK)
+        )
 
         v_w = {}
         for a in range(2):
@@ -133,14 +136,21 @@ def tile_list_sound_change_dating_kernel(
         for piece in w2_pieces[:4]:
             load_w2(*piece)
 
-        w2_bf = {(b, a): held([P, PACK, P, PACK], BF16, f"w2_bf{b}{a}") for b in range(2) for a in range(2)}
+        w2_bf = {
+            (0, 0): reused([P, PACK, P, PACK], BF16, "w2_bf00", 16384),
+            (0, 1): held([P, PACK, P, PACK], BF16, "w2_bf01"),
+            (1, 0): reused([P, PACK, P, PACK], BF16, "w2_bf10", 4096),
+            (1, 1): held([P, PACK, P, PACK], BF16, "w2_bf11"),
+        }
         w2_w = {(b, a): held([P, PASS], I32, f"w2_w{b}{a}") for b in range(2) for a in range(2)}
         w2_s = {(b, a): held([P, PASS], U8, f"w2_s{b}{a}") for b in range(2) for a in range(2)}
 
         def round_w2(b, a, c0, c1):
             dst = w2_bf[b, a][:, :, c0 // PACK : c1 // PACK, :].rearrange("p t m j -> p m j t")
             copy = nc.scalar.copy if (b, a) in ((1, 1),) else nc.vector.tensor_copy
-            copy(dst, w2_raw[b, a, c0][:].rearrange("p j (m t) -> p m j t", t=PACK))
+            src = w2_raw[b, a, c0][:].rearrange("p j (m t) -> p m j t", t=PACK)
+            for t0 in (0, 2):
+                copy(dst[:, :, :, t0 : t0 + 2], src[:, :, :, t0 : t0 + 2])
 
         def quantize_w2(b, a, t0, t1):
             cols = slice(P * t0, P * t1)
@@ -150,11 +160,10 @@ def tile_list_sound_change_dating_kernel(
                 w2_bf[b, a][:, t0:t1].rearrange("p t m j -> p (t m j)"),
             )
 
-        def first_stage(tag, weights, evacuate):
-            x = ring.tile([P, S], F32, name=tag, bufs=4)
+        def first_stage(tag, weights, evacuate, x):
             for h in range(2):
                 cols = slice(BANK * h, BANK * (h + 1))
-                acc = bank(tag + "_bank")
+                acc = bank()
                 for a in range(2):
                     w, s = weights(a)
                     nc.tensor.matmul_mx(
@@ -164,17 +173,20 @@ def tile_list_sound_change_dating_kernel(
                 evacuate(x[:, cols], acc[:])
             return x
 
-        def ancestor(b, t):
+        def features(b, t):
             first = S + PASS * b + P * t
-            x1 = first_stage(
-                "x1", lambda a: (w1_w[b][:, a, t, :].bitcast(FP4X4), planes[a][:, first : first + P]), nc.scalar.copy
+            return first_stage(
+                "x1", lambda a: (w1_w[:, a, b, t, :].bitcast(FP4X4), planes[a][:, first : first + P]), nc.scalar.copy,
+                held([P, S], F32, "x1_last") if (b, t) == (1, PACK - 1) else ring.tile([P, S], F32, name="x1", bufs=3),
             )
-            sig = ring.tile([P, M], F32, name="sig", bufs=2)
+
+        def ancestor(b, t, x1):
+            sig = ring.tile([P, M], F32, name="sig", bufs=3)
             nc.scalar.activation(sig[:], x1[:].indirect(p1[:]), ACT.Sigmoid, scale=2.0)
             if b == 0 and t < 2:
-                anc = held([P, M], F32, ("tab_w0", "w1_raw1")[t])
+                anc = reused([P, M], F32, f"anc{t}", 4096)
             else:
-                anc = ring.tile([P, M], F32, name="anc", bufs=3)
+                anc = ring.tile([P, M], F32, name="anc", bufs=4)
             if PACK * b + t in AFFINE_ON_SCALAR:
                 nc.scalar.activation(anc[:], sig[:], ACT.Copy, scale=2.0, bias=-1.0)
             else:
@@ -184,46 +196,57 @@ def tile_list_sound_change_dating_kernel(
         def reflexes(b, t):
             cols = slice(P * t, P * (t + 1))
             evacuate = nc.vector.tensor_copy if (b, t) == (0, 0) else nc.scalar.copy
-            return first_stage("x2", lambda a: (w2_w[b, a][:, cols].bitcast(FP8X4), w2_s[b, a][:, cols]), evacuate)
+            return first_stage("x2", lambda a: (w2_w[b, a][:, cols].bitcast(FP8X4), w2_s[b, a][:, cols]), evacuate,
+                               ring.tile([P, S], F32, name="x2", bufs=4))
 
-        z = {(b, h): held([P, PACK, HALF], F32, f"z{b}{h}") for b in range(2) for h in range(2)}
+        chunks = {0: [(0, 256), (256, 512)], 1: [(0, 256), (256, 384), (384, 512)]}
+        z = {(b, m0): held([P, PACK, m1 - m0], F32, f"z{b}{m0}") for b in range(2) for m0, m1 in chunks[b]}
         z_w, z_s = {}, {}
 
         def combine(b, t, anc, x2):
             weighed = ring.tile([P, M], F32, name="weighed", bufs=2)
-            for h in range(2):
-                cols = slice(HALF * h, HALF * (h + 1))
+
+            def weigh(m0, m1):
                 nc.vector.tensor_tensor(
-                    weighed[:, cols], x2[:].indirect(p2[:, 16 * h : 16 * (h + 1)]), anc[:, cols], ALU.mult
-                )
-            for h in range(2):
-                cols = slice(HALF * h, HALF * (h + 1))
-                nc.vector.tensor_tensor(
-                    z[b, h][:, t, :], x2[:].indirect(p3[:, 16 * h : 16 * (h + 1)]), weighed[:, cols], ALU.add
+                    weighed[:, m0:m1], x2[:].indirect(p2[:, m0 // 16 : m1 // 16]), anc[:, m0:m1], ALU.mult
                 )
 
-        def quantize_z(b, h, copy):
-            z_bf = held([P, HALF, PACK], BF16, f"z_bf{b}{h}")
-            copy(z_bf[:].rearrange("p (c i) t -> p c t i", i=4), z[b, h][:].rearrange("p t (c i) -> p c t i", i=4))
-            z_w[b, h] = held([P, HALF], I32, f"z_w{b}{h}")[:]
-            z_s[b, h] = held([P, HALF], U8, f"z_s{b}{h}")[:]
-            nc.vector.quantize_mx(z_w[b, h].bitcast(FP8X4), z_s[b, h], z_bf[:].rearrange("p m t -> p (m t)"))
+            def add_loan(m0, m1):
+                nc.vector.tensor_tensor(
+                    z[b, m0][:, t, :], x2[:].indirect(p3[:, m0 // 16 : m1 // 16]), weighed[:, m0:m1], ALU.add
+                )
 
-        def score(h):
-            y = held([P, N // P, HALF], F32, f"y{h}")
+            weigh(0, HALF)
+            if (b, t) == (1, PACK - 1):
+                add_loan(*chunks[b][0])
+            weigh(HALF, M)
+            for m0, m1 in chunks[b][(b, t) == (1, PACK - 1) :]:
+                add_loan(m0, m1)
+
+        def round_z(b, m0, m1, copy, z_bf):
+            copy(z_bf.rearrange("p (c i) t -> p c t i", i=4), z[b, m0][:].rearrange("p t (c i) -> p c t i", i=4))
+            z_w[b, m0] = held([P, m1 - m0], I32, f"z_w{b}{m0}")
+            z_s[b, m0] = held([P, m1 - m0], U8, f"z_s{b}{m0}")
+            nc.vector.quantize_mx(z_w[b, m0][:].bitcast(FP8X4), z_s[b, m0][:], z_bf.rearrange("p m t -> p (m t)"))
+
+        def score(m0, m1, on_vector):
+            y = held([P, N // P, m1 - m0], F32, f"y{m0}")
+            first = m0 // HALF * HALF
             for c in range(N // P):
                 cols = slice(P * c, P * (c + 1))
-                acc = bank(("x1_bank", "x2_bank")[h])
-                for b in range(2):
+                acc = bank()[:, : m1 - m0]
+                for b, start in ((0, first), (1, m0)):
+                    part = slice(m0 - start, m1 - start)
                     nc.tensor.matmul_mx(
-                        acc[:, :HALF], lhsT=w3_w[:, b, cols].bitcast(FP8X4), lhsT_scale=w3_s[:, b, cols],
-                        rhs=z_w[b, h].bitcast(FP8X4), rhs_scale=z_s[b, h], start=b == 0, stop=b == 1,
+                        acc, lhsT=w3_w[:, b, cols].bitcast(FP8X4), lhsT_scale=w3_s[:, b, cols],
+                        rhs=z_w[b, start][:, part].bitcast(FP8X4), rhs_scale=z_s[b, start][:, part],
+                        start=b == 0, stop=b == 1,
                     )
-                if h == 1 and c == 1:
-                    nc.vector.tensor_scalar(y[:, c, :], acc[:, :HALF], prior[:, c : c + 1], None, ALU.add)
+                if c in on_vector:
+                    nc.vector.tensor_scalar(y[:, c, :], acc, prior[:, c : c + 1], None, ALU.add)
                 else:
-                    nc.scalar.activation(y[:, c, :], acc[:, :HALF], ACT.Identity, bias=prior[:, c : c + 1])
-                nc.sync.dma_start(out[cols, HALF * h : HALF * (h + 1)], y[:, c, :])
+                    nc.scalar.activation(y[:, c, :], acc, ACT.Identity, bias=prior[:, c : c + 1])
+            nc.sync.dma_start(out.rearrange("(c p) m -> p c m", p=P)[:, :, m0:m1], y[:])
 
         round_w2(0, 0, 0, PASS)
         load_w2(*w2_pieces[4])
@@ -231,27 +254,30 @@ def tile_list_sound_change_dating_kernel(
         round_w2(0, 1, 0, PASS // 2)
         round_w2(0, 1, PASS // 2, PASS)
         quantize_w2(0, 1, 0, 1)
-        anc = {}
-        anc[0, 0] = ancestor(0, 0)
-        anc[0, 1] = ancestor(0, 1)
+        tiles = [(b, t) for b in range(2) for t in range(PACK)]
+        anc = ancestor(0, 0, features(0, 0))
         quantize_w2(0, 1, 1, 2)
         quantize_w2(0, 1, 2, PACK)
-        order = [(b, t) for b in range(2) for t in range(PACK)]
-        for i, (b, t) in enumerate(order):
+        for i, (b, t) in enumerate(tiles):
+            ahead = tiles[i + 1] if i + 1 < len(tiles) else None
+            x1 = features(*ahead) if ahead else None
             x2 = reflexes(b, t)
-            if i + 2 < len(order):
-                anc[order[i + 2]] = ancestor(*order[i + 2])
-            combine(b, t, anc[b, t], x2)
-            if b == 0 and t < 2:
-                round_w2(1, t, 0, PASS)
-            if (b, t) == (0, 0):
-                w3_w = held([P, 2, N], I32, "tab_w1")
+            anc_ahead = ancestor(*ahead, x1) if ahead else None
+            combine(b, t, anc, x2)
+            anc = anc_ahead
+            if (b, t) == (0, 1):
+                round_w2(1, 0, 0, PASS)
+                w3_w = reused([P, 2, N], I32, "w3_w", 16384 + 4096)
                 nc.sync.dma_start(w3_w[:], w3_words.rearrange("a p c i -> p a (c i)").bitcast(I32))
-            if b == 0 and 1 <= t < 3:
-                quantize_w2(1, t - 1, 0, PACK)
-        quantize_z(0, 0, nc.scalar.copy)
-        quantize_z(0, 1, nc.scalar.copy)
-        quantize_z(1, 0, nc.scalar.copy)
-        quantize_z(1, 1, nc.vector.tensor_copy)
-        score(0)
-        score(1)
+            if (b, t) == (0, 2):
+                quantize_w2(1, 0, 0, PACK)
+                round_w2(1, 1, 0, PASS)
+                quantize_w2(1, 1, 0, PACK)
+        z0_bf = held([P, M, PACK], BF16, "x1_last")
+        for m0, m1 in chunks[0]:
+            round_z(0, m0, m1, nc.scalar.copy, z0_bf[:, m0:m1])
+        for i, (m0, m1) in enumerate(chunks[1]):
+            z1_bf = held([P, m1 - m0, PACK], BF16, f"z1_bf{m0}")
+            round_z(1, m0, m1, (nc.scalar.copy, nc.scalar.copy, nc.vector.tensor_copy)[i], z1_bf[:])
+        for i, (m0, m1) in enumerate(chunks[1]):
+            score(m0, m1, ((), (1,), (1,))[i])

@@ -18,10 +18,18 @@ ALU = mybir.AluOpType
 
 P = 128
 PACK = 4
-PASS = 512
+PASS = P * PACK
 BANK = 512
+BANKS = 8
+LIST = 16
+SCALE_ROWS = 32
 HALF = M // 2
-AFFINE_ON_SCALAR = ()
+
+CHUNKS = ([(0, HALF), (HALF, M)], [(0, HALF), (HALF, HALF + P), (HALF + P, M)])
+
+TABLE_0, TABLE_1, W1, X1 = 0, 4 * T, 8 * T, 10 * T
+QUARTER = T
+X_BYTES = 4 * S
 
 
 def tile_list_sound_change_dating_kernel(
@@ -43,13 +51,13 @@ def tile_list_sound_change_dating_kernel(
         taken = []
 
         def bank():
-            taken.append(psum.tile([P, BANK], F32, name=f"bank{len(taken) % 8}"))
+            taken.append(psum.tile([P, BANK], F32, name=f"bank{len(taken) % BANKS}"))
             return taken[-1]
 
-        idx = keep.tile([P, S // 16], U16, name="idx")
-        p1 = keep.tile([P, M // 16], U16, name="p1")
-        p2 = keep.tile([P, M // 16], U16, name="p2")
-        p3 = keep.tile([P, M // 16], U16, name="p3")
+        idx = keep.tile([P, S // LIST], U16, name="idx")
+        p1 = keep.tile([P, M // LIST], U16, name="p1")
+        p2 = keep.tile([P, M // LIST], U16, name="p2")
+        p3 = keep.tile([P, M // LIST], U16, name="p3")
 
         tab_s = held([P, T], U8, "tab_s")
         w1_s_raw = held([P, H], U8, "w1_s_raw")
@@ -59,38 +67,19 @@ def tile_list_sound_change_dating_kernel(
             for rows in (slice(32, 64), slice(64, P)):
                 nc.gpsimd.memset(raw[rows, :].bitcast(I32), 0)
         nc.gpsimd.memset(planes[1][:].bitcast(I32), 0)
-        warm = held([P, 2], F32, "warm")
-        nc.vector.memset(warm[:, 0:1], 0.0)
-        nc.scalar.activation(warm[:, 1:2], warm[:, 0:1], ACT.Sigmoid)
 
         nc.sync.dma_start(idx[:], offs)
-        for dst, src in ((tab_s[:32, :], tab_scales), (w1_s_raw[:32, :], w1_scales)):
-            nc.sync.dma_start(dst.bitcast(I32), src.rearrange("a q c -> (a q) c").bitcast(I32))
+        for raw, scales in ((tab_s, tab_scales), (w1_s_raw, w1_scales)):
+            nc.sync.dma_start(raw[:SCALE_ROWS, :].bitcast(I32), scales.rearrange("a q c -> (a q) c").bitcast(I32))
         nc.sync.dma_start(p1[:], pos1)
         nc.sync.dma_start(p2[:], pos2)
         nc.sync.dma_start(p3[:], pos3)
-        w1_raw = reused([P, 2, 2 * H], U8, "w1_raw", 32768)
+        w1_raw = reused([P, 2, 2 * H], U8, "w1_raw", W1)
         nc.sync.dma_start(w1_raw[:].bitcast(I32), w1_words.rearrange("a p c -> p a c").bitcast(I32))
         tab_w = []
-        for a in range(2):
-            words = reused([P, T], I32, f"tab_w{a}", 16384 * a)
-            nc.sync.dma_start(words[:], tab_words[a].rearrange("p t i -> p (t i)").bitcast(I32))
-            tab_w.append(words)
-
-        w2_pieces = [
-            (0, 0, 0, PASS, 32768),
-            (0, 1, 0, PASS // 2, 0),
-            (0, 1, PASS // 2, PASS, 4096),
-            (1, 0, 0, PASS, 16384 + 4096),
-            (1, 1, 0, PASS, 32768),
-        ]
-        w2_raw = {}
-
-        def load_w2(b, a, c0, c1, space):
-            raw = reused([P, PACK, c1 - c0], F32, f"w2_raw{b}{a}{c0}", space)
-            rows = w2[PASS * a : PASS * (a + 1), PASS * b + c0 : PASS * b + c1]
-            nc.sync.dma_start(raw[:], rows.rearrange("(p j) c -> p j c", j=PACK))
-            w2_raw[b, a, c0] = raw
+        for a, offset in enumerate((TABLE_0, TABLE_1)):
+            tab_w.append(reused([P, T], I32, f"tab_w{a}", offset))
+            nc.sync.dma_start(tab_w[a][:], tab_words[a].rearrange("p t i -> p (t i)").bitcast(I32))
 
         v_s_raw = held([P, S], U8, "v_s_raw")
         nc.vector.tensor_copy(v_s_raw[:], tab_s[:].indirect(idx[:]))
@@ -126,30 +115,33 @@ def tile_list_sound_change_dating_kernel(
 
         v_w = {}
         for a in range(2):
-            for h in range(2):
-                words = held([P, BANK], I32, f"v_w{a}{h}")
-                nc.vector.tensor_copy(
-                    words[:].bitcast(U32), tab_w[a][:].bitcast(U32).indirect(idx[:, 32 * h : 32 * (h + 1)])
-                )
-                v_w[a, h] = words
+            for h in range(S // BANK):
+                v_w[a, h] = held([P, BANK], I32, f"v_w{a}{h}")
+                entries = idx[:, BANK // LIST * h : BANK // LIST * (h + 1)]
+                nc.vector.tensor_copy(v_w[a, h][:].bitcast(U32), tab_w[a][:].bitcast(U32).indirect(entries))
 
-        for piece in w2_pieces[:4]:
-            load_w2(*piece)
+        w2_raw = {}
 
-        w2_bf = {
-            (0, 0): reused([P, PACK, P, PACK], BF16, "w2_bf00", 16384),
-            (0, 1): held([P, PACK, P, PACK], BF16, "w2_bf01"),
-            (1, 0): reused([P, PACK, P, PACK], BF16, "w2_bf10", 4096),
-            (1, 1): held([P, PACK, P, PACK], BF16, "w2_bf11"),
-        }
+        def load_w2(b, a, c0, c1, offset):
+            w2_raw[b, a, c0] = reused([P, PACK, c1 - c0], F32, f"w2_raw{b}{a}{c0}", offset)
+            rows = w2[PASS * a : PASS * (a + 1), PASS * b + c0 : PASS * b + c1]
+            nc.sync.dma_start(w2_raw[b, a, c0][:], rows.rearrange("(p j) c -> p j c", j=PACK))
+
+        load_w2(0, 0, 0, PASS, W1)
+        load_w2(0, 1, 0, PASS // 2, TABLE_0)
+        load_w2(0, 1, PASS // 2, PASS, TABLE_0 + QUARTER)
+        load_w2(1, 0, 0, PASS, TABLE_1 + QUARTER)
+
+        w2_bf = {(0, 0): reused([P, PACK, P, PACK], BF16, "w2_bf00", TABLE_1)}
+        for b, a in ((0, 1), (1, 0), (1, 1)):
+            w2_bf[b, a] = held([P, PACK, P, PACK], BF16, f"w2_bf{b}{a}")
         w2_w = {(b, a): held([P, PASS], I32, f"w2_w{b}{a}") for b in range(2) for a in range(2)}
         w2_s = {(b, a): held([P, PASS], U8, f"w2_s{b}{a}") for b in range(2) for a in range(2)}
 
-        def round_w2(b, a, c0, c1):
+        def round_w2(b, a, c0, c1, copy):
             dst = w2_bf[b, a][:, :, c0 // PACK : c1 // PACK, :].rearrange("p t m j -> p m j t")
-            copy = nc.scalar.copy if (b, a) in ((1, 1),) else nc.vector.tensor_copy
             src = w2_raw[b, a, c0][:].rearrange("p j (m t) -> p m j t", t=PACK)
-            for t0 in (0, 2):
+            for t0 in range(0, PACK, 2):
                 copy(dst[:, :, :, t0 : t0 + 2], src[:, :, :, t0 : t0 + 2])
 
         def quantize_w2(b, a, t0, t1):
@@ -160,124 +152,122 @@ def tile_list_sound_change_dating_kernel(
                 w2_bf[b, a][:, t0:t1].rearrange("p t m j -> p (t m j)"),
             )
 
-        def first_stage(tag, weights, evacuate, x):
-            for h in range(2):
+        def first_stage(x, words, scales, copy):
+            for h in range(S // BANK):
                 cols = slice(BANK * h, BANK * (h + 1))
                 acc = bank()
                 for a in range(2):
-                    w, s = weights(a)
                     nc.tensor.matmul_mx(
-                        acc[:], lhsT=w, lhsT_scale=s, rhs=v_w[a, h][:].bitcast(FP8X4), rhs_scale=planes[a][:, cols],
+                        acc[:], lhsT=words[a], lhsT_scale=scales[a],
+                        rhs=v_w[a, h][:].bitcast(FP8X4), rhs_scale=planes[a][:, cols],
                         start=a == 0, stop=a == 1,
                     )
-                evacuate(x[:, cols], acc[:])
+                copy(x[:, cols], acc[:])
             return x
 
         def features(b, t):
+            if (b, t) == (0, 0):
+                place, copy = X1 + X_BYTES // 2, nc.vector.tensor_copy
+            else:
+                place, copy = X1 + X_BYTES * (t % 2), nc.scalar.copy
+            x1 = reused([P, S], F32, f"x1_{b}{t}", place)
             first = S + PASS * b + P * t
-            return first_stage(
-                "x1", lambda a: (w1_w[:, a, b, t, :].bitcast(FP4X4), planes[a][:, first : first + P]), nc.scalar.copy,
-                held([P, S], F32, "x1_last") if (b, t) == (1, PACK - 1) else ring.tile([P, S], F32, name="x1", bufs=3),
-            )
+            words = [w1_w[:, a, b, t, :].bitcast(FP4X4) for a in range(2)]
+            return first_stage(x1, words, [planes[a][:, first : first + P] for a in range(2)], copy)
+
+        def reflexes(b, t):
+            x2 = ring.tile([P, S], F32, name="x2", bufs=4)
+            cols = slice(P * t, P * (t + 1))
+            words = [w2_w[b, a][:, cols].bitcast(FP8X4) for a in range(2)]
+            return first_stage(x2, words, [w2_s[b, a][:, cols] for a in range(2)], nc.scalar.copy)
 
         def ancestor(b, t, x1):
             sig = ring.tile([P, M], F32, name="sig", bufs=3)
             nc.scalar.activation(sig[:], x1[:].indirect(p1[:]), ACT.Sigmoid, scale=2.0)
             if b == 0 and t < 2:
-                anc = reused([P, M], F32, f"anc{t}", 4096)
+                anc = reused([P, M], F32, f"anc{t}", TABLE_0 + QUARTER)
             else:
                 anc = ring.tile([P, M], F32, name="anc", bufs=4)
-            if PACK * b + t in AFFINE_ON_SCALAR:
-                nc.scalar.activation(anc[:], sig[:], ACT.Copy, scale=2.0, bias=-1.0)
-            else:
-                nc.vector.tensor_scalar(anc[:], sig[:], 2.0, -1.0, ALU.mult, ALU.add)
+            nc.vector.tensor_scalar(anc[:], sig[:], 2.0, -1.0, ALU.mult, ALU.add)
             return anc
 
-        def reflexes(b, t):
-            cols = slice(P * t, P * (t + 1))
-            evacuate = nc.vector.tensor_copy if (b, t) == (0, 0) else nc.scalar.copy
-            return first_stage("x2", lambda a: (w2_w[b, a][:, cols].bitcast(FP8X4), w2_s[b, a][:, cols]), evacuate,
-                               ring.tile([P, S], F32, name="x2", bufs=4))
-
-        chunks = {0: [(0, 256), (256, 512)], 1: [(0, 256), (256, 384), (384, 512)]}
-        z = {(b, m0): held([P, PACK, m1 - m0], F32, f"z{b}{m0}") for b in range(2) for m0, m1 in chunks[b]}
+        z = {(b, m0): held([P, PACK, m1 - m0], F32, f"z{b}{m0}") for b in range(2) for m0, m1 in CHUNKS[b]}
         z_w, z_s = {}, {}
 
         def combine(b, t, anc, x2):
             weighed = ring.tile([P, M], F32, name="weighed", bufs=2)
 
             def weigh(m0, m1):
-                nc.vector.tensor_tensor(
-                    weighed[:, m0:m1], x2[:].indirect(p2[:, m0 // 16 : m1 // 16]), anc[:, m0:m1], ALU.mult
-                )
+                picked = x2[:].indirect(p2[:, m0 // LIST : m1 // LIST])
+                nc.vector.tensor_tensor(weighed[:, m0:m1], picked, anc[:, m0:m1], ALU.mult)
 
             def add_loan(m0, m1):
-                nc.vector.tensor_tensor(
-                    z[b, m0][:, t, :], x2[:].indirect(p3[:, m0 // 16 : m1 // 16]), weighed[:, m0:m1], ALU.add
-                )
+                picked = x2[:].indirect(p3[:, m0 // LIST : m1 // LIST])
+                nc.vector.tensor_tensor(z[b, m0][:, t, :], picked, weighed[:, m0:m1], ALU.add)
 
+            last = (b, t) == (1, PACK - 1)
             weigh(0, HALF)
-            if (b, t) == (1, PACK - 1):
-                add_loan(*chunks[b][0])
+            if last:
+                add_loan(*CHUNKS[b][0])
             weigh(HALF, M)
-            for m0, m1 in chunks[b][(b, t) == (1, PACK - 1) :]:
+            for m0, m1 in CHUNKS[b][1:] if last else CHUNKS[b]:
                 add_loan(m0, m1)
 
-        def round_z(b, m0, m1, copy, z_bf):
+        def quantize_z(b, m0, m1, copy, z_bf):
             copy(z_bf.rearrange("p (c i) t -> p c t i", i=4), z[b, m0][:].rearrange("p t (c i) -> p c t i", i=4))
             z_w[b, m0] = held([P, m1 - m0], I32, f"z_w{b}{m0}")
             z_s[b, m0] = held([P, m1 - m0], U8, f"z_s{b}{m0}")
             nc.vector.quantize_mx(z_w[b, m0][:].bitcast(FP8X4), z_s[b, m0][:], z_bf.rearrange("p m t -> p (m t)"))
 
-        def score(m0, m1, on_vector):
+        def score(m0, m1):
             y = held([P, N // P, m1 - m0], F32, f"y{m0}")
-            first = m0 // HALF * HALF
+            chunk_starts = (m0 // HALF * HALF, m0)
             for c in range(N // P):
                 cols = slice(P * c, P * (c + 1))
                 acc = bank()[:, : m1 - m0]
-                for b, start in ((0, first), (1, m0)):
+                for b, start in enumerate(chunk_starts):
                     part = slice(m0 - start, m1 - start)
                     nc.tensor.matmul_mx(
                         acc, lhsT=w3_w[:, b, cols].bitcast(FP8X4), lhsT_scale=w3_s[:, b, cols],
                         rhs=z_w[b, start][:, part].bitcast(FP8X4), rhs_scale=z_s[b, start][:, part],
                         start=b == 0, stop=b == 1,
                     )
-                if c in on_vector:
+                if c == 1 and m1 - m0 < HALF:
                     nc.vector.tensor_scalar(y[:, c, :], acc, prior[:, c : c + 1], None, ALU.add)
                 else:
                     nc.scalar.activation(y[:, c, :], acc, ACT.Identity, bias=prior[:, c : c + 1])
             nc.sync.dma_start(out.rearrange("(c p) m -> p c m", p=P)[:, :, m0:m1], y[:])
 
-        round_w2(0, 0, 0, PASS)
-        load_w2(*w2_pieces[4])
+        round_w2(0, 0, 0, PASS, nc.vector.tensor_copy)
+        load_w2(1, 1, 0, PASS, W1)
         quantize_w2(0, 0, 0, PACK)
-        round_w2(0, 1, 0, PASS // 2)
-        round_w2(0, 1, PASS // 2, PASS)
-        quantize_w2(0, 1, 0, 1)
-        tiles = [(b, t) for b in range(2) for t in range(PACK)]
+        round_w2(0, 1, 0, PASS // 2, nc.vector.tensor_copy)
+        round_w2(0, 1, PASS // 2, PASS, nc.vector.tensor_copy)
+        quantize_w2(0, 1, 0, 2)
         anc = ancestor(0, 0, features(0, 0))
-        quantize_w2(0, 1, 1, 2)
         quantize_w2(0, 1, 2, PACK)
-        for i, (b, t) in enumerate(tiles):
-            ahead = tiles[i + 1] if i + 1 < len(tiles) else None
+
+        tiles = [(b, t) for b in range(2) for t in range(PACK)]
+        for (b, t), ahead in zip(tiles, tiles[1:] + [None]):
             x1 = features(*ahead) if ahead else None
             x2 = reflexes(b, t)
             anc_ahead = ancestor(*ahead, x1) if ahead else None
             combine(b, t, anc, x2)
             anc = anc_ahead
-            if (b, t) == (0, 1):
-                round_w2(1, 0, 0, PASS)
-                w3_w = reused([P, 2, N], I32, "w3_w", 16384 + 4096)
+            if (b, t) == (0, 0):
+                round_w2(1, 0, 0, PASS, nc.vector.tensor_copy)
+                w3_w = reused([P, 2, N], I32, "w3_w", TABLE_1 + QUARTER)
                 nc.sync.dma_start(w3_w[:], w3_words.rearrange("a p c i -> p a (c i)").bitcast(I32))
-            if (b, t) == (0, 2):
                 quantize_w2(1, 0, 0, PACK)
-                round_w2(1, 1, 0, PASS)
+            if (b, t) == (0, 2):
+                round_w2(1, 1, 0, PASS, nc.scalar.copy)
                 quantize_w2(1, 1, 0, PACK)
-        z0_bf = held([P, M, PACK], BF16, "x1_last")
-        for m0, m1 in chunks[0]:
-            round_z(0, m0, m1, nc.scalar.copy, z0_bf[:, m0:m1])
-        for i, (m0, m1) in enumerate(chunks[1]):
+
+        z0_bf = reused([P, M, PACK], BF16, "z0_bf", X1 + X_BYTES)
+        for m0, m1 in CHUNKS[0]:
+            quantize_z(0, m0, m1, nc.scalar.copy, z0_bf[:, m0:m1])
+        for m0, m1 in CHUNKS[1]:
             z1_bf = held([P, m1 - m0, PACK], BF16, f"z1_bf{m0}")
-            round_z(1, m0, m1, (nc.scalar.copy, nc.scalar.copy, nc.vector.tensor_copy)[i], z1_bf[:])
-        for i, (m0, m1) in enumerate(chunks[1]):
-            score(m0, m1, ((), (1,), (1,))[i])
+            quantize_z(1, m0, m1, nc.vector.tensor_copy if m1 == M else nc.scalar.copy, z1_bf[:])
+        for m0, m1 in CHUNKS[1]:
+            score(m0, m1)

@@ -25,11 +25,11 @@ LIST = 16
 SCALE_ROWS = 32
 HALF = M // 2
 
-CHUNKS = ([(0, HALF), (HALF, M)], [(0, HALF), (HALF, HALF + P), (HALF + P, M)])
+CHUNKS = ([(0, M)], [(0, HALF), (HALF, HALF + P), (HALF + P, M)])
 
 TABLE_0, TABLE_1, W1, X1 = 0, 4 * T, 8 * T, 10 * T
-QUARTER = T
 X_BYTES = 4 * S
+PIECE = 2 * T
 
 
 def tile_list_sound_change_dating_kernel(
@@ -51,7 +51,8 @@ def tile_list_sound_change_dating_kernel(
         taken = []
 
         def bank():
-            taken.append(psum.tile([P, BANK], F32, name=f"bank{len(taken) % BANKS}"))
+            shift = BANKS // 2 if len(taken) >= BANKS else 0
+            taken.append(psum.tile([P, BANK], F32, name=f"bank{(len(taken) + shift) % BANKS}"))
             return taken[-1]
 
         idx = keep.tile([P, S // LIST], U16, name="idx")
@@ -63,23 +64,34 @@ def tile_list_sound_change_dating_kernel(
         w1_s_raw = held([P, H], U8, "w1_s_raw")
         planes = [held([P, S + H], U8, f"plane{a}") for a in range(2)]
         v_cols, w1_cols = slice(0, S), slice(S, S + H)
-        for raw in (tab_s, w1_s_raw):
+        for raw, engine in ((tab_s, nc.vector), (w1_s_raw, nc.gpsimd)):
             for rows in (slice(32, 64), slice(64, P)):
-                nc.gpsimd.memset(raw[rows, :].bitcast(I32), 0)
+                engine.memset(raw[rows, :].bitcast(I32), 0)
         nc.gpsimd.memset(planes[1][:].bitcast(I32), 0)
 
+        warm = held([P, 2], F32, "warm")
+        nc.gpsimd.memset(warm[:, 0:1], 0.0)
+        nc.scalar.activation(warm[:, 1:2], warm[:, 0:1], ACT.Sigmoid)
+
         nc.sync.dma_start(idx[:], offs)
-        for raw, scales in ((tab_s, tab_scales), (w1_s_raw, w1_scales)):
-            nc.sync.dma_start(raw[:SCALE_ROWS, :].bitcast(I32), scales.rearrange("a q c -> (a q) c").bitcast(I32))
+        tab_w = [reused([P, T], I32, f"tab_w{a}", offset) for a, offset in enumerate((TABLE_0, TABLE_1))]
+        w1_raw = reused([P, 2, 2 * H], U8, "w1_raw", W1)
+        nc.sync.dma_start(tab_s[:SCALE_ROWS, :].bitcast(I32), tab_scales.rearrange("a q c -> (a q) c").bitcast(I32))
+        nc.sync.dma_start(w1_s_raw[:SCALE_ROWS, :].bitcast(I32), w1_scales.rearrange("a q c -> (a q) c").bitcast(I32))
         nc.sync.dma_start(p1[:], pos1)
         nc.sync.dma_start(p2[:], pos2)
         nc.sync.dma_start(p3[:], pos3)
-        w1_raw = reused([P, 2, 2 * H], U8, "w1_raw", W1)
+        nc.sync.dma_start(tab_w[0][:], tab_words[0].rearrange("p t i -> p (t i)").bitcast(I32))
         nc.sync.dma_start(w1_raw[:].bitcast(I32), w1_words.rearrange("a p c -> p a c").bitcast(I32))
-        tab_w = []
-        for a, offset in enumerate((TABLE_0, TABLE_1)):
-            tab_w.append(reused([P, T], I32, f"tab_w{a}", offset))
-            nc.sync.dma_start(tab_w[a][:], tab_words[a].rearrange("p t i -> p (t i)").bitcast(I32))
+        nc.sync.dma_start(tab_w[1][:], tab_words[1].rearrange("p t i -> p (t i)").bitcast(I32))
+
+        w2_raw = {}
+
+        def load_w2(b, a, tile):
+            w2_raw[b, a] = tile
+            rows = w2[PASS * a : PASS * (a + 1), PASS * b : PASS * (b + 1)]
+            nc.sync.dma_start(tile[:], rows.rearrange("(p j) c -> p j c", j=PACK))
+
 
         v_s_raw = held([P, S], U8, "v_s_raw")
         nc.vector.tensor_copy(v_s_raw[:], tab_s[:].indirect(idx[:]))
@@ -92,67 +104,59 @@ def tile_list_sound_change_dating_kernel(
             for q in range(4):
                 if (a, q) != (0, 0):
                     row = 16 * a + 4 * q
-                    queue = nc.gpsimd if a == 1 and q >= 2 else nc.scalar
+                    queue = nc.gpsimd if (a, q) == (1, 3) else nc.scalar
                     queue.dma_start(
                         planes[a][32 * q : 32 * q + 4, :].bitcast(I32), planes[0][row : row + 4, :].bitcast(I32)
                     )
 
-        w3_s = held([P, 2, N], U8, "w1_s_raw")
-        nc.gpsimd.memset(w3_s[:].bitcast(I32), 0)
-        for q in range(4):
-            nc.gpsimd.dma_start(
-                w3_s[32 * q : 32 * q + 4].bitcast(I32),
-                w3_scales[:, 4 * q : 4 * q + 4, :].rearrange("a r c -> r a c").bitcast(I32),
-            )
-        prior = held([P, N // P], F32, "v_s_raw")
-        with nc.allow_non_contiguous_dma(reason="one value of period to a partition"):
-            nc.gpsimd.dma_start(prior[:], period.rearrange("(c p) -> p c", p=P))
-
-        w1_w = held([P, 2, 2, PACK, 2 * P], U8, "w1_w")
-        nc.vector.tensor_copy(
-            w1_w[:].bitcast(U16), w1_raw[:].bitcast(U16).rearrange("p a (b m t) -> p a b t m", b=2, t=PACK)
-        )
-
         v_w = {}
-        for a in range(2):
+
+        def gather_table(a):
             for h in range(S // BANK):
                 v_w[a, h] = held([P, BANK], I32, f"v_w{a}{h}")
                 entries = idx[:, BANK // LIST * h : BANK // LIST * (h + 1)]
                 nc.vector.tensor_copy(v_w[a, h][:].bitcast(U32), tab_w[a][:].bitcast(U32).indirect(entries))
 
-        w2_raw = {}
+        gather_table(0)
+        w1_w = held([P, 2, 2, PACK, 2 * P], U8, "w1_w")
+        nc.vector.tensor_copy(
+            w1_w[:].bitcast(U16), w1_raw[:].bitcast(U16).rearrange("p a (b m t) -> p a b t m", b=2, t=PACK)
+        )
+        gather_table(1)
 
-        def load_w2(b, a, c0, c1, offset):
-            w2_raw[b, a, c0] = reused([P, PACK, c1 - c0], F32, f"w2_raw{b}{a}{c0}", offset)
-            rows = w2[PASS * a : PASS * (a + 1), PASS * b + c0 : PASS * b + c1]
-            nc.sync.dma_start(w2_raw[b, a, c0][:], rows.rearrange("(p j) c -> p j c", j=PACK))
+        for (b, a), offset in (((0, 0), TABLE_0), ((0, 1), W1), ((1, 0), TABLE_1)):
+            load_w2(b, a, reused([P, PACK, PASS], F32, f"w2_raw{b}{a}", offset))
 
-        load_w2(0, 0, 0, PASS, W1)
-        load_w2(0, 1, 0, PASS // 2, TABLE_0)
-        load_w2(0, 1, PASS // 2, PASS, TABLE_0 + QUARTER)
-        load_w2(1, 0, 0, PASS, TABLE_1 + QUARTER)
-
-        w2_bf = {(0, 0): reused([P, PACK, P, PACK], BF16, "w2_bf00", TABLE_1)}
-        for b, a in ((0, 1), (1, 0), (1, 1)):
-            w2_bf[b, a] = held([P, PACK, P, PACK], BF16, f"w2_bf{b}{a}")
-        w2_w = {(b, a): held([P, PASS], I32, f"w2_w{b}{a}") for b in range(2) for a in range(2)}
-        w2_s = {(b, a): held([P, PASS], U8, f"w2_s{b}{a}") for b in range(2) for a in range(2)}
-
-        def round_w2(b, a, c0, c1, copy):
-            dst = w2_bf[b, a][:, :, c0 // PACK : c1 // PACK, :].rearrange("p t m j -> p m j t")
-            src = w2_raw[b, a, c0][:].rearrange("p j (m t) -> p m j t", t=PACK)
-            for t0 in range(0, PACK, 2):
-                copy(dst[:, :, :, t0 : t0 + 2], src[:, :, :, t0 : t0 + 2])
-
-        def quantize_w2(b, a, t0, t1):
-            cols = slice(P * t0, P * t1)
-            nc.vector.quantize_mx(
-                w2_w[b, a][:, cols].bitcast(FP8X4),
-                w2_s[b, a][:, cols],
-                w2_bf[b, a][:, t0:t1].rearrange("p t m j -> p (t m j)"),
+        w3_s = reused([P, 2, N], U8, "w3_s", TABLE_1 + PIECE)
+        nc.gpsimd.memset(w3_s[:].bitcast(I32), 0)
+        for q in range(4):
+            nc.sync.dma_start(
+                w3_s[32 * q : 32 * q + 4].bitcast(I32),
+                w3_scales[:, 4 * q : 4 * q + 4, :].rearrange("a r c -> r a c").bitcast(I32),
             )
+        prior = reused([P, N // P], F32, "prior", TABLE_1 + PIECE + 2 * N)
+        with nc.allow_non_contiguous_dma(reason="one value of period to a partition"):
+            nc.sync.dma_start(prior[:], period.rearrange("(c p) -> p c", p=P))
 
-        def first_stage(x, words, scales, copy):
+        w2_w, w2_s = {}, {}
+
+        def prepare_w2(b, a, copies=(nc.vector.tensor_copy, nc.vector.tensor_copy)):
+            src = w2_raw[b, a][:].rearrange("p j (m t) -> p m j t", t=PACK)
+            rounded = []
+            for u in range(2):
+                if (b, a) == (0, 0):
+                    rounded.append(reused([P, 2, P, PACK], BF16, f"w2_bf00{u}", TABLE_1 + 3 * T + u * T // 2))
+                else:
+                    rounded.append(held([P, 2, P, PACK], BF16, f"w2_bf{b}{a}{u}"))
+                copies[u](rounded[u][:].rearrange("p t m j -> p m j t"), src[:, :, :, 2 * u : 2 * u + 2])
+            for u in range(2):
+                w2_w[b, a, u] = held([P, 2 * P], I32, f"w2_w{b}{a}{u}")
+                w2_s[b, a, u] = held([P, 2 * P], U8, f"w2_s{b}{a}{u}")
+                nc.vector.quantize_mx(
+                    w2_w[b, a, u][:].bitcast(FP8X4), w2_s[b, a, u][:], rounded[u][:].rearrange("p t m j -> p (t m j)")
+                )
+
+        def first_stage(x, words, scales):
             for h in range(S // BANK):
                 cols = slice(BANK * h, BANK * (h + 1))
                 acc = bank()
@@ -162,56 +166,44 @@ def tile_list_sound_change_dating_kernel(
                         rhs=v_w[a, h][:].bitcast(FP8X4), rhs_scale=planes[a][:, cols],
                         start=a == 0, stop=a == 1,
                     )
-                copy(x[:, cols], acc[:])
+                nc.scalar.copy(x[:, cols], acc[:])
             return x
 
-        def features(b, t):
-            if (b, t) == (0, 0):
-                place, copy = X1 + X_BYTES // 2, nc.vector.tensor_copy
-            else:
-                place, copy = X1 + X_BYTES * (t % 2), nc.scalar.copy
-            x1 = reused([P, S], F32, f"x1_{b}{t}", place)
+        def ancestor(b, t):
+            x1 = reused([P, S], F32, f"x1_{b}{t}", X1 + X_BYTES * ((b, t) == (0, 1)))
             first = S + PASS * b + P * t
             words = [w1_w[:, a, b, t, :].bitcast(FP4X4) for a in range(2)]
-            return first_stage(x1, words, [planes[a][:, first : first + P] for a in range(2)], copy)
-
-        def reflexes(b, t):
-            x2 = ring.tile([P, S], F32, name="x2", bufs=4)
-            cols = slice(P * t, P * (t + 1))
-            words = [w2_w[b, a][:, cols].bitcast(FP8X4) for a in range(2)]
-            return first_stage(x2, words, [w2_s[b, a][:, cols] for a in range(2)], nc.scalar.copy)
-
-        def ancestor(b, t, x1):
-            sig = ring.tile([P, M], F32, name="sig", bufs=3)
+            first_stage(x1, words, [planes[a][:, first : first + P] for a in range(2)])
+            sig = ring.tile([P, M], F32, name="sig", bufs=4)
             nc.scalar.activation(sig[:], x1[:].indirect(p1[:]), ACT.Sigmoid, scale=2.0)
-            if b == 0 and t < 2:
-                anc = reused([P, M], F32, f"anc{t}", TABLE_0 + QUARTER)
-            else:
+            return sig
+
+        def to_tanh(sig, anc=None):
+            if anc is None:
                 anc = ring.tile([P, M], F32, name="anc", bufs=4)
             nc.vector.tensor_scalar(anc[:], sig[:], 2.0, -1.0, ALU.mult, ALU.add)
             return anc
 
+        def reflexes(b, t):
+            x2 = ring.tile([P, S], F32, name="x2", bufs=4)
+            u, cols = t // 2, slice(P * (t % 2), P * (t % 2 + 1))
+            words = [w2_w[b, a, u][:, cols].bitcast(FP8X4) for a in range(2)]
+            return first_stage(x2, words, [w2_s[b, a, u][:, cols] for a in range(2)])
+
         z = {(b, m0): held([P, PACK, m1 - m0], F32, f"z{b}{m0}") for b in range(2) for m0, m1 in CHUNKS[b]}
         z_w, z_s = {}, {}
 
-        def combine(b, t, anc, x2):
-            weighed = ring.tile([P, M], F32, name="weighed", bufs=2)
+        def weigh(anc, x2, m0, m1):
+            weighed = ring.tile([P, m1 - m0], F32, name="weighed", bufs=3)
+            picked = x2[:].indirect(p2[:, m0 // LIST : m1 // LIST])
+            nc.vector.tensor_tensor(weighed[:], picked, anc[:, m0:m1], ALU.mult)
+            return weighed
 
-            def weigh(m0, m1):
-                picked = x2[:].indirect(p2[:, m0 // LIST : m1 // LIST])
-                nc.vector.tensor_tensor(weighed[:, m0:m1], picked, anc[:, m0:m1], ALU.mult)
-
-            def add_loan(m0, m1):
+        def add_loan(b, t, weighed, x2, chunks):
+            first = chunks[0][0]
+            for m0, m1 in chunks:
                 picked = x2[:].indirect(p3[:, m0 // LIST : m1 // LIST])
-                nc.vector.tensor_tensor(z[b, m0][:, t, :], picked, weighed[:, m0:m1], ALU.add)
-
-            last = (b, t) == (1, PACK - 1)
-            weigh(0, HALF)
-            if last:
-                add_loan(*CHUNKS[b][0])
-            weigh(HALF, M)
-            for m0, m1 in CHUNKS[b][1:] if last else CHUNKS[b]:
-                add_loan(m0, m1)
+                nc.vector.tensor_tensor(z[b, m0][:, t, :], picked, weighed[:, m0 - first : m1 - first], ALU.add)
 
         def quantize_z(b, m0, m1, copy, z_bf):
             copy(z_bf.rearrange("p (c i) t -> p c t i", i=4), z[b, m0][:].rearrange("p t (c i) -> p c t i", i=4))
@@ -221,7 +213,7 @@ def tile_list_sound_change_dating_kernel(
 
         def score(m0, m1):
             y = held([P, N // P, m1 - m0], F32, f"y{m0}")
-            chunk_starts = (m0 // HALF * HALF, m0)
+            chunk_starts = (0, m0)
             for c in range(N // P):
                 cols = slice(P * c, P * (c + 1))
                 acc = bank()[:, : m1 - m0]
@@ -238,36 +230,39 @@ def tile_list_sound_change_dating_kernel(
                     nc.scalar.activation(y[:, c, :], acc, ACT.Identity, bias=prior[:, c : c + 1])
             nc.sync.dma_start(out.rearrange("(c p) m -> p c m", p=P)[:, :, m0:m1], y[:])
 
-        round_w2(0, 0, 0, PASS, nc.vector.tensor_copy)
-        load_w2(1, 1, 0, PASS, W1)
-        quantize_w2(0, 0, 0, PACK)
-        round_w2(0, 1, 0, PASS // 2, nc.vector.tensor_copy)
-        round_w2(0, 1, PASS // 2, PASS, nc.vector.tensor_copy)
-        quantize_w2(0, 1, 0, 2)
-        anc = ancestor(0, 0, features(0, 0))
-        quantize_w2(0, 1, 2, PACK)
+        def round_z(b, m0, m1, copy):
+            quantize_z(b, m0, m1, copy, held([P, m1 - m0, PACK], BF16, f"z_bf{b}{m0}")[:])
 
-        tiles = [(b, t) for b in range(2) for t in range(PACK)]
-        for (b, t), ahead in zip(tiles, tiles[1:] + [None]):
-            x1 = features(*ahead) if ahead else None
+        prepare_w2(0, 0)
+        load_w2(1, 1, reused([P, PACK, PASS], F32, "w2_raw11", TABLE_0))
+        sig = [ancestor(0, t) for t in range(2)]
+        prepare_w2(0, 1)
+        w3_w = reused([P, 2, N], I32, "w3_w", W1 + T)
+        nc.sync.dma_start(w3_w[:], w3_words.rearrange("a p c i -> p a (c i)").bitcast(I32))
+        anc = [to_tanh(sig[t], reused([P, M], F32, f"anc{t}", W1 + 4 * M * t)) for t in range(2)]
+        x2 = [reflexes(0, t) for t in range(2)]
+        prepare_w2(1, 0)
+        weighed = [weigh(anc[t], x2[t], 0, M) for t in range(2)]
+        add_loan(0, 0, weighed[0], x2[0], CHUNKS[0])
+        waiting = (0, 1, weighed[1], x2[1], CHUNKS[0])
+        for b, t in [(b, t) for b in range(2) for t in range(PACK)][2:]:
+            sig = ancestor(b, t)
             x2 = reflexes(b, t)
-            anc_ahead = ancestor(*ahead, x1) if ahead else None
-            combine(b, t, anc, x2)
-            anc = anc_ahead
-            if (b, t) == (0, 0):
-                round_w2(1, 0, 0, PASS, nc.vector.tensor_copy)
-                w3_w = reused([P, 2, N], I32, "w3_w", TABLE_1 + QUARTER)
-                nc.sync.dma_start(w3_w[:], w3_words.rearrange("a p c i -> p a (c i)").bitcast(I32))
-                quantize_w2(1, 0, 0, PACK)
             if (b, t) == (0, 2):
-                round_w2(1, 1, 0, PASS, nc.scalar.copy)
-                quantize_w2(1, 1, 0, PACK)
+                prepare_w2(1, 1, (nc.scalar.copy, nc.scalar.copy))
+            anc = to_tanh(sig)
+            if (b, t) == (1, PACK - 1):
+                add_loan(*waiting)
+                add_loan(b, t, weigh(anc, x2, 0, HALF), x2, CHUNKS[b][:1])
+                add_loan(b, t, weigh(anc, x2, HALF, M), x2, CHUNKS[b][1:])
+            else:
+                weighed = weigh(anc, x2, 0, M)
+                add_loan(*waiting)
+                waiting = (b, t, weighed, x2, CHUNKS[b])
+            if (b, t) == (1, 0):
+                round_z(0, 0, M, nc.vector.tensor_copy)
 
-        z0_bf = reused([P, M, PACK], BF16, "z0_bf", X1 + X_BYTES)
-        for m0, m1 in CHUNKS[0]:
-            quantize_z(0, m0, m1, nc.scalar.copy, z0_bf[:, m0:m1])
         for m0, m1 in CHUNKS[1]:
-            z1_bf = held([P, m1 - m0, PACK], BF16, f"z1_bf{m0}")
-            quantize_z(1, m0, m1, nc.vector.tensor_copy if m1 == M else nc.scalar.copy, z1_bf[:])
+            round_z(1, m0, m1, nc.vector.tensor_copy if m1 == M else nc.scalar.copy)
         for m0, m1 in CHUNKS[1]:
             score(m0, m1)

@@ -193,17 +193,23 @@ def tile_list_sound_change_dating_kernel(
         z = {(b, m0): held([P, PACK, m1 - m0], F32, f"z{b}{m0}") for b in range(2) for m0, m1 in CHUNKS[b]}
         z_w, z_s = {}, {}
 
-        def weigh(anc, x2, m0, m1):
-            weighed = ring.tile([P, m1 - m0], F32, name="weighed", bufs=3)
+        def weigh(anc, x2, m0, m1, weighed=None):
+            if weighed is None:
+                weighed = ring.tile([P, m1 - m0], F32, name="weighed", bufs=4)
             picked = x2[:].indirect(p2[:, m0 // LIST : m1 // LIST])
             nc.vector.tensor_tensor(weighed[:], picked, anc[:, m0:m1], ALU.mult)
             return weighed
 
-        def add_loan(b, t, weighed, x2, chunks):
-            first = chunks[0][0]
-            for m0, m1 in chunks:
-                picked = x2[:].indirect(p3[:, m0 // LIST : m1 // LIST])
-                nc.vector.tensor_tensor(z[b, m0][:, t, :], picked, weighed[:, m0 - first : m1 - first], ALU.add)
+        def add_loan(b, t, weighed, x2, m0, m1):
+            start = max(c0 for c0, c1 in CHUNKS[b] if c0 <= m0)
+            picked = x2[:].indirect(p3[:, m0 // LIST : m1 // LIST])
+            nc.vector.tensor_tensor(z[b, start][:, t, m0 - start : m1 - start], picked, weighed, ALU.add)
+
+        def combine(b, t, anc, x2):
+            low, high = weigh(anc, x2, 0, HALF), weigh(anc, x2, HALF, M)
+            add_loan(b, t, low[:], x2, 0, HALF)
+            for m0, m1 in CHUNKS[b][1:] or [(HALF, M)]:
+                add_loan(b, t, high[:, m0 - HALF : m1 - HALF], x2, m0, m1)
 
         def quantize_z(b, m0, m1, copy, z_bf):
             copy(z_bf.rearrange("p (c i) t -> p c t i", i=4), z[b, m0][:].rearrange("p t (c i) -> p c t i", i=4))
@@ -242,25 +248,23 @@ def tile_list_sound_change_dating_kernel(
         anc = [to_tanh(sig[t], reused([P, M], F32, f"anc{t}", W1 + 4 * M * t)) for t in range(2)]
         x2 = [reflexes(0, t) for t in range(2)]
         prepare_w2(1, 0)
-        weighed = [weigh(anc[t], x2[t], 0, M) for t in range(2)]
-        add_loan(0, 0, weighed[0], x2[0], CHUNKS[0])
-        waiting = (0, 1, weighed[1], x2[1], CHUNKS[0])
-        for b, t in [(b, t) for b in range(2) for t in range(PACK)][2:]:
+        for t in range(2):
+            combine(0, t, anc[t], x2[t])
+        for b, t in [(b, t) for b in range(2) for t in range(PACK)][2:-1]:
             sig = ancestor(b, t)
             x2 = reflexes(b, t)
             if (b, t) == (0, 2):
                 prepare_w2(1, 1, (nc.scalar.copy, nc.scalar.copy))
-            anc = to_tanh(sig)
-            if (b, t) == (1, PACK - 1):
-                add_loan(*waiting)
-                add_loan(b, t, weigh(anc, x2, 0, HALF), x2, CHUNKS[b][:1])
-                add_loan(b, t, weigh(anc, x2, HALF, M), x2, CHUNKS[b][1:])
-            else:
-                weighed = weigh(anc, x2, 0, M)
-                add_loan(*waiting)
-                waiting = (b, t, weighed, x2, CHUNKS[b])
-            if (b, t) == (1, 0):
-                round_z(0, 0, M, nc.vector.tensor_copy)
+            combine(b, t, to_tanh(sig), x2)
+
+        b, t = 1, PACK - 1
+        anc = to_tanh(ancestor(b, t))
+        x2 = reflexes(b, t)
+        quantize_z(0, 0, M, nc.scalar.copy, reused([P, M, PACK], BF16, "z0_bf", X1)[:])
+        add_loan(b, t, weigh(anc, x2, 0, HALF)[:], x2, 0, HALF)
+        high = weigh(anc, x2, HALF, M, reused([P, HALF], F32, "last_weighed", X1))
+        for m0, m1 in CHUNKS[b][1:]:
+            add_loan(b, t, high[:, m0 - HALF : m1 - HALF], x2, m0, m1)
 
         for m0, m1 in CHUNKS[1]:
             round_z(1, m0, m1, nc.vector.tensor_copy if m1 == M else nc.scalar.copy)

@@ -156,24 +156,26 @@ def tile_list_sound_change_dating_kernel(
                     w2_w[b, a, u][:].bitcast(FP8X4), w2_s[b, a, u][:], rounded[u][:].rearrange("p t m j -> p (t m j)")
                 )
 
-        def first_stage(x, words, scales):
-            for h in range(S // BANK):
-                cols = slice(BANK * h, BANK * (h + 1))
-                acc = bank()
-                for a in range(2):
-                    nc.tensor.matmul_mx(
-                        acc[:], lhsT=words[a], lhsT_scale=scales[a],
-                        rhs=v_w[a, h][:].bitcast(FP8X4), rhs_scale=planes[a][:, cols],
-                        start=a == 0, stop=a == 1,
-                    )
-                nc.scalar.copy(x[:, cols], acc[:])
-            return x
+        def first_stage(x, h, words, scales):
+            cols = slice(BANK * h, BANK * (h + 1))
+            acc = bank()
+            for a in range(2):
+                nc.tensor.matmul_mx(
+                    acc[:], lhsT=words[a], lhsT_scale=scales[a],
+                    rhs=v_w[a, h][:].bitcast(FP8X4), rhs_scale=planes[a][:, cols],
+                    start=a == 0, stop=a == 1,
+                )
+            nc.scalar.copy(x[:, cols], acc[:])
 
-        def ancestor(b, t):
+        def features(b, t):
             x1 = reused([P, S], F32, f"x1_{b}{t}", X1 + X_BYTES * ((b, t) == (0, 1)))
             first = S + PASS * b + P * t
             words = [w1_w[:, a, b, t, :].bitcast(FP4X4) for a in range(2)]
-            first_stage(x1, words, [planes[a][:, first : first + P] for a in range(2)])
+            for h in range(2):
+                first_stage(x1, h, words, [planes[a][:, first : first + P] for a in range(2)])
+            return x1
+
+        def sigmoid(x1):
             sig = ring.tile([P, M], F32, name="sig", bufs=4)
             nc.scalar.activation(sig[:], x1[:].indirect(p1[:]), ACT.Sigmoid, scale=2.0)
             return sig
@@ -181,14 +183,22 @@ def tile_list_sound_change_dating_kernel(
         def to_tanh(sig, anc=None):
             if anc is None:
                 anc = ring.tile([P, M], F32, name="anc", bufs=4)
-            nc.vector.tensor_scalar(anc[:], sig[:], 2.0, -1.0, ALU.mult, ALU.add)
+            for m0 in (0, HALF):
+                nc.vector.tensor_scalar(anc[:, m0 : m0 + HALF], sig[:, m0 : m0 + HALF], 2.0, -1.0, ALU.mult, ALU.add)
             return anc
 
-        def reflexes(b, t):
-            x2 = ring.tile([P, S], F32, name="x2", bufs=4)
+        def reflexes(b, t, x2, h):
             u, cols = t // 2, slice(P * (t % 2), P * (t % 2 + 1))
             words = [w2_w[b, a, u][:, cols].bitcast(FP8X4) for a in range(2)]
-            return first_stage(x2, words, [w2_s[b, a, u][:, cols] for a in range(2)])
+            first_stage(x2, h, words, [w2_s[b, a, u][:, cols] for a in range(2)])
+
+        def row_tile(b, t):
+            x1 = features(b, t)
+            x2 = ring.tile([P, S], F32, name="x2", bufs=4)
+            reflexes(b, t, x2, 0)
+            sig = sigmoid(x1)
+            reflexes(b, t, x2, 1)
+            return sig, x2
 
         z = {(b, m0): held([P, PACK, m1 - m0], F32, f"z{b}{m0}") for b in range(2) for m0, m1 in CHUNKS[b]}
         z_w, z_s = {}, {}
@@ -241,30 +251,35 @@ def tile_list_sound_change_dating_kernel(
 
         prepare_w2(0, 0)
         load_w2(1, 1, reused([P, PACK, PASS], F32, "w2_raw11", TABLE_0))
-        sig = [ancestor(0, t) for t in range(2)]
+        sig = [sigmoid(x1) for x1 in [features(0, t) for t in range(2)]]
         prepare_w2(0, 1)
         w3_w = reused([P, 2, N], I32, "w3_w", W1 + T)
         nc.sync.dma_start(w3_w[:], w3_words.rearrange("a p c i -> p a (c i)").bitcast(I32))
         anc = [to_tanh(sig[t], reused([P, M], F32, f"anc{t}", W1 + 4 * M * t)) for t in range(2)]
-        x2 = [reflexes(0, t) for t in range(2)]
+        x2 = []
+        for t in range(2):
+            x2.append(ring.tile([P, S], F32, name="x2", bufs=4))
+            for h in range(2):
+                reflexes(0, t, x2[t], h)
         prepare_w2(1, 0)
         for t in range(2):
             combine(0, t, anc[t], x2[t])
         for b, t in [(b, t) for b in range(2) for t in range(PACK)][2:-1]:
-            sig = ancestor(b, t)
-            x2 = reflexes(b, t)
+            sig, x2 = row_tile(b, t)
             if (b, t) == (0, 2):
                 prepare_w2(1, 1, (nc.scalar.copy, nc.scalar.copy))
             combine(b, t, to_tanh(sig), x2)
 
         b, t = 1, PACK - 1
-        anc = to_tanh(ancestor(b, t))
-        x2 = reflexes(b, t)
+        sig, x2 = row_tile(b, t)
+        anc = to_tanh(sig)
         quantize_z(0, 0, M, nc.scalar.copy, reused([P, M, PACK], BF16, "z0_bf", X1)[:])
-        add_loan(b, t, weigh(anc, x2, 0, HALF)[:], x2, 0, HALF)
-        high = weigh(anc, x2, HALF, M, reused([P, HALF], F32, "last_weighed", X1))
-        for m0, m1 in CHUNKS[b][1:]:
-            add_loan(b, t, high[:, m0 - HALF : m1 - HALF], x2, m0, m1)
+        first, second, third = CHUNKS[b]
+        weighed = [weigh(anc, x2, *first), weigh(anc, x2, *second)]
+        add_loan(b, t, weighed[0][:], x2, *first)
+        weighed.append(weigh(anc, x2, *third, reused([P, P], F32, "last_weighed", X1)))
+        add_loan(b, t, weighed[1][:], x2, *second)
+        add_loan(b, t, weighed[2][:], x2, *third)
 
         for m0, m1 in CHUNKS[1]:
             round_z(1, m0, m1, nc.vector.tensor_copy if m1 == M else nc.scalar.copy)

@@ -48,12 +48,8 @@ def tile_list_sound_change_dating_kernel(
         def reused(shape, dtype, name, offset):
             return reuse.tile(shape, dtype, name=name, offset=offset, align_bytes=64)
 
-        taken = []
-
-        def bank():
-            shift = BANKS // 2 if len(taken) >= BANKS else 0
-            taken.append(psum.tile([P, BANK], F32, name=f"bank{(len(taken) + shift) % BANKS}"))
-            return taken[-1]
+        def bank(i):
+            return psum.tile([P, BANK], F32, name=f"bank{i % BANKS}")
 
         idx = keep.tile([P, S // LIST], U16, name="idx")
         p1 = keep.tile([P, M // LIST], U16, name="p1")
@@ -156,9 +152,9 @@ def tile_list_sound_change_dating_kernel(
                     w2_w[b, a, u][:].bitcast(FP8X4), w2_s[b, a, u][:], rounded[u][:].rearrange("p t m j -> p (t m j)")
                 )
 
-        def first_stage(x, h, words, scales):
+        def first_stage(x, h, words, scales, pair):
             cols = slice(BANK * h, BANK * (h + 1))
-            acc = bank()
+            acc = bank(2 * pair + h)
             for a in range(2):
                 nc.tensor.matmul_mx(
                     acc[:], lhsT=words[a], lhsT_scale=scales[a],
@@ -168,11 +164,14 @@ def tile_list_sound_change_dating_kernel(
             nc.scalar.copy(x[:, cols], acc[:])
 
         def features(b, t):
-            x1 = reused([P, S], F32, f"x1_{b}{t}", X1 + X_BYTES * ((b, t) == (0, 1)))
+            if (b, t) == (1, PACK - 1):
+                x1 = reused([P, S], F32, "x1_last", X1)
+            else:
+                x1 = ring.tile([P, S], F32, name="x1", bufs=3)
             first = S + PASS * b + P * t
             words = [w1_w[:, a, b, t, :].bitcast(FP4X4) for a in range(2)]
             for h in range(2):
-                first_stage(x1, h, words, [planes[a][:, first : first + P] for a in range(2)])
+                first_stage(x1, h, words, [planes[a][:, first : first + P] for a in range(2)], PACK * b + t)
             return x1
 
         def sigmoid(x1):
@@ -183,22 +182,16 @@ def tile_list_sound_change_dating_kernel(
         def to_tanh(sig, anc=None):
             if anc is None:
                 anc = ring.tile([P, M], F32, name="anc", bufs=4)
-            for m0 in (0, HALF):
-                nc.vector.tensor_scalar(anc[:, m0 : m0 + HALF], sig[:, m0 : m0 + HALF], 2.0, -1.0, ALU.mult, ALU.add)
+            nc.vector.tensor_scalar(anc[:], sig[:], 2.0, -1.0, ALU.mult, ALU.add)
             return anc
 
         def reflexes(b, t, x2, h):
             u, cols = t // 2, slice(P * (t % 2), P * (t % 2 + 1))
             words = [w2_w[b, a, u][:, cols].bitcast(FP8X4) for a in range(2)]
-            first_stage(x2, h, words, [w2_s[b, a, u][:, cols] for a in range(2)])
+            first_stage(x2, h, words, [w2_s[b, a, u][:, cols] for a in range(2)], PACK * b + t + 3)
 
-        def row_tile(b, t):
-            x1 = features(b, t)
-            x2 = ring.tile([P, S], F32, name="x2", bufs=4)
-            reflexes(b, t, x2, 0)
-            sig = sigmoid(x1)
-            reflexes(b, t, x2, 1)
-            return sig, x2
+        def x2_tile():
+            return ring.tile([P, S], F32, name="x2", bufs=4)
 
         z = {(b, m0): held([P, PACK, m1 - m0], F32, f"z{b}{m0}") for b in range(2) for m0, m1 in CHUNKS[b]}
         z_w, z_s = {}, {}
@@ -232,7 +225,7 @@ def tile_list_sound_change_dating_kernel(
             chunk_starts = (0, m0)
             for c in range(N // P):
                 cols = slice(P * c, P * (c + 1))
-                acc = bank()[:, : m1 - m0]
+                acc = bank(3 * CHUNKS[1].index((m0, m1)) + c + 6)[:, : m1 - m0]
                 for b, start in enumerate(chunk_starts):
                     part = slice(m0 - start, m1 - start)
                     nc.tensor.matmul_mx(
@@ -251,28 +244,40 @@ def tile_list_sound_change_dating_kernel(
 
         prepare_w2(0, 0)
         load_w2(1, 1, reused([P, PACK, PASS], F32, "w2_raw11", TABLE_0))
-        sig = [sigmoid(x1) for x1 in [features(0, t) for t in range(2)]]
+        tiles = [(b, t) for b in range(2) for t in range(PACK)]
+        x1 = [features(0, t) for t in range(2)]
+        sig = [sigmoid(x1[0])]
+        x1.append(features(0, 2))
+        sig.append(sigmoid(x1[1]))
         prepare_w2(0, 1)
         w3_w = reused([P, 2, N], I32, "w3_w", W1 + T)
         nc.sync.dma_start(w3_w[:], w3_words.rearrange("a p c i -> p a (c i)").bitcast(I32))
         anc = [to_tanh(sig[t], reused([P, M], F32, f"anc{t}", W1 + 4 * M * t)) for t in range(2)]
-        x2 = []
-        for t in range(2):
-            x2.append(ring.tile([P, S], F32, name="x2", bufs=4))
-            for h in range(2):
-                reflexes(0, t, x2[t], h)
+        x2 = [x2_tile()]
+        for h in range(2):
+            reflexes(0, 0, x2[0], h)
+        anc.append(to_tanh(sigmoid(x1[2])))
+        x2.append(x2_tile())
+        for h in range(2):
+            reflexes(0, 1, x2[1], h)
+        combine(0, 0, anc[0], x2[0])
         prepare_w2(1, 0)
-        for t in range(2):
-            combine(0, t, anc[t], x2[t])
-        for b, t in [(b, t) for b in range(2) for t in range(PACK)][2:-1]:
-            sig, x2 = row_tile(b, t)
-            if (b, t) == (0, 2):
+        combine(0, 1, anc[1], x2[1])
+        for k in range(2, len(tiles) - 1):
+            ahead = features(*tiles[k + 1])
+            x2 = x2_tile()
+            reflexes(*tiles[k], x2, 0)
+            reflexes(*tiles[k], x2, 1)
+            anc.append(to_tanh(sigmoid(ahead)))
+            if k == 2:
                 prepare_w2(1, 1, (nc.scalar.copy, nc.scalar.copy))
-            combine(b, t, to_tanh(sig), x2)
+            combine(*tiles[k], anc[k], x2)
 
-        b, t = 1, PACK - 1
-        sig, x2 = row_tile(b, t)
-        anc = to_tanh(sig)
+        b, t = tiles[-1]
+        x2 = x2_tile()
+        for h in range(2):
+            reflexes(b, t, x2, h)
+        anc = anc[-1]
         quantize_z(0, 0, M, nc.scalar.copy, reused([P, M, PACK], BF16, "z0_bf", X1)[:])
         first, second, third = CHUNKS[b]
         weighed = [weigh(anc, x2, *first), weigh(anc, x2, *second)]

@@ -25,7 +25,7 @@ LIST = 16
 SCALE_ROWS = 32
 HALF = M // 2
 
-CHUNKS = ([(0, M)], [(0, HALF), (HALF, HALF + P), (HALF + P, M)])
+CHUNKS = ([(0, HALF), (HALF, M)], [(0, HALF), (HALF, HALF + P), (HALF + P, M)])
 
 TABLE_0, TABLE_1, W1, X1 = 0, 4 * T, 8 * T, 10 * T
 X_BYTES = 4 * S
@@ -71,14 +71,15 @@ def tile_list_sound_change_dating_kernel(
 
         nc.sync.dma_start(idx[:], offs)
         tab_w = [reused([P, T], I32, f"tab_w{a}", offset) for a, offset in enumerate((TABLE_0, TABLE_1))]
-        w1_raw = reused([P, 2, 2 * H], U8, "w1_raw", W1)
-        nc.sync.dma_start(tab_s[:SCALE_ROWS, :].bitcast(I32), tab_scales.rearrange("a q c -> (a q) c").bitcast(I32))
+        w1_halves = w1_words.rearrange("a p (b c) -> b p a c", b=2)
+        w1_raw = held([P, 2, H], U8, "w1_raw")
         nc.sync.dma_start(w1_s_raw[:SCALE_ROWS, :].bitcast(I32), w1_scales.rearrange("a q c -> (a q) c").bitcast(I32))
+        nc.sync.dma_start(tab_s[:SCALE_ROWS, :].bitcast(I32), tab_scales.rearrange("a q c -> (a q) c").bitcast(I32))
         nc.sync.dma_start(p1[:], pos1)
         nc.sync.dma_start(p2[:], pos2)
         nc.sync.dma_start(p3[:], pos3)
+        nc.sync.dma_start(w1_raw[:].bitcast(I32), w1_halves[0].bitcast(I32))
         nc.sync.dma_start(tab_w[0][:], tab_words[0].rearrange("p t i -> p (t i)").bitcast(I32))
-        nc.sync.dma_start(w1_raw[:].bitcast(I32), w1_words.rearrange("a p c -> p a c").bitcast(I32))
         nc.sync.dma_start(tab_w[1][:], tab_words[1].rearrange("p t i -> p (t i)").bitcast(I32))
 
         w2_raw = {}
@@ -90,11 +91,11 @@ def tile_list_sound_change_dating_kernel(
 
 
         v_s_raw = held([P, S], U8, "v_s_raw")
-        nc.vector.tensor_copy(v_s_raw[:], tab_s[:].indirect(idx[:]))
         nc.vector.tensor_copy(
             planes[0][:, w1_cols].rearrange("p (b t m) -> p b t m", b=2, t=PACK),
             w1_s_raw[:].rearrange("p (b m t) -> p b t m", b=2, t=PACK),
         )
+        nc.vector.tensor_copy(v_s_raw[:], tab_s[:].indirect(idx[:]))
         nc.vector.tensor_copy(planes[0][:, v_cols].bitcast(I32), v_s_raw[:].bitcast(I32))
         for a in range(2):
             for q in range(4):
@@ -113,18 +114,24 @@ def tile_list_sound_change_dating_kernel(
                 entries = idx[:, BANK // LIST * h : BANK // LIST * (h + 1)]
                 nc.vector.tensor_copy(v_w[a, h][:].bitcast(U32), tab_w[a][:].bitcast(U32).indirect(entries))
 
+        w1_w = {}
+
+        def order_w1(b, raw):
+            w1_w[b] = held([P, 2, PACK, 2 * P], U8, f"w1_w{b}")
+            nc.vector.tensor_copy(w1_w[b][:].bitcast(U16), raw[:].bitcast(U16).rearrange("p a (m t) -> p a t m", t=PACK))
+
+        order_w1(0, w1_raw)
         gather_table(0)
-        w1_w = held([P, 2, 2, PACK, 2 * P], U8, "w1_w")
-        nc.vector.tensor_copy(
-            w1_w[:].bitcast(U16), w1_raw[:].bitcast(U16).rearrange("p a (b m t) -> p a b t m", b=2, t=PACK)
-        )
         gather_table(1)
 
-        for (b, a), offset in (((0, 0), TABLE_0), ((0, 1), W1), ((1, 0), TABLE_1)):
-            load_w2(b, a, reused([P, PACK, PASS], F32, f"w2_raw{b}{a}", offset))
+        load_w2(0, 0, reused([P, PACK, PASS], F32, "w2_raw00", TABLE_0 + PIECE))
+        load_w2(0, 1, reused([P, PACK, PASS], F32, "w2_raw01", TABLE_0))
+        w1_late = reused([P, 2, H], U8, "w1_late", TABLE_1 + PIECE + H)
+        nc.sync.dma_start(w1_late[:].bitcast(I32), w1_halves[1].bitcast(I32))
+        load_w2(1, 0, reused([P, PACK, PASS], F32, "w2_raw10", TABLE_1))
 
         w3_s = reused([P, 2, N], U8, "w3_s", TABLE_1 + PIECE)
-        nc.gpsimd.memset(w3_s[:].bitcast(I32), 0)
+        nc.vector.memset(w3_s[:].bitcast(I32), 0)
         for q in range(4):
             nc.sync.dma_start(
                 w3_s[32 * q : 32 * q + 4].bitcast(I32),
@@ -152,9 +159,9 @@ def tile_list_sound_change_dating_kernel(
                     w2_w[b, a, u][:].bitcast(FP8X4), w2_s[b, a, u][:], rounded[u][:].rearrange("p t m j -> p (t m j)")
                 )
 
-        def first_stage(x, h, words, scales, pair):
+        def first_stage(x, h, words, scales, pair, shift=0):
             cols = slice(BANK * h, BANK * (h + 1))
-            acc = bank(2 * pair + h)
+            acc = bank(2 * pair + h + shift)
             for a in range(2):
                 nc.tensor.matmul_mx(
                     acc[:], lhsT=words[a], lhsT_scale=scales[a],
@@ -163,15 +170,17 @@ def tile_list_sound_change_dating_kernel(
                 )
             nc.scalar.copy(x[:, cols], acc[:])
 
-        def features(b, t):
-            if (b, t) == (1, PACK - 1):
+        def features(b, t, x1=None, halves=(0, 1), shift=0):
+            if x1 is not None:
+                pass
+            elif (b, t) == (1, PACK - 1):
                 x1 = reused([P, S], F32, "x1_last", X1)
             else:
                 x1 = ring.tile([P, S], F32, name="x1", bufs=3)
             first = S + PASS * b + P * t
-            words = [w1_w[:, a, b, t, :].bitcast(FP4X4) for a in range(2)]
-            for h in range(2):
-                first_stage(x1, h, words, [planes[a][:, first : first + P] for a in range(2)], PACK * b + t)
+            words = [w1_w[b][:, a, t, :].bitcast(FP4X4) for a in range(2)]
+            for h in halves:
+                first_stage(x1, h, words, [planes[a][:, first : first + P] for a in range(2)], PACK * b + t, shift)
             return x1
 
         def sigmoid(x1):
@@ -222,18 +231,18 @@ def tile_list_sound_change_dating_kernel(
 
         def score(m0, m1):
             y = held([P, N // P, m1 - m0], F32, f"y{m0}")
-            chunk_starts = (0, m0)
-            for c in range(N // P):
-                cols = slice(P * c, P * (c + 1))
-                acc = bank(3 * CHUNKS[1].index((m0, m1)) + c + 6)[:, : m1 - m0]
-                for b, start in enumerate(chunk_starts):
-                    part = slice(m0 - start, m1 - start)
+            accs = [bank(3 * CHUNKS[1].index((m0, m1)) + c + 6)[:, : m1 - m0] for c in range(N // P)]
+            for b, start in enumerate((min(m0, HALF), m0)):
+                part = slice(m0 - start, m1 - start)
+                for c, acc in enumerate(accs):
+                    cols = slice(P * c, P * (c + 1))
                     nc.tensor.matmul_mx(
                         acc, lhsT=w3_w[:, b, cols].bitcast(FP8X4), lhsT_scale=w3_s[:, b, cols],
                         rhs=z_w[b, start][:, part].bitcast(FP8X4), rhs_scale=z_s[b, start][:, part],
                         start=b == 0, stop=b == 1,
                     )
-                if c == 1 and m1 - m0 < HALF:
+            for c, acc in enumerate(accs):
+                if c == 1 and m0:
                     nc.vector.tensor_scalar(y[:, c, :], acc, prior[:, c : c + 1], None, ALU.add)
                 else:
                     nc.scalar.activation(y[:, c, :], acc, ACT.Identity, bias=prior[:, c : c + 1])
@@ -243,25 +252,27 @@ def tile_list_sound_change_dating_kernel(
             quantize_z(b, m0, m1, copy, held([P, m1 - m0, PACK], BF16, f"z_bf{b}{m0}")[:])
 
         prepare_w2(0, 0)
-        load_w2(1, 1, reused([P, PACK, PASS], F32, "w2_raw11", TABLE_0))
+        load_w2(1, 1, reused([P, PACK, PASS], F32, "w2_raw11", TABLE_0 + PIECE))
         tiles = [(b, t) for b in range(2) for t in range(PACK)]
         x1 = [features(0, t) for t in range(2)]
         sig = [sigmoid(x1[0])]
-        x1.append(features(0, 2))
+        x1.append(features(0, 2, halves=(0,)))
         sig.append(sigmoid(x1[1]))
         prepare_w2(0, 1)
-        w3_w = reused([P, 2, N], I32, "w3_w", W1 + T)
+        w3_w = reused([P, 2, N], I32, "w3_w", TABLE_0 + T)
         nc.sync.dma_start(w3_w[:], w3_words.rearrange("a p c i -> p a (c i)").bitcast(I32))
-        anc = [to_tanh(sig[t], reused([P, M], F32, f"anc{t}", W1 + 4 * M * t)) for t in range(2)]
+        anc = [to_tanh(sig[t], reused([P, M], F32, f"anc{t}", TABLE_0 + 4 * M * t)) for t in range(2)]
         x2 = [x2_tile()]
         for h in range(2):
             reflexes(0, 0, x2[0], h)
-        anc.append(to_tanh(sigmoid(x1[2])))
+        features(0, 2, x1[2], halves=(1,), shift=1)
         x2.append(x2_tile())
         for h in range(2):
             reflexes(0, 1, x2[1], h)
+        anc.append(to_tanh(sigmoid(x1[2])))
         combine(0, 0, anc[0], x2[0])
         prepare_w2(1, 0)
+        order_w1(1, w1_late)
         combine(0, 1, anc[1], x2[1])
         for k in range(2, len(tiles) - 1):
             ahead = features(*tiles[k + 1])
@@ -278,7 +289,8 @@ def tile_list_sound_change_dating_kernel(
         for h in range(2):
             reflexes(b, t, x2, h)
         anc = anc[-1]
-        quantize_z(0, 0, M, nc.scalar.copy, reused([P, M, PACK], BF16, "z0_bf", X1)[:])
+        for m0, m1 in CHUNKS[0]:
+            quantize_z(0, m0, m1, nc.scalar.copy, reused([P, HALF, PACK], BF16, f"z0_bf{m0}", X1 + 2 * PACK * m0)[:])
         first, second, third = CHUNKS[b]
         weighed = [weigh(anc, x2, *first), weigh(anc, x2, *second)]
         add_loan(b, t, weighed[0][:], x2, *first)
@@ -287,6 +299,6 @@ def tile_list_sound_change_dating_kernel(
         add_loan(b, t, weighed[2][:], x2, *third)
 
         for m0, m1 in CHUNKS[1]:
-            round_z(1, m0, m1, nc.vector.tensor_copy if m1 == M else nc.scalar.copy)
+            round_z(1, m0, m1, nc.scalar.copy if m0 == HALF else nc.vector.tensor_copy)
         for m0, m1 in CHUNKS[1]:
             score(m0, m1)

@@ -69,16 +69,16 @@ def tile_list_sound_change_dating_kernel(
         nc.gpsimd.memset(warm[:, 0:1], 0.0)
         nc.scalar.activation(warm[:, 1:2], warm[:, 0:1], ACT.Sigmoid)
 
-        nc.sync.dma_start(idx[:], offs)
         tab_w = [reused([P, T], I32, f"tab_w{a}", offset) for a, offset in enumerate((TABLE_0, TABLE_1))]
         w1_halves = w1_words.rearrange("a p (b c) -> b p a c", b=2)
         w1_raw = held([P, 2, H], U8, "w1_raw")
-        nc.sync.dma_start(w1_s_raw[:SCALE_ROWS, :].bitcast(I32), w1_scales.rearrange("a q c -> (a q) c").bitcast(I32))
         nc.sync.dma_start(tab_s[:SCALE_ROWS, :].bitcast(I32), tab_scales.rearrange("a q c -> (a q) c").bitcast(I32))
+        nc.sync.dma_start(idx[:], offs)
+        nc.sync.dma_start(w1_raw[:].bitcast(I32), w1_halves[0].bitcast(I32))
+        nc.sync.dma_start(w1_s_raw[:SCALE_ROWS, :].bitcast(I32), w1_scales.rearrange("a q c -> (a q) c").bitcast(I32))
         nc.sync.dma_start(p1[:], pos1)
         nc.sync.dma_start(p2[:], pos2)
         nc.sync.dma_start(p3[:], pos3)
-        nc.sync.dma_start(w1_raw[:].bitcast(I32), w1_halves[0].bitcast(I32))
         nc.sync.dma_start(tab_w[0][:], tab_words[0].rearrange("p t i -> p (t i)").bitcast(I32))
         nc.sync.dma_start(tab_w[1][:], tab_words[1].rearrange("p t i -> p (t i)").bitcast(I32))
 
@@ -91,11 +91,11 @@ def tile_list_sound_change_dating_kernel(
 
 
         v_s_raw = held([P, S], U8, "v_s_raw")
+        nc.vector.tensor_copy(v_s_raw[:], tab_s[:].indirect(idx[:]))
         nc.vector.tensor_copy(
             planes[0][:, w1_cols].rearrange("p (b t m) -> p b t m", b=2, t=PACK),
             w1_s_raw[:].rearrange("p (b m t) -> p b t m", b=2, t=PACK),
         )
-        nc.vector.tensor_copy(v_s_raw[:], tab_s[:].indirect(idx[:]))
         nc.vector.tensor_copy(planes[0][:, v_cols].bitcast(I32), v_s_raw[:].bitcast(I32))
         for a in range(2):
             for q in range(4):
@@ -202,7 +202,7 @@ def tile_list_sound_change_dating_kernel(
         def x2_tile():
             return ring.tile([P, S], F32, name="x2", bufs=4)
 
-        z = {(b, m0): held([P, PACK, m1 - m0], F32, f"z{b}{m0}") for b in range(2) for m0, m1 in CHUNKS[b]}
+        z = {(b, m0): held([P, PACK, m1 - m0], F32, f"z{b}{m0}") for b in range(2) for m0, m1 in CHUNKS[0]}
         z_w, z_s = {}, {}
 
         def weigh(anc, x2, m0, m1, weighed=None):
@@ -213,18 +213,22 @@ def tile_list_sound_change_dating_kernel(
             return weighed
 
         def add_loan(b, t, weighed, x2, m0, m1):
-            start = max(c0 for c0, c1 in CHUNKS[b] if c0 <= m0)
+            start = min(m0, HALF)
             picked = x2[:].indirect(p3[:, m0 // LIST : m1 // LIST])
             nc.vector.tensor_tensor(z[b, start][:, t, m0 - start : m1 - start], picked, weighed, ALU.add)
 
         def combine(b, t, anc, x2):
             low, high = weigh(anc, x2, 0, HALF), weigh(anc, x2, HALF, M)
             add_loan(b, t, low[:], x2, 0, HALF)
-            for m0, m1 in CHUNKS[b][1:] or [(HALF, M)]:
-                add_loan(b, t, high[:, m0 - HALF : m1 - HALF], x2, m0, m1)
+            add_loan(b, t, high[:], x2, HALF, M)
 
-        def quantize_z(b, m0, m1, copy, z_bf):
-            copy(z_bf.rearrange("p (c i) t -> p c t i", i=4), z[b, m0][:].rearrange("p t (c i) -> p c t i", i=4))
+        def quantize_z(b, m0, m1, copies, z_bf):
+            start = min(m0, HALF)
+            share = (m1 - m0) // len(copies)
+            for n, copy in enumerate(copies):
+                src = z[b, start][:, :, m0 - start + share * n : m0 - start + share * (n + 1)]
+                dst = z_bf[:, share * n : share * (n + 1), :]
+                copy(dst.rearrange("p (c i) t -> p c t i", i=4), src.rearrange("p t (c i) -> p c t i", i=4))
             z_w[b, m0] = held([P, m1 - m0], I32, f"z_w{b}{m0}")
             z_s[b, m0] = held([P, m1 - m0], U8, f"z_s{b}{m0}")
             nc.vector.quantize_mx(z_w[b, m0][:].bitcast(FP8X4), z_s[b, m0][:], z_bf.rearrange("p m t -> p (m t)"))
@@ -242,11 +246,14 @@ def tile_list_sound_change_dating_kernel(
                         start=b == 0, stop=b == 1,
                     )
             for c, acc in enumerate(accs):
-                if c == 1 and m0:
+                if c == 1 and m1 == M:
                     nc.vector.tensor_scalar(y[:, c, :], acc, prior[:, c : c + 1], None, ALU.add)
                 else:
                     nc.scalar.activation(y[:, c, :], acc, ACT.Identity, bias=prior[:, c : c + 1])
-            nc.sync.dma_start(out.rearrange("(c p) m -> p c m", p=P)[:, :, m0:m1], y[:])
+                if m0 == 0:
+                    nc.sync.dma_start(out[P * c : P * (c + 1), m0:m1], y[:, c, :])
+            if m0:
+                nc.sync.dma_start(out.rearrange("(c p) m -> p c m", p=P)[:, :, m0:m1], y[:])
 
         def round_z(b, m0, m1, copy):
             quantize_z(b, m0, m1, copy, held([P, m1 - m0, PACK], BF16, f"z_bf{b}{m0}")[:])
@@ -283,14 +290,15 @@ def tile_list_sound_change_dating_kernel(
             if k == 2:
                 prepare_w2(1, 1, (nc.scalar.copy, nc.scalar.copy))
             combine(*tiles[k], anc[k], x2)
+            if k == PACK - 1:
+                round_z(0, 0, HALF, [nc.vector.tensor_copy])
 
         b, t = tiles[-1]
         x2 = x2_tile()
         for h in range(2):
             reflexes(b, t, x2, h)
         anc = anc[-1]
-        for m0, m1 in CHUNKS[0]:
-            quantize_z(0, m0, m1, nc.scalar.copy, reused([P, HALF, PACK], BF16, f"z0_bf{m0}", X1 + 2 * PACK * m0)[:])
+        quantize_z(0, HALF, M, [nc.scalar.copy], reused([P, HALF, PACK], BF16, "z0_bf", X1)[:])
         first, second, third = CHUNKS[b]
         weighed = [weigh(anc, x2, *first), weigh(anc, x2, *second)]
         add_loan(b, t, weighed[0][:], x2, *first)
@@ -298,7 +306,8 @@ def tile_list_sound_change_dating_kernel(
         add_loan(b, t, weighed[1][:], x2, *second)
         add_loan(b, t, weighed[2][:], x2, *third)
 
-        for m0, m1 in CHUNKS[1]:
-            round_z(1, m0, m1, nc.scalar.copy if m0 == HALF else nc.vector.tensor_copy)
+        round_z(1, *first, [nc.vector.tensor_copy, nc.scalar.copy])
+        round_z(1, *second, [nc.scalar.copy])
+        round_z(1, *third, [nc.vector.tensor_copy])
         for m0, m1 in CHUNKS[1]:
             score(m0, m1)

@@ -130,13 +130,6 @@ def tile_list_sound_change_dating_kernel(
         nc.sync.dma_start(w1_late[:].bitcast(I32), w1_halves[1].bitcast(I32))
         load_w2(1, 0, reused([P, PACK, PASS], F32, "w2_raw10", TABLE_1))
 
-        w3_s = reused([P, 2, N], U8, "w3_s", TABLE_1 + PIECE)
-        nc.vector.memset(w3_s[:].bitcast(I32), 0)
-        for q in range(4):
-            nc.sync.dma_start(
-                w3_s[32 * q : 32 * q + 4].bitcast(I32),
-                w3_scales[:, 4 * q : 4 * q + 4, :].rearrange("a r c -> r a c").bitcast(I32),
-            )
         prior = reused([P, N // P], F32, "prior", TABLE_1 + PIECE + 2 * N)
         with nc.allow_non_contiguous_dma(reason="one value of period to a partition"):
             nc.sync.dma_start(prior[:], period.rearrange("(c p) -> p c", p=P))
@@ -241,7 +234,7 @@ def tile_list_sound_change_dating_kernel(
                 for c, acc in enumerate(accs):
                     cols = slice(P * c, P * (c + 1))
                     nc.tensor.matmul_mx(
-                        acc, lhsT=w3_w[:, b, cols].bitcast(FP8X4), lhsT_scale=w3_s[:, b, cols],
+                        acc, lhsT=w3_w[:, b, cols].bitcast(FP8X4), lhsT_scale=w1_late[:, b, cols],
                         rhs=z_w[b, start][:, part].bitcast(FP8X4), rhs_scale=z_s[b, start][:, part],
                         start=b == 0, stop=b == 1,
                     )
@@ -250,9 +243,9 @@ def tile_list_sound_change_dating_kernel(
                     nc.vector.tensor_scalar(y[:, c, :], acc, prior[:, c : c + 1], None, ALU.add)
                 else:
                     nc.scalar.activation(y[:, c, :], acc, ACT.Identity, bias=prior[:, c : c + 1])
-                if m0 == 0:
+                if m0 != HALF:
                     nc.sync.dma_start(out[P * c : P * (c + 1), m0:m1], y[:, c, :])
-            if m0:
+            if m0 == HALF:
                 nc.sync.dma_start(out.rearrange("(c p) m -> p c m", p=P)[:, :, m0:m1], y[:])
 
         def round_z(b, m0, m1, copy):
@@ -280,6 +273,11 @@ def tile_list_sound_change_dating_kernel(
         combine(0, 0, anc[0], x2[0])
         prepare_w2(1, 0)
         order_w1(1, w1_late)
+        for q in range(4):
+            nc.sync.dma_start(
+                w1_late[32 * q : 32 * q + 4, :, :N].bitcast(I32),
+                w3_scales[:, 4 * q : 4 * q + 4, :].rearrange("a r c -> r a c").bitcast(I32),
+            )
         combine(0, 1, anc[1], x2[1])
         for k in range(2, len(tiles) - 1):
             ahead = features(*tiles[k + 1])
@@ -288,7 +286,7 @@ def tile_list_sound_change_dating_kernel(
             reflexes(*tiles[k], x2, 1)
             anc.append(to_tanh(sigmoid(ahead)))
             if k == 2:
-                prepare_w2(1, 1, (nc.scalar.copy, nc.scalar.copy))
+                prepare_w2(1, 1, (nc.vector.tensor_copy, nc.scalar.copy))
             combine(*tiles[k], anc[k], x2)
             if k == PACK - 1:
                 round_z(0, 0, HALF, [nc.vector.tensor_copy])

@@ -210,21 +210,26 @@ def tile_list_sound_change_dating_kernel(
             picked = x2[:].indirect(p3[:, m0 // LIST : m1 // LIST])
             nc.vector.tensor_tensor(z[b, start][:, t, m0 - start : m1 - start], picked, weighed, ALU.add)
 
-        def combine(b, t, anc, x2):
-            low, high = weigh(anc, x2, 0, HALF), weigh(anc, x2, HALF, M)
+        def combine(b, t, anc, x2, low=None):
+            low, high = weigh(anc, x2, 0, HALF, low), weigh(anc, x2, HALF, M)
             add_loan(b, t, low[:], x2, 0, HALF)
             add_loan(b, t, high[:], x2, HALF, M)
 
-        def quantize_z(b, m0, m1, copies, z_bf):
+        def round_z(b, m0, m1, copies, z_bf=None):
+            if z_bf is None:
+                z_bf = held([P, m1 - m0, PACK], BF16, f"z_bf{b}{m0}")
             start = min(m0, HALF)
             share = (m1 - m0) // len(copies)
             for n, copy in enumerate(copies):
                 src = z[b, start][:, :, m0 - start + share * n : m0 - start + share * (n + 1)]
                 dst = z_bf[:, share * n : share * (n + 1), :]
                 copy(dst.rearrange("p (c i) t -> p c t i", i=4), src.rearrange("p t (c i) -> p c t i", i=4))
-            z_w[b, m0] = held([P, m1 - m0], I32, f"z_w{b}{m0}")
+            return z_bf
+
+        def quantize_z(b, m0, m1, z_bf, words=None):
+            z_w[b, m0] = words if words is not None else held([P, m1 - m0], I32, f"z_w{b}{m0}")
             z_s[b, m0] = held([P, m1 - m0], U8, f"z_s{b}{m0}")
-            nc.vector.quantize_mx(z_w[b, m0][:].bitcast(FP8X4), z_s[b, m0][:], z_bf.rearrange("p m t -> p (m t)"))
+            nc.vector.quantize_mx(z_w[b, m0][:].bitcast(FP8X4), z_s[b, m0][:], z_bf[:].rearrange("p m t -> p (m t)"))
 
         def score(m0, m1):
             y = held([P, N // P, m1 - m0], F32, f"y{m0}")
@@ -247,9 +252,6 @@ def tile_list_sound_change_dating_kernel(
                     nc.sync.dma_start(out[P * c : P * (c + 1), m0:m1], y[:, c, :])
             if m0 == HALF:
                 nc.sync.dma_start(out.rearrange("(c p) m -> p c m", p=P)[:, :, m0:m1], y[:])
-
-        def round_z(b, m0, m1, copy):
-            quantize_z(b, m0, m1, copy, held([P, m1 - m0, PACK], BF16, f"z_bf{b}{m0}")[:])
 
         prepare_w2(0, 0)
         load_w2(1, 1, reused([P, PACK, PASS], F32, "w2_raw11", TABLE_0 + PIECE))
@@ -283,20 +285,25 @@ def tile_list_sound_change_dating_kernel(
             ahead = features(*tiles[k + 1])
             x2 = x2_tile()
             reflexes(*tiles[k], x2, 0)
+            if k < len(tiles) - 2:
+                anc.append(to_tanh(sigmoid(ahead)))
             reflexes(*tiles[k], x2, 1)
-            anc.append(to_tanh(sigmoid(ahead)))
+            if k == len(tiles) - 2:
+                anc.append(to_tanh(sigmoid(ahead)))
             if k == 2:
                 prepare_w2(1, 1, (nc.vector.tensor_copy, nc.scalar.copy))
-            combine(*tiles[k], anc[k], x2)
+            combine(*tiles[k], anc[k], x2, held([P, HALF], F32, "z_w_low") if k == PACK else None)
             if k == PACK - 1:
-                round_z(0, 0, HALF, [nc.vector.tensor_copy])
+                z_low = round_z(0, 0, HALF, [nc.vector.tensor_copy])
+            if k == PACK:
+                quantize_z(0, 0, HALF, z_low, held([P, HALF], I32, "z_w_low"))
 
         b, t = tiles[-1]
         x2 = x2_tile()
         for h in range(2):
             reflexes(b, t, x2, h)
         anc = anc[-1]
-        quantize_z(0, HALF, M, [nc.scalar.copy], reused([P, HALF, PACK], BF16, "z0_bf", X1)[:])
+        quantize_z(0, HALF, M, round_z(0, HALF, M, [nc.scalar.copy], reused([P, HALF, PACK], BF16, "z0_bf", X1)))
         first, second, third = CHUNKS[b]
         weighed = [weigh(anc, x2, *first), weigh(anc, x2, *second)]
         add_loan(b, t, weighed[0][:], x2, *first)
@@ -304,8 +311,8 @@ def tile_list_sound_change_dating_kernel(
         add_loan(b, t, weighed[1][:], x2, *second)
         add_loan(b, t, weighed[2][:], x2, *third)
 
-        round_z(1, *first, [nc.vector.tensor_copy, nc.scalar.copy])
-        round_z(1, *second, [nc.scalar.copy])
-        round_z(1, *third, [nc.vector.tensor_copy])
+        quantize_z(1, *first, round_z(1, *first, [nc.vector.tensor_copy, nc.scalar.copy]))
+        quantize_z(1, *second, round_z(1, *second, [nc.scalar.copy]))
+        quantize_z(1, *third, round_z(1, *third, [nc.vector.tensor_copy]))
         for m0, m1 in CHUNKS[1]:
             score(m0, m1)

@@ -25,11 +25,12 @@ LIST = 16
 SCALE_ROWS = 32
 HALF = M // 2
 
-CHUNKS = ([(0, HALF), (HALF, M)], [(0, HALF), (HALF, HALF + P), (HALF + P, M)])
+CHUNKS = [(0, HALF), (HALF, HALF + P), (HALF + P, M)]
 
-TABLE_0, TABLE_1, W1, X1 = 0, 4 * T, 8 * T, 10 * T
-X_BYTES = 4 * S
-PIECE = 2 * T
+PIECE = 4 * PACK * PASS
+TABLE_0 = PIECE - 64
+W1_LATE = PIECE
+TABLE_1 = 3 * PIECE + 2 * H
 
 
 def tile_list_sound_change_dating_kernel(
@@ -80,15 +81,8 @@ def tile_list_sound_change_dating_kernel(
         nc.sync.dma_start(p2[:], pos2)
         nc.sync.dma_start(p3[:], pos3)
         nc.sync.dma_start(tab_w[0][:], tab_words[0].rearrange("p t i -> p (t i)").bitcast(I32))
-        nc.sync.dma_start(tab_w[1][:], tab_words[1].rearrange("p t i -> p (t i)").bitcast(I32))
-
-        w2_raw = {}
-
-        def load_w2(b, a, tile):
-            w2_raw[b, a] = tile
-            rows = w2[PASS * a : PASS * (a + 1), PASS * b : PASS * (b + 1)]
-            nc.sync.dma_start(tile[:], rows.rearrange("(p j) c -> p j c", j=PACK))
-
+        for cols in (slice(0, T // 2), slice(T // 2, T)):
+            nc.sync.dma_start(tab_w[1][:, cols], tab_words[1].rearrange("p t i -> p (t i)").bitcast(I32)[:, cols])
 
         v_s_raw = held([P, S], U8, "v_s_raw")
         nc.vector.tensor_copy(v_s_raw[:], tab_s[:].indirect(idx[:]))
@@ -106,15 +100,13 @@ def tile_list_sound_change_dating_kernel(
                         planes[a][32 * q : 32 * q + 4, :].bitcast(I32), planes[0][row : row + 4, :].bitcast(I32)
                     )
 
-        v_w = {}
+        v_w, w1_w = {}, {}
 
         def gather_table(a):
             for h in range(S // BANK):
                 v_w[a, h] = held([P, BANK], I32, f"v_w{a}{h}")
                 entries = idx[:, BANK // LIST * h : BANK // LIST * (h + 1)]
                 nc.vector.tensor_copy(v_w[a, h][:].bitcast(U32), tab_w[a][:].bitcast(U32).indirect(entries))
-
-        w1_w = {}
 
         def order_w1(b, raw):
             w1_w[b] = held([P, 2, PACK, 2 * P], U8, f"w1_w{b}")
@@ -124,116 +116,111 @@ def tile_list_sound_change_dating_kernel(
         gather_table(0)
         gather_table(1)
 
-        load_w2(0, 0, reused([P, PACK, PASS], F32, "w2_raw00", TABLE_0 + PIECE))
-        load_w2(0, 1, reused([P, PACK, PASS], F32, "w2_raw01", TABLE_0))
-        w1_late = reused([P, 2, H], U8, "w1_late", TABLE_1 + PIECE + H)
-        nc.sync.dma_start(w1_late[:].bitcast(I32), w1_halves[1].bitcast(I32))
-        load_w2(1, 0, reused([P, PACK, PASS], F32, "w2_raw10", TABLE_1))
+        w2_raw = {}
 
-        prior = reused([P, N // P], F32, "prior", TABLE_1 + PIECE + 2 * N)
+        def load_w2(b, a, offset):
+            w2_raw[b, a] = reused([P, PACK, PASS], F32, f"w2_raw{b}{a}", offset)
+            rows = w2[PASS * a : PASS * (a + 1), PASS * b : PASS * (b + 1)]
+            nc.sync.dma_start(w2_raw[b, a][:], rows.rearrange("(p j) c -> p j c", j=PACK))
+
+        load_w2(0, 0, 0)
+        w1_late = reused([P, 2, H], U8, "w1_late", W1_LATE)
+        nc.sync.dma_start(w1_late[:].bitcast(I32), w1_halves[1].bitcast(I32))
+        load_w2(0, 1, W1_LATE + 2 * H)
+        load_w2(1, 0, W1_LATE + 2 * H + PIECE)
+        load_w2(1, 1, TABLE_1)
+        w3_w = reused([P, 2, N], I32, "w3_w", TABLE_1 + PIECE)
+        nc.sync.dma_start(w3_w[:], w3_words.rearrange("a p c i -> p a (c i)").bitcast(I32))
+        prior = reused([P, N // P], F32, "prior", TABLE_1 + PIECE + 8 * N)
         with nc.allow_non_contiguous_dma(reason="one value of period to a partition"):
             nc.sync.dma_start(prior[:], period.rearrange("(c p) -> p c", p=P))
 
-        w2_w, w2_s = {}, {}
+        w2_bf, w2_w, w2_s = {}, {}, {}
 
-        def prepare_w2(b, a, copies=(nc.vector.tensor_copy, nc.vector.tensor_copy)):
+        def round_w2(b, a):
             src = w2_raw[b, a][:].rearrange("p j (m t) -> p m j t", t=PACK)
-            rounded = []
             for u in range(2):
-                if (b, a) == (0, 0):
-                    rounded.append(reused([P, 2, P, PACK], BF16, f"w2_bf00{u}", TABLE_1 + 3 * T + u * T // 2))
-                else:
-                    rounded.append(held([P, 2, P, PACK], BF16, f"w2_bf{b}{a}{u}"))
-                copies[u](rounded[u][:].rearrange("p t m j -> p m j t"), src[:, :, :, 2 * u : 2 * u + 2])
+                w2_bf[b, a, u] = held([P, 2, P, PACK], BF16, f"w2_bf{b}{a}{u}")
+                nc.vector.tensor_copy(w2_bf[b, a, u][:].rearrange("p t m j -> p m j t"), src[:, :, :, 2 * u : 2 * u + 2])
+
+        def quantize_w2(b, a):
             for u in range(2):
                 w2_w[b, a, u] = held([P, 2 * P], I32, f"w2_w{b}{a}{u}")
                 w2_s[b, a, u] = held([P, 2 * P], U8, f"w2_s{b}{a}{u}")
                 nc.vector.quantize_mx(
-                    w2_w[b, a, u][:].bitcast(FP8X4), w2_s[b, a, u][:], rounded[u][:].rearrange("p t m j -> p (t m j)")
+                    w2_w[b, a, u][:].bitcast(FP8X4), w2_s[b, a, u][:], w2_bf[b, a, u][:].rearrange("p t m j -> p (t m j)")
                 )
 
-        def first_stage(x, h, words, scales, pair, shift=0):
+        tiles = [(b, t) for b in range(2) for t in range(PACK)]
+
+        def first_stage(x, h, words, scales, pair, copy):
             cols = slice(BANK * h, BANK * (h + 1))
-            acc = bank(2 * pair + h + shift)
+            acc = bank(2 * pair + h)
             for a in range(2):
                 nc.tensor.matmul_mx(
                     acc[:], lhsT=words[a], lhsT_scale=scales[a],
                     rhs=v_w[a, h][:].bitcast(FP8X4), rhs_scale=planes[a][:, cols],
                     start=a == 0, stop=a == 1,
                 )
-            nc.scalar.copy(x[:, cols], acc[:])
+            copy(x[:, cols], acc[:])
 
-        def features(b, t, x1=None, halves=(0, 1), shift=0):
-            if x1 is not None:
-                pass
-            elif (b, t) == (1, PACK - 1):
-                x1 = reused([P, S], F32, "x1_last", X1)
-            else:
-                x1 = ring.tile([P, S], F32, name="x1", bufs=3)
+        x1, x2 = {}, {}
+
+        def features(k, h, copy):
+            b, t = tiles[k]
+            if k not in x1:
+                x1[k] = ring.tile([P, S], F32, name="x1", bufs=4)
             first = S + PASS * b + P * t
             words = [w1_w[b][:, a, t, :].bitcast(FP4X4) for a in range(2)]
-            for h in halves:
-                first_stage(x1, h, words, [planes[a][:, first : first + P] for a in range(2)], PACK * b + t, shift)
-            return x1
+            first_stage(x1[k], h, words, [planes[a][:, first : first + P] for a in range(2)], k, copy)
 
-        def sigmoid(x1):
-            sig = ring.tile([P, M], F32, name="sig", bufs=4)
-            nc.scalar.activation(sig[:], x1[:].indirect(p1[:]), ACT.Sigmoid, scale=2.0)
-            return sig
-
-        def to_tanh(sig, anc=None):
-            if anc is None:
-                anc = ring.tile([P, M], F32, name="anc", bufs=4)
-            nc.vector.tensor_scalar(anc[:], sig[:], 2.0, -1.0, ALU.mult, ALU.add)
-            return anc
-
-        def reflexes(b, t, x2, h):
+        def reflexes(k):
+            b, t = tiles[k]
+            x2[k] = ring.tile([P, S], F32, name="x2", bufs=5)
             u, cols = t // 2, slice(P * (t % 2), P * (t % 2 + 1))
             words = [w2_w[b, a, u][:, cols].bitcast(FP8X4) for a in range(2)]
-            first_stage(x2, h, words, [w2_s[b, a, u][:, cols] for a in range(2)], PACK * b + t + 3)
+            for h in range(2):
+                first_stage(x2[k], h, words, [w2_s[b, a, u][:, cols] for a in range(2)], k, nc.scalar.copy)
 
-        def x2_tile():
-            return ring.tile([P, S], F32, name="x2", bufs=4)
+        sig = [held([P, 2, M], F32, f"sig{n}") for n in range(4)]
+        anc = [held([P, 2, M], F32, f"anc{n}") for n in range(4)]
+        weighed = [held([P, PACK, M], F32, f"weighed{b}") for b in range(2)]
+        loan = [held([P, PACK, M], F32, f"loan{b}") for b in range(2)]
 
-        z = {(b, m0): held([P, PACK, m1 - m0], F32, f"z{b}{m0}") for b in range(2) for m0, m1 in CHUNKS[0]}
-        z_w, z_s = {}, {}
+        def sigmoid(k):
+            nc.scalar.activation(sig[k // 2][:, k % 2, :], x1[k][:].indirect(p1[:]), ACT.Sigmoid, scale=2.0)
 
-        def weigh(anc, x2, m0, m1, weighed=None):
-            if weighed is None:
-                weighed = ring.tile([P, m1 - m0], F32, name="weighed", bufs=4)
-            picked = x2[:].indirect(p2[:, m0 // LIST : m1 // LIST])
-            nc.vector.tensor_tensor(weighed[:], picked, anc[:, m0:m1], ALU.mult)
-            return weighed
+        def to_tanh(n):
+            nc.vector.tensor_scalar(anc[n][:], sig[n][:], 2.0, -1.0, ALU.mult, ALU.add)
 
-        def add_loan(b, t, weighed, x2, m0, m1):
-            start = min(m0, HALF)
-            picked = x2[:].indirect(p3[:, m0 // LIST : m1 // LIST])
-            nc.vector.tensor_tensor(z[b, start][:, t, m0 - start : m1 - start], picked, weighed, ALU.add)
+        def weigh(k):
+            b, t = tiles[k]
+            nc.vector.tensor_tensor(weighed[b][:, t, :], x2[k][:].indirect(p2[:]), anc[k // 2][:, k % 2, :], ALU.mult)
 
-        def combine(b, t, anc, x2, low=None):
-            low, high = weigh(anc, x2, 0, HALF, low), weigh(anc, x2, HALF, M)
-            add_loan(b, t, low[:], x2, 0, HALF)
-            add_loan(b, t, high[:], x2, HALF, M)
+        def borrow(k, m0, m1):
+            b, t = tiles[k]
+            picked = x2[k][:].indirect(p3[:, m0 // LIST : m1 // LIST])
+            nc.scalar.activation(loan[b][:, t, m0:m1], picked, ACT.Copy)
 
-        def round_z(b, m0, m1, copies, z_bf=None):
-            if z_bf is None:
-                z_bf = held([P, m1 - m0, PACK], BF16, f"z_bf{b}{m0}")
-            start = min(m0, HALF)
-            share = (m1 - m0) // len(copies)
-            for n, copy in enumerate(copies):
-                src = z[b, start][:, :, m0 - start + share * n : m0 - start + share * (n + 1)]
-                dst = z_bf[:, share * n : share * (n + 1), :]
-                copy(dst.rearrange("p (c i) t -> p c t i", i=4), src.rearrange("p t (c i) -> p c t i", i=4))
-            return z_bf
+        z_bf, z_w, z_s = {}, {}, {}
 
-        def quantize_z(b, m0, m1, z_bf, words=None):
-            z_w[b, m0] = words if words is not None else held([P, m1 - m0], I32, f"z_w{b}{m0}")
+        def sum_z(b, m0, m1):
+            z_bf[b, m0] = held([P, m1 - m0, PACK], BF16, f"z_bf{b}{m0}")
+            nc.vector.tensor_tensor(
+                z_bf[b, m0][:].rearrange("p (c i) t -> p c t i", i=2),
+                weighed[b][:, :, m0:m1].rearrange("p t (c i) -> p c t i", i=2),
+                loan[b][:, :, m0:m1].rearrange("p t (c i) -> p c t i", i=2),
+                ALU.add,
+            )
+
+        def quantize_z(b, m0, m1):
+            z_w[b, m0] = held([P, m1 - m0], I32, f"z_w{b}{m0}")
             z_s[b, m0] = held([P, m1 - m0], U8, f"z_s{b}{m0}")
-            nc.vector.quantize_mx(z_w[b, m0][:].bitcast(FP8X4), z_s[b, m0][:], z_bf[:].rearrange("p m t -> p (m t)"))
+            nc.vector.quantize_mx(z_w[b, m0][:].bitcast(FP8X4), z_s[b, m0][:], z_bf[b, m0][:].rearrange("p m t -> p (m t)"))
 
         def score(m0, m1):
             y = held([P, N // P, m1 - m0], F32, f"y{m0}")
-            accs = [bank(3 * CHUNKS[1].index((m0, m1)) + c + 6)[:, : m1 - m0] for c in range(N // P)]
+            accs = [bank(3 * CHUNKS.index((m0, m1)) + c)[:, : m1 - m0] for c in range(N // P)]
             for b, start in enumerate((min(m0, HALF), m0)):
                 part = slice(m0 - start, m1 - start)
                 for c, acc in enumerate(accs):
@@ -253,66 +240,72 @@ def tile_list_sound_change_dating_kernel(
             if m0 == HALF:
                 nc.sync.dma_start(out.rearrange("(c p) m -> p c m", p=P)[:, :, m0:m1], y[:])
 
-        prepare_w2(0, 0)
-        load_w2(1, 1, reused([P, PACK, PASS], F32, "w2_raw11", TABLE_0 + PIECE))
-        tiles = [(b, t) for b in range(2) for t in range(PACK)]
-        x1 = [features(0, t) for t in range(2)]
-        sig = [sigmoid(x1[0])]
-        x1.append(features(0, 2, halves=(0,)))
-        sig.append(sigmoid(x1[1]))
-        prepare_w2(0, 1)
-        w3_w = reused([P, 2, N], I32, "w3_w", TABLE_0 + T)
-        nc.sync.dma_start(w3_w[:], w3_words.rearrange("a p c i -> p a (c i)").bitcast(I32))
-        anc = [to_tanh(sig[t], reused([P, M], F32, f"anc{t}", TABLE_0 + 4 * M * t)) for t in range(2)]
-        x2 = [x2_tile()]
-        for h in range(2):
-            reflexes(0, 0, x2[0], h)
-        features(0, 2, x1[2], halves=(1,), shift=1)
-        x2.append(x2_tile())
-        for h in range(2):
-            reflexes(0, 1, x2[1], h)
-        anc.append(to_tanh(sigmoid(x1[2])))
-        combine(0, 0, anc[0], x2[0])
-        prepare_w2(1, 0)
+        by_scalar, by_vector = nc.scalar.copy, nc.vector.tensor_copy
+
+        for k in range(3):
+            features(k, 0, by_scalar)
+        features(0, 1, by_vector)
+        features(1, 1, by_vector)
+        sigmoid(0)
+        round_w2(0, 0)
+        features(2, 1, by_vector)
+        sigmoid(1)
+        quantize_w2(0, 0)
         order_w1(1, w1_late)
         for q in range(4):
             nc.sync.dma_start(
                 w1_late[32 * q : 32 * q + 4, :, :N].bitcast(I32),
                 w3_scales[:, 4 * q : 4 * q + 4, :].rearrange("a r c -> r a c").bitcast(I32),
             )
-        combine(0, 1, anc[1], x2[1])
-        for k in range(2, len(tiles) - 1):
-            ahead = features(*tiles[k + 1])
-            x2 = x2_tile()
-            reflexes(*tiles[k], x2, 0)
-            if k < len(tiles) - 2:
-                anc.append(to_tanh(sigmoid(ahead)))
-            reflexes(*tiles[k], x2, 1)
-            if k == len(tiles) - 2:
-                anc.append(to_tanh(sigmoid(ahead)))
-            if k == 2:
-                prepare_w2(1, 1, (nc.vector.tensor_copy, nc.scalar.copy))
-            combine(*tiles[k], anc[k], x2, held([P, HALF], F32, "z_w_low") if k == PACK else None)
-            if k == PACK - 1:
-                z_low = round_z(0, 0, HALF, [nc.vector.tensor_copy])
-            if k == PACK:
-                quantize_z(0, 0, HALF, z_low, held([P, HALF], I32, "z_w_low"))
+        features(3, 0, by_scalar)
+        features(3, 1, by_vector)
+        sigmoid(2)
+        round_w2(0, 1)
+        features(4, 0, by_vector)
+        features(4, 1, by_vector)
+        sigmoid(3)
+        quantize_w2(0, 1)
+        features(5, 0, by_scalar)
+        features(5, 1, by_vector)
+        sigmoid(4)
+        round_w2(1, 0)
+        features(6, 0, by_vector)
+        features(6, 1, by_vector)
+        sigmoid(5)
+        quantize_w2(1, 0)
+        features(7, 0, by_vector)
+        features(7, 1, by_vector)
+        sigmoid(6)
+        round_w2(1, 1)
+        sigmoid(7)
+        to_tanh(0)
+        quantize_w2(1, 1)
 
-        b, t = tiles[-1]
-        x2 = x2_tile()
-        for h in range(2):
-            reflexes(b, t, x2, h)
-        anc = anc[-1]
-        quantize_z(0, HALF, M, round_z(0, HALF, M, [nc.scalar.copy], reused([P, HALF, PACK], BF16, "z0_bf", X1)))
-        first, second, third = CHUNKS[b]
-        weighed = [weigh(anc, x2, *first), weigh(anc, x2, *second)]
-        add_loan(b, t, weighed[0][:], x2, *first)
-        weighed.append(weigh(anc, x2, *third, reused([P, P], F32, "last_weighed", X1)))
-        add_loan(b, t, weighed[1][:], x2, *second)
-        add_loan(b, t, weighed[2][:], x2, *third)
-
-        quantize_z(1, *first, round_z(1, *first, [nc.vector.tensor_copy, nc.scalar.copy]))
-        quantize_z(1, *second, round_z(1, *second, [nc.scalar.copy]))
-        quantize_z(1, *third, round_z(1, *third, [nc.vector.tensor_copy]))
-        for m0, m1 in CHUNKS[1]:
+        reflexes(0)
+        to_tanh(1)
+        for k in range(1, PACK + 1):
+            reflexes(k)
+            weigh(k - 1)
+            borrow(k - 1, 0, M)
+            if k % 2 == 1:
+                to_tanh(2 + k // 2)
+        for k in range(PACK + 1, 2 * PACK):
+            reflexes(k)
+            if k > PACK + 1:
+                quantize_z(0, HALF * (k - PACK - 2), HALF * (k - PACK - 1))
+            weigh(k - 1)
+            if k < 2 * PACK - 1:
+                sum_z(0, HALF * (k - PACK - 1), HALF * (k - PACK))
+        weigh(2 * PACK - 1)
+        for m0, m1 in CHUNKS:
+            for k in range(PACK, 2 * PACK):
+                borrow(k, m0, m1)
+        first, second, third = CHUNKS
+        sum_z(1, *first)
+        sum_z(1, *second)
+        quantize_z(1, *first)
+        quantize_z(1, *second)
+        sum_z(1, *third)
+        quantize_z(1, *third)
+        for m0, m1 in CHUNKS:
             score(m0, m1)

@@ -138,18 +138,18 @@ def tile_list_sound_change_dating_kernel(
         w2_bf, w2_w, w2_s = {}, {}, {}
 
         def round_w2(b, a):
-            src = w2_raw[b, a][:].rearrange("p j (m t) -> p m j t", t=PACK)
-            for u in range(2):
-                w2_bf[b, a, u] = held([P, 2, P, PACK], BF16, f"w2_bf{b}{a}{u}")
-                nc.vector.tensor_copy(w2_bf[b, a, u][:].rearrange("p t m j -> p m j t"), src[:, :, :, 2 * u : 2 * u + 2])
+            w2_bf[b, a] = held([P, PACK, P, PACK], BF16, f"w2_bf{b}{a}")
+            nc.vector.tensor_copy(
+                w2_bf[b, a][:].rearrange("p (u t) m j -> p u m j t", u=2),
+                w2_raw[b, a][:].rearrange("p j (m u t) -> p u m j t", u=2, t=2),
+            )
 
         def quantize_w2(b, a):
-            for u in range(2):
-                w2_w[b, a, u] = held([P, 2 * P], I32, f"w2_w{b}{a}{u}")
-                w2_s[b, a, u] = held([P, 2 * P], U8, f"w2_s{b}{a}{u}")
-                nc.vector.quantize_mx(
-                    w2_w[b, a, u][:].bitcast(FP8X4), w2_s[b, a, u][:], w2_bf[b, a, u][:].rearrange("p t m j -> p (t m j)")
-                )
+            w2_w[b, a] = held([P, PASS], I32, f"w2_w{b}{a}")
+            w2_s[b, a] = held([P, PASS], U8, f"w2_s{b}{a}")
+            nc.vector.quantize_mx(
+                w2_w[b, a][:].bitcast(FP8X4), w2_s[b, a][:], w2_bf[b, a][:].rearrange("p t m j -> p (t m j)")
+            )
 
         tiles = [(b, t) for b in range(2) for t in range(PACK)]
 
@@ -177,25 +177,25 @@ def tile_list_sound_change_dating_kernel(
         def reflexes(k):
             b, t = tiles[k]
             x2[k] = ring.tile([P, S], F32, name="x2", bufs=5)
-            u, cols = t // 2, slice(P * (t % 2), P * (t % 2 + 1))
-            words = [w2_w[b, a, u][:, cols].bitcast(FP8X4) for a in range(2)]
+            cols = slice(P * t, P * (t + 1))
+            words = [w2_w[b, a][:, cols].bitcast(FP8X4) for a in range(2)]
             for h in range(2):
-                first_stage(x2[k], h, words, [w2_s[b, a, u][:, cols] for a in range(2)], k, nc.scalar.copy)
+                first_stage(x2[k], h, words, [w2_s[b, a][:, cols] for a in range(2)], k, nc.scalar.copy)
 
-        sig = [held([P, 2, M], F32, f"sig{n}") for n in range(4)]
-        anc = [held([P, 2, M], F32, f"anc{n}") for n in range(4)]
+        sig = [held([P, PACK, M], F32, f"sig{b}") for b in range(2)]
+        anc = [held([P, PACK, M], F32, f"anc{b}") for b in range(2)]
         weighed = [held([P, PACK, M], F32, f"weighed{b}") for b in range(2)]
         loan = [held([P, PACK, M], F32, f"loan{b}") for b in range(2)]
 
         def sigmoid(k):
-            nc.scalar.activation(sig[k // 2][:, k % 2, :], x1[k][:].indirect(p1[:]), ACT.Sigmoid, scale=2.0)
+            nc.scalar.activation(sig[k // PACK][:, k % PACK, :], x1[k][:].indirect(p1[:]), ACT.Sigmoid, scale=2.0)
 
-        def to_tanh(n):
-            nc.vector.tensor_scalar(anc[n][:], sig[n][:], 2.0, -1.0, ALU.mult, ALU.add)
+        def to_tanh(b):
+            nc.vector.tensor_scalar(anc[b][:], sig[b][:], 2.0, -1.0, ALU.mult, ALU.add)
 
         def weigh(k):
             b, t = tiles[k]
-            nc.vector.tensor_tensor(weighed[b][:, t, :], x2[k][:].indirect(p2[:]), anc[k // 2][:, k % 2, :], ALU.mult)
+            nc.vector.tensor_tensor(weighed[b][:, t, :], x2[k][:].indirect(p2[:]), anc[b][:, t, :], ALU.mult)
 
         def borrow(k, m0, m1):
             b, t = tiles[k]
@@ -221,7 +221,7 @@ def tile_list_sound_change_dating_kernel(
         def score(m0, m1):
             y = held([P, N // P, m1 - m0], F32, f"y{m0}")
             accs = [bank(3 * CHUNKS.index((m0, m1)) + c)[:, : m1 - m0] for c in range(N // P)]
-            for b, start in enumerate((min(m0, HALF), m0)):
+            for b, start in enumerate((0, m0)):
                 part = slice(m0 - start, m1 - start)
                 for c, acc in enumerate(accs):
                     cols = slice(P * c, P * (c + 1))
@@ -242,70 +242,69 @@ def tile_list_sound_change_dating_kernel(
 
         by_scalar, by_vector = nc.scalar.copy, nc.vector.tensor_copy
 
-        for k in range(3):
-            features(k, 0, by_scalar)
-        features(0, 1, by_vector)
-        features(1, 1, by_vector)
+        features(0, 0, by_scalar)
+        features(1, 0, by_scalar)
+        features(0, 1, by_scalar)
         sigmoid(0)
         round_w2(0, 0)
+        features(1, 1, by_vector)
+        features(2, 0, by_vector)
         features(2, 1, by_vector)
         sigmoid(1)
-        quantize_w2(0, 0)
         order_w1(1, w1_late)
         for q in range(4):
             nc.sync.dma_start(
                 w1_late[32 * q : 32 * q + 4, :, :N].bitcast(I32),
                 w3_scales[:, 4 * q : 4 * q + 4, :].rearrange("a r c -> r a c").bitcast(I32),
             )
-        features(3, 0, by_scalar)
+        features(3, 0, by_vector)
         features(3, 1, by_vector)
         sigmoid(2)
-        round_w2(0, 1)
-        features(4, 0, by_vector)
-        features(4, 1, by_vector)
+        quantize_w2(0, 0)
+        features(4, 0, by_scalar)
         sigmoid(3)
-        quantize_w2(0, 1)
+        round_w2(0, 1)
+        features(4, 1, by_vector)
         features(5, 0, by_scalar)
-        features(5, 1, by_vector)
         sigmoid(4)
-        round_w2(1, 0)
+        quantize_w2(0, 1)
+        features(5, 1, by_vector)
         features(6, 0, by_vector)
         features(6, 1, by_vector)
         sigmoid(5)
-        quantize_w2(1, 0)
+        round_w2(1, 0)
         features(7, 0, by_vector)
         features(7, 1, by_vector)
         sigmoid(6)
-        round_w2(1, 1)
-        sigmoid(7)
+        quantize_w2(1, 0)
         to_tanh(0)
-        quantize_w2(1, 1)
+        sigmoid(7)
+        round_w2(1, 1)
 
         reflexes(0)
-        to_tanh(1)
         for k in range(1, PACK + 1):
             reflexes(k)
             weigh(k - 1)
             borrow(k - 1, 0, M)
-            if k % 2 == 1:
-                to_tanh(2 + k // 2)
-        for k in range(PACK + 1, 2 * PACK):
-            reflexes(k)
-            if k > PACK + 1:
-                quantize_z(0, HALF * (k - PACK - 2), HALF * (k - PACK - 1))
-            weigh(k - 1)
-            if k < 2 * PACK - 1:
-                sum_z(0, HALF * (k - PACK - 1), HALF * (k - PACK))
-        weigh(2 * PACK - 1)
+            if k == 1:
+                quantize_w2(1, 1)
+            if k == 2:
+                to_tanh(1)
+        reflexes(5)
+        weigh(4)
+        sum_z(0, 0, M)
+        reflexes(6)
+        weigh(5)
+        quantize_z(0, 0, M)
+        reflexes(7)
+        weigh(6)
+        weigh(7)
         for m0, m1 in CHUNKS:
             for k in range(PACK, 2 * PACK):
                 borrow(k, m0, m1)
         first, second, third = CHUNKS
-        sum_z(1, *first)
-        sum_z(1, *second)
-        quantize_z(1, *first)
-        quantize_z(1, *second)
-        sum_z(1, *third)
-        quantize_z(1, *third)
+        for m0, m1 in CHUNKS:
+            sum_z(1, m0, m1)
+            quantize_z(1, m0, m1)
         for m0, m1 in CHUNKS:
             score(m0, m1)

@@ -30,7 +30,7 @@ CHUNKS = [(0, HALF), (HALF, HALF + P), (HALF + P, M)]
 PIECE = 4 * PACK * PASS
 TABLE_0 = PIECE - 64
 W1_LATE = PIECE
-TABLE_1 = 3 * PIECE + 2 * H
+TABLE_1 = 4 * PIECE
 
 
 def tile_list_sound_change_dating_kernel(
@@ -72,10 +72,10 @@ def tile_list_sound_change_dating_kernel(
 
         tab_w = [reused([P, T], I32, f"tab_w{a}", offset) for a, offset in enumerate((TABLE_0, TABLE_1))]
         w1_halves = w1_words.rearrange("a p (b c) -> b p a c", b=2)
-        w1_raw = held([P, 2, H], U8, "w1_raw")
+        w1_raw = [held([P, H], U8, "w1_raw0"), reused([P, H], U8, "w1_raw1", TABLE_0 + 4 * T - H)]
         nc.sync.dma_start(tab_s[:SCALE_ROWS, :].bitcast(I32), tab_scales.rearrange("a q c -> (a q) c").bitcast(I32))
         nc.sync.dma_start(idx[:], offs)
-        nc.sync.dma_start(w1_raw[:].bitcast(I32), w1_halves[0].bitcast(I32))
+        nc.sync.dma_start(w1_raw[0][:].bitcast(I32), w1_halves[0][:, 0, :].bitcast(I32))
         nc.sync.dma_start(w1_s_raw[:SCALE_ROWS, :].bitcast(I32), w1_scales.rearrange("a q c -> (a q) c").bitcast(I32))
         nc.sync.dma_start(p1[:], pos1)
         nc.sync.dma_start(p2[:], pos2)
@@ -112,9 +112,15 @@ def tile_list_sound_change_dating_kernel(
             w1_w[b] = held([P, 2, PACK, 2 * P], U8, f"w1_w{b}")
             nc.vector.tensor_copy(w1_w[b][:].bitcast(U16), raw[:].bitcast(U16).rearrange("p a (m t) -> p a t m", t=PACK))
 
-        order_w1(0, w1_raw)
+        def order_first(a, copy):
+            copy(w1_w[0][:, a].bitcast(U16), w1_raw[a][:].bitcast(U16).rearrange("p (m t) -> p t m", t=PACK))
+
+        w1_w[0] = held([P, 2, PACK, 2 * P], U8, "w1_w0")
+        order_first(0, nc.vector.tensor_copy)
         gather_table(0)
         gather_table(1)
+        nc.sync.dma_start(w1_raw[1][:].bitcast(I32), w1_halves[0][:, 1, :].bitcast(I32))
+        order_first(1, nc.scalar.copy)
 
         w2_raw = {}
 
@@ -127,11 +133,11 @@ def tile_list_sound_change_dating_kernel(
         w1_late = reused([P, 2, H], U8, "w1_late", W1_LATE)
         nc.sync.dma_start(w1_late[:].bitcast(I32), w1_halves[1].bitcast(I32))
         load_w2(0, 1, W1_LATE + 2 * H)
-        load_w2(1, 0, W1_LATE + 2 * H + PIECE)
+        load_w2(1, 0, TABLE_1 + PIECE)
         load_w2(1, 1, TABLE_1)
-        w3_w = reused([P, 2, N], I32, "w3_w", TABLE_1 + PIECE)
+        w3_w = reused([P, 2, N], I32, "w3_w", 0)
         nc.sync.dma_start(w3_w[:], w3_words.rearrange("a p c i -> p a (c i)").bitcast(I32))
-        prior = reused([P, N // P], F32, "prior", TABLE_1 + PIECE + 8 * N)
+        prior = reused([P, N // P], F32, "prior", 8 * N)
         with nc.allow_non_contiguous_dma(reason="one value of period to a partition"):
             nc.sync.dma_start(prior[:], period.rearrange("(c p) -> p c", p=P))
 

@@ -199,9 +199,10 @@ def tile_list_sound_change_dating_kernel(
         def to_tanh(b):
             nc.vector.tensor_scalar(anc[b][:], sig[b][:], 2.0, -1.0, ALU.mult, ALU.add)
 
-        def weigh(k):
+        def weigh(k, m0=0, m1=M):
             b, t = tiles[k]
-            nc.vector.tensor_tensor(weighed[b][:, t, :], x2[k][:].indirect(p2[:]), anc[b][:, t, :], ALU.mult)
+            picked = x2[k][:].indirect(p2[:, m0 // LIST : m1 // LIST])
+            nc.vector.tensor_tensor(weighed[b][:, t, m0:m1], picked, anc[b][:, t, m0:m1], ALU.mult)
 
         def borrow(k, m0, m1):
             b, t = tiles[k]
@@ -251,10 +252,10 @@ def tile_list_sound_change_dating_kernel(
         features(0, 0, by_scalar)
         features(1, 0, by_scalar)
         features(0, 1, by_scalar)
+        features(2, 0, by_scalar)
         sigmoid(0)
         round_w2(0, 0)
         features(1, 1, by_vector)
-        features(2, 0, by_vector)
         features(2, 1, by_vector)
         sigmoid(1)
         order_w1(1, w1_late)
@@ -304,13 +305,17 @@ def tile_list_sound_change_dating_kernel(
         quantize_z(0, 0, M)
         reflexes(7)
         weigh(6)
-        weigh(7)
+        weigh(7, 0, HALF)
+        weigh(7, HALF, M)
         for m0, m1 in CHUNKS:
             for k in range(PACK, 2 * PACK):
                 borrow(k, m0, m1)
         first, second, third = CHUNKS
-        for m0, m1 in CHUNKS:
-            sum_z(1, m0, m1)
-            quantize_z(1, m0, m1)
+        sum_z(1, *first)
+        sum_z(1, *second)
+        quantize_z(1, *first)
+        sum_z(1, *third)
+        quantize_z(1, *second)
+        quantize_z(1, *third)
         for m0, m1 in CHUNKS:
             score(m0, m1)

@@ -135,11 +135,6 @@ def tile_list_sound_change_dating_kernel(
         load_w2(0, 1, W1_LATE + 2 * H)
         load_w2(1, 0, TABLE_1 + PIECE)
         load_w2(1, 1, TABLE_1)
-        w3_w = reused([P, 2, N], I32, "w3_w", 0)
-        nc.sync.dma_start(w3_w[:], w3_words.rearrange("a p c i -> p a (c i)").bitcast(I32))
-        prior = reused([P, N // P], F32, "prior", 8 * N)
-        with nc.allow_non_contiguous_dma(reason="one value of period to a partition"):
-            nc.sync.dma_start(prior[:], period.rearrange("(c p) -> p c", p=P))
 
         w2_bf, w2_w, w2_s = {}, {}, {}
 
@@ -174,7 +169,9 @@ def tile_list_sound_change_dating_kernel(
 
         def features(k, h, copy):
             b, t = tiles[k]
-            if k not in x1:
+            if k not in x1 and k in (2, 3):
+                x1[k] = reused([P, S], F32, f"x1_{k}", 4 * S * (k - 2))
+            elif k not in x1:
                 x1[k] = ring.tile([P, S], F32, name="x1", bufs=4)
             first = S + PASS * b + P * t
             words = [w1_w[b][:, a, t, :].bitcast(FP4X4) for a in range(2)]
@@ -252,13 +249,13 @@ def tile_list_sound_change_dating_kernel(
         features(0, 0, by_scalar)
         features(1, 0, by_scalar)
         features(0, 1, by_scalar)
-        features(2, 0, by_scalar)
+        features(1, 1, by_scalar)
         sigmoid(0)
-        round_w2(0, 0)
-        features(1, 1, by_vector)
-        features(2, 1, by_vector)
         sigmoid(1)
+        round_w2(0, 0)
         order_w1(1, w1_late)
+        features(2, 0, by_vector)
+        features(2, 1, by_vector)
         for q in range(4):
             nc.sync.dma_start(
                 w1_late[32 * q : 32 * q + 4, :, :N].bitcast(I32),
@@ -271,6 +268,12 @@ def tile_list_sound_change_dating_kernel(
         features(4, 0, by_scalar)
         sigmoid(3)
         round_w2(0, 1)
+        w3_w = reused([P, 2, N], I32, "w3_w", W1_LATE + 2 * H)
+        nc.sync.dma_start(w3_w[:], w3_words.rearrange("a p c i -> p a (c i)").bitcast(I32))
+        prior = reused([P, N // P], F32, "prior", W1_LATE + 2 * H + 8 * N)
+        with nc.allow_non_contiguous_dma(reason="one value of period to a partition"):
+            nc.sync.dma_start(prior[:], period.rearrange("(c p) -> p c", p=P))
+
         features(4, 1, by_vector)
         features(5, 0, by_scalar)
         sigmoid(4)

@@ -138,8 +138,14 @@ def tile_list_sound_change_dating_kernel(
 
         w2_bf, w2_w, w2_s = {}, {}, {}
 
-        def round_w2(b, a):
-            w2_bf[b, a] = held([P, PACK, P, PACK], BF16, f"w2_bf{b}{a}")
+        def round_by_gpsimd(b, a, rounded):
+            w2_bf[b, a] = rounded
+            nc.gpsimd.tensor_scalar(
+                rounded[:], w2_raw[b, a][:].rearrange("p j (m t) -> p t m j", t=PACK), 1.0, 0.0, ALU.mult, ALU.add
+            )
+
+        def round_w2(b, a, rounded):
+            w2_bf[b, a] = rounded
             nc.vector.tensor_copy(
                 w2_bf[b, a][:].rearrange("p (u t) m j -> p u m j t", u=2),
                 w2_raw[b, a][:].rearrange("p j (m u t) -> p u m j t", u=2, t=2),
@@ -186,7 +192,7 @@ def tile_list_sound_change_dating_kernel(
                 first_stage(x2[k], h, words, [w2_s[b, a][:, cols] for a in range(2)], k, nc.scalar.copy)
 
         sig = [held([P, PACK, M], F32, f"sig{b}") for b in range(2)]
-        anc = [held([P, PACK, M], F32, f"anc{b}") for b in range(2)]
+        anc = [reused([P, PACK, M], F32, "anc0", TABLE_1 + PIECE + PIECE // 2), held([P, PACK, M], F32, "anc1")]
         weighed = [held([P, PACK, M], F32, f"weighed{b}") for b in range(2)]
         loan = [held([P, PACK, M], F32, f"loan{b}") for b in range(2)]
 
@@ -246,50 +252,44 @@ def tile_list_sound_change_dating_kernel(
 
         by_scalar, by_vector = nc.scalar.copy, nc.vector.tensor_copy
 
+        rounded_shape = [P, PACK, P, PACK]
+
         features(0, 0, by_scalar)
         features(1, 0, by_scalar)
         features(0, 1, by_scalar)
         features(1, 1, by_scalar)
         sigmoid(0)
         sigmoid(1)
-        round_w2(0, 0)
+        round_w2(0, 0, held(rounded_shape, BF16, "w2_bf00"))
         order_w1(1, w1_late)
-        features(2, 0, by_vector)
         features(2, 1, by_vector)
+        features(2, 0, by_scalar)
         for q in range(4):
             nc.sync.dma_start(
                 w1_late[32 * q : 32 * q + 4, :, :N].bitcast(I32),
                 w3_scales[:, 4 * q : 4 * q + 4, :].rearrange("a r c -> r a c").bitcast(I32),
             )
-        features(3, 0, by_vector)
-        features(3, 1, by_vector)
-        sigmoid(2)
         quantize_w2(0, 0)
-        features(4, 0, by_scalar)
-        sigmoid(3)
-        round_w2(0, 1)
+        sigmoid(2)
+        round_w2(0, 1, held(rounded_shape, BF16, "w2_bf"))
         w3_w = reused([P, 2, N], I32, "w3_w", W1_LATE + 2 * H)
         nc.sync.dma_start(w3_w[:], w3_words.rearrange("a p c i -> p a (c i)").bitcast(I32))
         prior = reused([P, N // P], F32, "prior", W1_LATE + 2 * H + 8 * N)
         with nc.allow_non_contiguous_dma(reason="one value of period to a partition"):
             nc.sync.dma_start(prior[:], period.rearrange("(c p) -> p c", p=P))
-
-        features(4, 1, by_vector)
-        features(5, 0, by_scalar)
-        sigmoid(4)
+        features(3, 0, by_vector)
         quantize_w2(0, 1)
-        features(5, 1, by_vector)
-        features(6, 0, by_vector)
-        features(6, 1, by_vector)
-        sigmoid(5)
-        round_w2(1, 0)
-        features(7, 0, by_vector)
-        features(7, 1, by_vector)
-        sigmoid(6)
-        quantize_w2(1, 0)
-        to_tanh(0)
+        round_by_gpsimd(1, 0, held(rounded_shape, BF16, "w2_bf"))
+        features(3, 1, by_vector)
+        for k in range(PACK, 2 * PACK):
+            sigmoid(k - 1)
+            features(k, 0, by_vector)
+            features(k, 1, by_vector)
         sigmoid(7)
-        round_w2(1, 1)
+        quantize_w2(1, 0)
+        round_w2(1, 1, reused(rounded_shape, BF16, "w2_bf11", TABLE_1 + PIECE))
+        to_tanh(0)
+        quantize_w2(1, 1)
 
         reflexes(0)
         for k in range(1, PACK + 1):
@@ -297,8 +297,6 @@ def tile_list_sound_change_dating_kernel(
             weigh(k - 1)
             borrow(k - 1, 0, M)
             if k == 1:
-                quantize_w2(1, 1)
-            if k == 2:
                 to_tanh(1)
         reflexes(5)
         weigh(4)

@@ -31,6 +31,8 @@ PIECE = 4 * PACK * PASS
 TABLE_0 = PIECE - 64
 W1_LATE = PIECE
 TABLE_1 = 4 * PIECE
+ANCESTORS = 6 * PIECE
+FIFTH = 7 * PIECE
 
 
 def tile_list_sound_change_dating_kernel(
@@ -138,12 +140,6 @@ def tile_list_sound_change_dating_kernel(
 
         w2_bf, w2_w, w2_s = {}, {}, {}
 
-        def round_by_gpsimd(b, a, rounded):
-            w2_bf[b, a] = rounded
-            nc.gpsimd.tensor_scalar(
-                rounded[:], w2_raw[b, a][:].rearrange("p j (m t) -> p t m j", t=PACK), 1.0, 0.0, ALU.mult, ALU.add
-            )
-
         def round_w2(b, a, rounded):
             w2_bf[b, a] = rounded
             nc.vector.tensor_copy(
@@ -191,21 +187,32 @@ def tile_list_sound_change_dating_kernel(
             for h in range(2):
                 first_stage(x2[k], h, words, [w2_s[b, a][:, cols] for a in range(2)], k, nc.scalar.copy)
 
-        sig = [held([P, PACK, M], F32, f"sig{b}") for b in range(2)]
-        anc = [reused([P, PACK, M], F32, "anc0", TABLE_1 + PIECE + PIECE // 2), held([P, PACK, M], F32, "anc1")]
+        groups = [(0, 1), (2, 3), (4,), (5, 6, 7)]
+        sig, anc = {}, {}
         weighed = [held([P, PACK, M], F32, f"weighed{b}") for b in range(2)]
         loan = [held([P, PACK, M], F32, f"loan{b}") for b in range(2)]
 
         def sigmoid(k):
-            nc.scalar.activation(sig[k // PACK][:, k % PACK, :], x1[k][:].indirect(p1[:]), ACT.Sigmoid, scale=2.0)
+            group = [g for g in groups if k in g][0]
+            if group == (4,):
+                sig[group] = reused([P, 1, M], F32, "sig4", FIFTH + PIECE // 2 - 2 * M)
+            elif group not in sig:
+                sig[group] = held([P, len(group), M], F32, f"sig{k}")
+            nc.scalar.activation(sig[group][:, k - group[0], :], x1[k][:].indirect(p1[:]), ACT.Sigmoid, scale=2.0)
 
-        def to_tanh(b):
-            nc.vector.tensor_scalar(anc[b][:], sig[b][:], 2.0, -1.0, ALU.mult, ALU.add)
+        def to_tanh(group, engine):
+            if group[0] < PACK:
+                tanh = reused([P, len(group), M], F32, f"anc{group[0]}", ANCESTORS + 4 * M * group[0])
+            else:
+                tanh = held([P, len(group), M], F32, f"anc{group[0]}")
+            engine.tensor_scalar(tanh[:], sig[group][:], 2.0, -1.0, ALU.mult, ALU.add)
+            for i, k in enumerate(group):
+                anc[k] = tanh[:, i, :]
 
         def weigh(k, m0=0, m1=M):
             b, t = tiles[k]
             picked = x2[k][:].indirect(p2[:, m0 // LIST : m1 // LIST])
-            nc.vector.tensor_tensor(weighed[b][:, t, m0:m1], picked, anc[b][:, t, m0:m1], ALU.mult)
+            nc.vector.tensor_tensor(weighed[b][:, t, m0:m1], picked, anc[k][:, m0:m1], ALU.mult)
 
         def borrow(k, m0, m1):
             b, t = tiles[k]
@@ -271,7 +278,7 @@ def tile_list_sound_change_dating_kernel(
             )
         quantize_w2(0, 0)
         sigmoid(2)
-        round_w2(0, 1, held(rounded_shape, BF16, "w2_bf"))
+        round_w2(0, 1, reused(rounded_shape, BF16, "w2_bf01", ANCESTORS + 4 * M))
         w3_w = reused([P, 2, N], I32, "w3_w", W1_LATE + 2 * H)
         nc.sync.dma_start(w3_w[:], w3_words.rearrange("a p c i -> p a (c i)").bitcast(I32))
         prior = reused([P, N // P], F32, "prior", W1_LATE + 2 * H + 8 * N)
@@ -279,17 +286,18 @@ def tile_list_sound_change_dating_kernel(
             nc.sync.dma_start(prior[:], period.rearrange("(c p) -> p c", p=P))
         features(3, 0, by_vector)
         quantize_w2(0, 1)
-        round_by_gpsimd(1, 0, held(rounded_shape, BF16, "w2_bf"))
+        to_tanh(groups[0], nc.gpsimd)
         features(3, 1, by_vector)
         for k in range(PACK, 2 * PACK):
             sigmoid(k - 1)
+            if k < 2 * PACK - 2:
+                to_tanh(groups[k - 3], nc.gpsimd)
             features(k, 0, by_vector)
             features(k, 1, by_vector)
         sigmoid(7)
+        round_w2(1, 0, reused(rounded_shape, BF16, "w2_bf10", FIFTH))
+        round_w2(1, 1, reused(rounded_shape, BF16, "w2_bf11", FIFTH + PIECE // 2))
         quantize_w2(1, 0)
-        round_w2(1, 1, reused(rounded_shape, BF16, "w2_bf11", TABLE_1 + PIECE))
-        to_tanh(0)
-        quantize_w2(1, 1)
 
         reflexes(0)
         for k in range(1, PACK + 1):
@@ -297,7 +305,9 @@ def tile_list_sound_change_dating_kernel(
             weigh(k - 1)
             borrow(k - 1, 0, M)
             if k == 1:
-                to_tanh(1)
+                quantize_w2(1, 1)
+            if k == 2:
+                to_tanh(groups[-1], nc.vector)
         reflexes(5)
         weigh(4)
         sum_z(0, 0, M)

@@ -171,31 +171,35 @@ def tile_list_sound_change_dating_kernel(
 
         def features(k, h, copy):
             b, t = tiles[k]
-            if k not in x1 and k in (2, 3):
-                x1[k] = reused([P, S], F32, f"x1_{k}", 4 * S * (k - 2))
+            if k not in x1 and k == 3:
+                x1[k] = reused([P, S], F32, "x1_3", 0)
             elif k not in x1:
-                x1[k] = ring.tile([P, S], F32, name="x1", bufs=4)
+                x1[k] = ring.tile([P, S], F32, name="x1", bufs=5)
             first = S + PASS * b + P * t
             words = [w1_w[b][:, a, t, :].bitcast(FP4X4) for a in range(2)]
             first_stage(x1[k], h, words, [planes[a][:, first : first + P] for a in range(2)], k, copy)
 
-        def reflexes(k):
+        def reflex(k, h, copy):
             b, t = tiles[k]
-            x2[k] = ring.tile([P, S], F32, name="x2", bufs=5)
+            if k not in x2:
+                x2[k] = ring.tile([P, S], F32, name="x2", bufs=5)
             cols = slice(P * t, P * (t + 1))
             words = [w2_w[b, a][:, cols].bitcast(FP8X4) for a in range(2)]
-            for h in range(2):
-                first_stage(x2[k], h, words, [w2_s[b, a][:, cols] for a in range(2)], k, nc.scalar.copy)
+            first_stage(x2[k], h, words, [w2_s[b, a][:, cols] for a in range(2)], k, copy)
 
-        groups = [(0, 1), (2, 3), (4,), (5, 6, 7)]
+        def reflexes(k):
+            for h in range(2):
+                reflex(k, h, nc.scalar.copy)
+
+        groups = [(0, 1), (2, 3), (4, 5, 6, 7)]
         sig, anc = {}, {}
         weighed = [held([P, PACK, M], F32, f"weighed{b}") for b in range(2)]
         loan = [held([P, PACK, M], F32, f"loan{b}") for b in range(2)]
 
         def sigmoid(k):
             group = [g for g in groups if k in g][0]
-            if group == (4,):
-                sig[group] = reused([P, 1, M], F32, "sig4", FIFTH + PIECE // 2 - 2 * M)
+            if k == 2:
+                sig[group] = reused([P, 2, M], F32, "sig2", FIFTH + PIECE // 4)
             elif group not in sig:
                 sig[group] = held([P, len(group), M], F32, f"sig{k}")
             nc.scalar.activation(sig[group][:, k - group[0], :], x1[k][:].indirect(p1[:]), ACT.Sigmoid, scale=2.0)
@@ -263,43 +267,49 @@ def tile_list_sound_change_dating_kernel(
 
         features(0, 0, by_scalar)
         features(1, 0, by_scalar)
+        features(2, 0, by_vector)
         features(0, 1, by_scalar)
         features(1, 1, by_scalar)
         sigmoid(0)
         sigmoid(1)
         round_w2(0, 0, held(rounded_shape, BF16, "w2_bf00"))
         order_w1(1, w1_late)
-        features(2, 1, by_vector)
-        features(2, 0, by_scalar)
+        features(2, 1, by_scalar)
+        features(3, 0, by_vector)
+        features(3, 1, by_vector)
         for q in range(4):
             nc.sync.dma_start(
                 w1_late[32 * q : 32 * q + 4, :, :N].bitcast(I32),
                 w3_scales[:, 4 * q : 4 * q + 4, :].rearrange("a r c -> r a c").bitcast(I32),
             )
-        quantize_w2(0, 0)
         sigmoid(2)
+        quantize_w2(0, 0)
+        features(4, 0, by_scalar)
+        features(4, 1, by_vector)
+        sigmoid(3)
         round_w2(0, 1, reused(rounded_shape, BF16, "w2_bf01", ANCESTORS + 4 * M))
         w3_w = reused([P, 2, N], I32, "w3_w", W1_LATE + 2 * H)
         nc.sync.dma_start(w3_w[:], w3_words.rearrange("a p c i -> p a (c i)").bitcast(I32))
         prior = reused([P, N // P], F32, "prior", W1_LATE + 2 * H + 8 * N)
         with nc.allow_non_contiguous_dma(reason="one value of period to a partition"):
             nc.sync.dma_start(prior[:], period.rearrange("(c p) -> p c", p=P))
-        features(3, 0, by_vector)
+        features(5, 0, by_vector)
         quantize_w2(0, 1)
         to_tanh(groups[0], nc.gpsimd)
-        features(3, 1, by_vector)
-        for k in range(PACK, 2 * PACK):
-            sigmoid(k - 1)
-            if k < 2 * PACK - 2:
-                to_tanh(groups[k - 3], nc.gpsimd)
+        to_tanh(groups[1], nc.gpsimd)
+        features(5, 1, by_vector)
+        for k in range(2 * PACK - 2, 2 * PACK):
+            sigmoid(k - 2)
             features(k, 0, by_vector)
             features(k, 1, by_vector)
+        reflex(0, 0, by_vector)
+        sigmoid(6)
         sigmoid(7)
         round_w2(1, 0, reused(rounded_shape, BF16, "w2_bf10", FIFTH))
         round_w2(1, 1, reused(rounded_shape, BF16, "w2_bf11", FIFTH + PIECE // 2))
         quantize_w2(1, 0)
 
-        reflexes(0)
+        reflex(0, 1, by_scalar)
         for k in range(1, PACK + 1):
             reflexes(k)
             weigh(k - 1)

@@ -191,21 +191,21 @@ def tile_list_sound_change_dating_kernel(
             for h in range(2):
                 reflex(k, h, nc.scalar.copy)
 
-        groups = [(0, 1), (2, 3), (4, 5, 6, 7)]
+        groups = [(0, 1), (2, 3, 4, 5, 6, 7)]
         sig, anc = {}, {}
         weighed = [held([P, PACK, M], F32, f"weighed{b}") for b in range(2)]
         loan = [held([P, PACK, M], F32, f"loan{b}") for b in range(2)]
 
         def sigmoid(k):
             group = [g for g in groups if k in g][0]
-            if k == 2:
-                sig[group] = reused([P, 2, M], F32, "sig2", FIFTH + PIECE // 4)
+            if k == 0:
+                sig[group] = reused([P, len(group), M], F32, "sig0", FIFTH + PIECE // 4)
             elif group not in sig:
                 sig[group] = held([P, len(group), M], F32, f"sig{k}")
             nc.scalar.activation(sig[group][:, k - group[0], :], x1[k][:].indirect(p1[:]), ACT.Sigmoid, scale=2.0)
 
         def to_tanh(group, engine):
-            if group[0] < PACK:
+            if group[0] == 0:
                 tanh = reused([P, len(group), M], F32, f"anc{group[0]}", ANCESTORS + 4 * M * group[0])
             else:
                 tanh = held([P, len(group), M], F32, f"anc{group[0]}")
@@ -285,7 +285,6 @@ def tile_list_sound_change_dating_kernel(
         sigmoid(2)
         quantize_w2(0, 0)
         features(4, 0, by_scalar)
-        features(4, 1, by_vector)
         sigmoid(3)
         round_w2(0, 1, reused(rounded_shape, BF16, "w2_bf01", ANCESTORS + 4 * M))
         w3_w = reused([P, 2, N], I32, "w3_w", W1_LATE + 2 * H)
@@ -293,31 +292,28 @@ def tile_list_sound_change_dating_kernel(
         prior = reused([P, N // P], F32, "prior", W1_LATE + 2 * H + 8 * N)
         with nc.allow_non_contiguous_dma(reason="one value of period to a partition"):
             nc.sync.dma_start(prior[:], period.rearrange("(c p) -> p c", p=P))
-        features(5, 0, by_vector)
+        features(4, 1, by_vector)
         quantize_w2(0, 1)
         to_tanh(groups[0], nc.gpsimd)
-        to_tanh(groups[1], nc.gpsimd)
+        features(5, 0, by_vector)
         features(5, 1, by_vector)
         for k in range(2 * PACK - 2, 2 * PACK):
             sigmoid(k - 2)
             features(k, 0, by_vector)
             features(k, 1, by_vector)
-        reflex(0, 0, by_vector)
         sigmoid(6)
         sigmoid(7)
         round_w2(1, 0, reused(rounded_shape, BF16, "w2_bf10", FIFTH))
         round_w2(1, 1, reused(rounded_shape, BF16, "w2_bf11", FIFTH + PIECE // 2))
         quantize_w2(1, 0)
+        quantize_w2(1, 1)
+        to_tanh(groups[1], nc.vector)
 
-        reflex(0, 1, by_scalar)
+        reflexes(0)
         for k in range(1, PACK + 1):
             reflexes(k)
             weigh(k - 1)
             borrow(k - 1, 0, M)
-            if k == 1:
-                quantize_w2(1, 1)
-            if k == 2:
-                to_tanh(groups[-1], nc.vector)
         reflexes(5)
         weigh(4)
         sum_z(0, 0, M)

@@ -24,6 +24,8 @@ BANKS = 8
 LIST = 16
 SCALE_ROWS = 32
 HALF = M // 2
+QUARTER = S // 4
+SHIFT = 3
 
 CHUNKS = [(0, HALF), (HALF, HALF + P), (HALF + P, M)]
 
@@ -104,11 +106,13 @@ def tile_list_sound_change_dating_kernel(
 
         v_w, w1_w = {}, {}
 
-        def gather_table(a):
-            for h in range(S // BANK):
-                v_w[a, h] = held([P, BANK], I32, f"v_w{a}{h}")
-                entries = idx[:, BANK // LIST * h : BANK // LIST * (h + 1)]
-                nc.vector.tensor_copy(v_w[a, h][:].bitcast(U32), tab_w[a][:].bitcast(U32).indirect(entries))
+        def gather_table(a, cuts):
+            for j0, j1 in zip(cuts, cuts[1:]):
+                h = j0 // BANK
+                if j0 % BANK == 0:
+                    v_w[a, h] = held([P, BANK], I32, f"v_w{a}{h}")
+                picked = tab_w[a][:].bitcast(U32).indirect(idx[:, j0 // LIST : j1 // LIST])
+                nc.vector.tensor_copy(v_w[a, h][:, j0 - BANK * h : j1 - BANK * h].bitcast(U32), picked)
 
         def order_w1(b, raw):
             w1_w[b] = held([P, 2, PACK, 2 * P], U8, f"w1_w{b}")
@@ -119,8 +123,8 @@ def tile_list_sound_change_dating_kernel(
 
         w1_w[0] = held([P, 2, PACK, 2 * P], U8, "w1_w0")
         order_first(0, nc.vector.tensor_copy)
-        gather_table(0)
-        gather_table(1)
+        gather_table(0, (0, BANK, S))
+        gather_table(1, (0, QUARTER, BANK, S))
         nc.sync.dma_start(w1_raw[1][:].bitcast(I32), w1_halves[0][:, 1, :].bitcast(I32))
         order_first(1, nc.scalar.copy)
 
@@ -156,28 +160,31 @@ def tile_list_sound_change_dating_kernel(
 
         tiles = [(b, t) for b in range(2) for t in range(PACK)]
 
-        def first_stage(x, h, words, scales, pair, copy):
-            cols = slice(BANK * h, BANK * (h + 1))
-            acc = bank(2 * pair + h)
+        def first_stage(x, j0, j1, words, scales, place, copy):
+            h = j0 // BANK
+            acc = bank(place)[:, : j1 - j0]
             for a in range(2):
                 nc.tensor.matmul_mx(
-                    acc[:], lhsT=words[a], lhsT_scale=scales[a],
-                    rhs=v_w[a, h][:].bitcast(FP8X4), rhs_scale=planes[a][:, cols],
+                    acc, lhsT=words[a], lhsT_scale=scales[a],
+                    rhs=v_w[a, h][:, j0 - BANK * h : j1 - BANK * h].bitcast(FP8X4), rhs_scale=planes[a][:, j0:j1],
                     start=a == 0, stop=a == 1,
                 )
-            copy(x[:, cols], acc[:])
+            copy(x[:, j0:j1], acc)
 
         x1, x2 = {}, {}
 
-        def features(k, h, copy):
+        def features(k, j0, j1, place, copy):
             b, t = tiles[k]
-            if k not in x1 and k == 3:
-                x1[k] = reused([P, S], F32, "x1_3", 0)
+            if k not in x1 and k == PACK:
+                x1[k] = reused([P, S], F32, "x1_4", 0)
             elif k not in x1:
                 x1[k] = ring.tile([P, S], F32, name="x1", bufs=5)
             first = S + PASS * b + P * t
             words = [w1_w[b][:, a, t, :].bitcast(FP4X4) for a in range(2)]
-            first_stage(x1[k], h, words, [planes[a][:, first : first + P] for a in range(2)], k, copy)
+            first_stage(x1[k], j0, j1, words, [planes[a][:, first : first + P] for a in range(2)], place, copy)
+
+        def feature_half(k, h, copy):
+            features(k, BANK * h, BANK * (h + 1), 2 * k + h + SHIFT, copy)
 
         def reflex(k, h, copy):
             b, t = tiles[k]
@@ -185,27 +192,28 @@ def tile_list_sound_change_dating_kernel(
                 x2[k] = ring.tile([P, S], F32, name="x2", bufs=5)
             cols = slice(P * t, P * (t + 1))
             words = [w2_w[b, a][:, cols].bitcast(FP8X4) for a in range(2)]
-            first_stage(x2[k], h, words, [w2_s[b, a][:, cols] for a in range(2)], k, copy)
+            scales = [w2_s[b, a][:, cols] for a in range(2)]
+            first_stage(x2[k], BANK * h, BANK * (h + 1), words, scales, 2 * k + h + SHIFT, copy)
 
         def reflexes(k):
             for h in range(2):
                 reflex(k, h, nc.scalar.copy)
 
-        groups = [(0, 1), (2, 3, 4, 5, 6, 7)]
+        groups = [(0, 1, 2), (3,), (4, 5, 6, 7)]
         sig, anc = {}, {}
         weighed = [held([P, PACK, M], F32, f"weighed{b}") for b in range(2)]
         loan = [held([P, PACK, M], F32, f"loan{b}") for b in range(2)]
 
         def sigmoid(k):
             group = [g for g in groups if k in g][0]
-            if k == 0:
-                sig[group] = reused([P, len(group), M], F32, "sig0", FIFTH + PIECE // 4)
+            if k == 3:
+                sig[group] = reused([P, 1, M], F32, "sig3", FIFTH + PIECE // 2 - 2 * M)
             elif group not in sig:
                 sig[group] = held([P, len(group), M], F32, f"sig{k}")
             nc.scalar.activation(sig[group][:, k - group[0], :], x1[k][:].indirect(p1[:]), ACT.Sigmoid, scale=2.0)
 
         def to_tanh(group, engine):
-            if group[0] == 0:
+            if group[0] < PACK:
                 tanh = reused([P, len(group), M], F32, f"anc{group[0]}", ANCESTORS + 4 * M * group[0])
             else:
                 tanh = held([P, len(group), M], F32, f"anc{group[0]}")
@@ -265,51 +273,50 @@ def tile_list_sound_change_dating_kernel(
 
         rounded_shape = [P, PACK, P, PACK]
 
-        features(0, 0, by_scalar)
-        features(1, 0, by_scalar)
-        features(2, 0, by_vector)
-        features(0, 1, by_scalar)
-        features(1, 1, by_scalar)
+        for q in range(2):
+            for k in range(SHIFT):
+                features(k, QUARTER * q, QUARTER * (q + 1), SHIFT * q + k, by_scalar)
+        for k in range(2):
+            features(k, BANK, S, 2 * SHIFT + k, by_scalar)
         sigmoid(0)
         sigmoid(1)
         round_w2(0, 0, held(rounded_shape, BF16, "w2_bf00"))
         order_w1(1, w1_late)
-        features(2, 1, by_scalar)
-        features(3, 0, by_vector)
-        features(3, 1, by_vector)
+        feature_half(2, 1, by_vector)
         for q in range(4):
             nc.sync.dma_start(
                 w1_late[32 * q : 32 * q + 4, :, :N].bitcast(I32),
                 w3_scales[:, 4 * q : 4 * q + 4, :].rearrange("a r c -> r a c").bitcast(I32),
             )
-        sigmoid(2)
         quantize_w2(0, 0)
-        features(4, 0, by_scalar)
-        sigmoid(3)
-        round_w2(0, 1, reused(rounded_shape, BF16, "w2_bf01", ANCESTORS + 4 * M))
+        sigmoid(2)
+        feature_half(3, 0, by_scalar)
+        feature_half(3, 1, by_scalar)
+        feature_half(4, 0, by_vector)
+        round_w2(0, 1, reused(rounded_shape, BF16, "w2_bf01", ANCESTORS + PIECE // 2))
         w3_w = reused([P, 2, N], I32, "w3_w", W1_LATE + 2 * H)
         nc.sync.dma_start(w3_w[:], w3_words.rearrange("a p c i -> p a (c i)").bitcast(I32))
         prior = reused([P, N // P], F32, "prior", W1_LATE + 2 * H + 8 * N)
         with nc.allow_non_contiguous_dma(reason="one value of period to a partition"):
             nc.sync.dma_start(prior[:], period.rearrange("(c p) -> p c", p=P))
-        features(4, 1, by_vector)
+        feature_half(4, 1, by_vector)
         quantize_w2(0, 1)
         to_tanh(groups[0], nc.gpsimd)
-        features(5, 0, by_vector)
-        features(5, 1, by_vector)
-        for k in range(2 * PACK - 2, 2 * PACK):
-            sigmoid(k - 2)
-            features(k, 0, by_vector)
-            features(k, 1, by_vector)
-        sigmoid(6)
+        sigmoid(3)
+        to_tanh(groups[1], nc.gpsimd)
+        for k in range(PACK + 1, 2 * PACK):
+            feature_half(k, 0, by_vector)
+            feature_half(k, 1, by_vector)
+            sigmoid(k - 1)
+        reflex(0, 0, by_vector)
+        reflex(0, 1, by_vector)
         sigmoid(7)
         round_w2(1, 0, reused(rounded_shape, BF16, "w2_bf10", FIFTH))
         round_w2(1, 1, reused(rounded_shape, BF16, "w2_bf11", FIFTH + PIECE // 2))
         quantize_w2(1, 0)
         quantize_w2(1, 1)
-        to_tanh(groups[1], nc.vector)
+        to_tanh(groups[2], nc.vector)
 
-        reflexes(0)
         for k in range(1, PACK + 1):
             reflexes(k)
             weigh(k - 1)

@@ -25,16 +25,15 @@ LIST = 16
 SCALE_ROWS = 32
 HALF = M // 2
 QUARTER = S // 4
-SHIFT = 3
-
+KB = 1024
+EARLY = 3
 CHUNKS = [(0, HALF), (HALF, HALF + P), (HALF + P, M)]
 
-PIECE = 4 * PACK * PASS
-TABLE_0 = PIECE - 64
-W1_LATE = PIECE
-TABLE_1 = 4 * PIECE
-ANCESTORS = 6 * PIECE
-FIFTH = 7 * PIECE
+TABLE = (0, 20 * KB)
+W2_RAW = {(0, 0): 0, (0, 1): 11 * KB, (1, 0): 20 * KB, (1, 1): 28 * KB}
+W1_LATE = 8 * KB
+W1_SECOND = 10 * KB
+ROUNDED = 36 * KB
 
 
 def tile_list_sound_change_dating_kernel(
@@ -43,7 +42,6 @@ def tile_list_sound_change_dating_kernel(
     nc = tc.nc
     with ExitStack() as ctx:
         keep = ctx.enter_context(tc.tile_pool(name="keep", bufs=1))
-        ring = ctx.enter_context(tc.tile_pool(name="ring", bufs=1))
         reuse = ctx.enter_context(tc.tile_pool(name="reuse", bufs=1))
         psum = ctx.enter_context(tc.psum_pool(name="psum", bufs=1))
 
@@ -53,8 +51,11 @@ def tile_list_sound_change_dating_kernel(
         def reused(shape, dtype, name, offset):
             return reuse.tile(shape, dtype, name=name, offset=offset, align_bytes=64)
 
-        def bank(i):
-            return psum.tile([P, BANK], F32, name=f"bank{i % BANKS}")
+        filled = []
+
+        def free_bank():
+            filled.append(psum.tile([P, BANK], F32, name=f"bank{len(filled) % BANKS}"))
+            return filled[-1]
 
         idx = keep.tile([P, S // LIST], U16, name="idx")
         p1 = keep.tile([P, M // LIST], U16, name="p1")
@@ -74,9 +75,9 @@ def tile_list_sound_change_dating_kernel(
         nc.gpsimd.memset(warm[:, 0:1], 0.0)
         nc.scalar.activation(warm[:, 1:2], warm[:, 0:1], ACT.Sigmoid)
 
-        tab_w = [reused([P, T], I32, f"tab_w{a}", offset) for a, offset in enumerate((TABLE_0, TABLE_1))]
+        tab_w = [reused([P, T], I32, f"tab_w{a}", TABLE[a]) for a in range(2)]
         w1_halves = w1_words.rearrange("a p (b c) -> b p a c", b=2)
-        w1_raw = [held([P, H], U8, "w1_raw0"), reused([P, H], U8, "w1_raw1", TABLE_0 + 4 * T - H)]
+        w1_raw = [held([P, H], U8, "w1_raw0"), reused([P, H], U8, "w1_raw1", W1_SECOND)]
         nc.sync.dma_start(tab_s[:SCALE_ROWS, :].bitcast(I32), tab_scales.rearrange("a q c -> (a q) c").bitcast(I32))
         nc.sync.dma_start(idx[:], offs)
         nc.sync.dma_start(w1_raw[0][:].bitcast(I32), w1_halves[0][:, 0, :].bitcast(I32))
@@ -104,7 +105,7 @@ def tile_list_sound_change_dating_kernel(
                         planes[a][32 * q : 32 * q + 4, :].bitcast(I32), planes[0][row : row + 4, :].bitcast(I32)
                     )
 
-        v_w, w1_w = {}, {}
+        v_w = {}
 
         def gather_table(a, cuts):
             for j0, j1 in zip(cuts, cuts[1:]):
@@ -114,55 +115,49 @@ def tile_list_sound_change_dating_kernel(
                 picked = tab_w[a][:].bitcast(U32).indirect(idx[:, j0 // LIST : j1 // LIST])
                 nc.vector.tensor_copy(v_w[a, h][:, j0 - BANK * h : j1 - BANK * h].bitcast(U32), picked)
 
-        def order_w1(b, raw):
-            w1_w[b] = held([P, 2, PACK, 2 * P], U8, f"w1_w{b}")
-            nc.vector.tensor_copy(w1_w[b][:].bitcast(U16), raw[:].bitcast(U16).rearrange("p a (m t) -> p a t m", t=PACK))
+        w1_w = [held([P, 2, PACK, 2 * P], U8, f"w1_w{b}") for b in range(2)]
 
         def order_first(a, copy):
             copy(w1_w[0][:, a].bitcast(U16), w1_raw[a][:].bitcast(U16).rearrange("p (m t) -> p t m", t=PACK))
 
-        w1_w[0] = held([P, 2, PACK, 2 * P], U8, "w1_w0")
         order_first(0, nc.vector.tensor_copy)
         gather_table(0, (0, BANK, S))
         gather_table(1, (0, QUARTER, BANK, S))
         nc.sync.dma_start(w1_raw[1][:].bitcast(I32), w1_halves[0][:, 1, :].bitcast(I32))
         order_first(1, nc.scalar.copy)
 
+        w1_late = reused([P, 2, H], U8, "w1_late", W1_LATE)
+        nc.sync.dma_start(w1_late[:].bitcast(I32), w1_halves[1].bitcast(I32))
         w2_raw = {}
-
-        def load_w2(b, a, offset):
+        for (b, a), offset in W2_RAW.items():
             w2_raw[b, a] = reused([P, PACK, PASS], F32, f"w2_raw{b}{a}", offset)
             rows = w2[PASS * a : PASS * (a + 1), PASS * b : PASS * (b + 1)]
             nc.sync.dma_start(w2_raw[b, a][:], rows.rearrange("(p j) c -> p j c", j=PACK))
+        nc.vector.tensor_copy(
+            w1_w[1][:].bitcast(U16), w1_late[:].bitcast(U16).rearrange("p a (m t) -> p a t m", t=PACK)
+        )
 
-        load_w2(0, 0, 0)
-        w1_late = reused([P, 2, H], U8, "w1_late", W1_LATE)
-        nc.sync.dma_start(w1_late[:].bitcast(I32), w1_halves[1].bitcast(I32))
-        load_w2(0, 1, W1_LATE + 2 * H)
-        load_w2(1, 0, TABLE_1 + PIECE)
-        load_w2(1, 1, TABLE_1)
+        def round_by_gpsimd(raw, rounded):
+            for ms in (slice(0, P // 2), slice(P // 2, P)):
+                nc.gpsimd.tensor_scalar(
+                    rounded[:, :, ms].rearrange("p t m j -> p m t j"),
+                    raw[:].rearrange("p j (m t) -> p m t j", t=PACK)[:, ms],
+                    1.0, 0.0, ALU.mult, ALU.add,
+                )
 
-        w2_bf, w2_w, w2_s = {}, {}, {}
-
-        def round_w2(b, a, rounded):
-            w2_bf[b, a] = rounded
+        def round_by_vector(raw, rounded):
             nc.vector.tensor_copy(
-                w2_bf[b, a][:].rearrange("p (u t) m j -> p u m j t", u=2),
-                w2_raw[b, a][:].rearrange("p j (m u t) -> p u m j t", u=2, t=2),
+                rounded.rearrange("p (u t) m j -> p u m j t", u=2),
+                raw[:].rearrange("p j (m u t) -> p u m j t", u=2, t=2),
             )
 
-        def quantize_w2(b, a):
-            w2_w[b, a] = held([P, PASS], I32, f"w2_w{b}{a}")
-            w2_s[b, a] = held([P, PASS], U8, f"w2_s{b}{a}")
-            nc.vector.quantize_mx(
-                w2_w[b, a][:].bitcast(FP8X4), w2_s[b, a][:], w2_bf[b, a][:].rearrange("p t m j -> p (t m j)")
-            )
-
+        w2_w = [held([P, 2, PASS], I32, f"w2_w{b}") for b in range(2)]
+        w2_s = [held([P, 2, PASS], U8, f"w2_s{b}") for b in range(2)]
         tiles = [(b, t) for b in range(2) for t in range(PACK)]
 
-        def first_stage(x, j0, j1, words, scales, place, copy):
+        def first_stage(x, j0, j1, words, scales, copy):
             h = j0 // BANK
-            acc = bank(place)[:, : j1 - j0]
+            acc = free_bank()[:, : j1 - j0]
             for a in range(2):
                 nc.tensor.matmul_mx(
                     acc, lhsT=words[a], lhsT_scale=scales[a],
@@ -171,60 +166,38 @@ def tile_list_sound_change_dating_kernel(
                 )
             copy(x[:, j0:j1], acc)
 
-        x1, x2 = {}, {}
+        x1 = [held([P, S], F32, f"x1_{k}") for k in range(7)] + [reused([P, S], F32, "x1_7", ROUNDED)]
+        x2 = [held([P, S], F32, f"x2_{k}") for k in range(8)]
 
-        def features(k, j0, j1, place, copy):
+        def features(k, j0, j1, copy):
             b, t = tiles[k]
-            if k not in x1 and k == PACK:
-                x1[k] = reused([P, S], F32, "x1_4", 0)
-            elif k not in x1:
-                x1[k] = ring.tile([P, S], F32, name="x1", bufs=5)
             first = S + PASS * b + P * t
             words = [w1_w[b][:, a, t, :].bitcast(FP4X4) for a in range(2)]
-            first_stage(x1[k], j0, j1, words, [planes[a][:, first : first + P] for a in range(2)], place, copy)
-
-        def feature_half(k, h, copy):
-            features(k, BANK * h, BANK * (h + 1), 2 * k + h + SHIFT, copy)
+            first_stage(x1[k], j0, j1, words, [planes[a][:, first : first + P] for a in range(2)], copy)
 
         def reflex(k, h, copy):
             b, t = tiles[k]
-            if k not in x2:
-                x2[k] = ring.tile([P, S], F32, name="x2", bufs=5)
             cols = slice(P * t, P * (t + 1))
-            words = [w2_w[b, a][:, cols].bitcast(FP8X4) for a in range(2)]
-            scales = [w2_s[b, a][:, cols] for a in range(2)]
-            first_stage(x2[k], BANK * h, BANK * (h + 1), words, scales, 2 * k + h + SHIFT, copy)
+            words = [w2_w[b][:, a, cols].bitcast(FP8X4) for a in range(2)]
+            scales = [w2_s[b][:, a, cols] for a in range(2)]
+            first_stage(x2[k], BANK * h, BANK * (h + 1), words, scales, copy)
 
-        def reflexes(k):
-            for h in range(2):
-                reflex(k, h, nc.scalar.copy)
-
-        groups = [(0, 1, 2), (3,), (4, 5, 6, 7)]
-        sig, anc = {}, {}
+        sig = [held([P, PACK, M], F32, f"sig{b}") for b in range(2)]
+        anc = [reused([P, PACK, M], F32, f"anc{b}", (24 + 8 * b) * KB) for b in range(2)]
         weighed = [held([P, PACK, M], F32, f"weighed{b}") for b in range(2)]
         loan = [held([P, PACK, M], F32, f"loan{b}") for b in range(2)]
 
         def sigmoid(k):
-            group = [g for g in groups if k in g][0]
-            if k == 3:
-                sig[group] = reused([P, 1, M], F32, "sig3", FIFTH + PIECE // 2 - 2 * M)
-            elif group not in sig:
-                sig[group] = held([P, len(group), M], F32, f"sig{k}")
-            nc.scalar.activation(sig[group][:, k - group[0], :], x1[k][:].indirect(p1[:]), ACT.Sigmoid, scale=2.0)
+            b, t = tiles[k]
+            nc.scalar.activation(sig[b][:, t, :], x1[k][:].indirect(p1[:]), ACT.Sigmoid, scale=2.0)
 
-        def to_tanh(group, engine):
-            if group[0] < PACK:
-                tanh = reused([P, len(group), M], F32, f"anc{group[0]}", ANCESTORS + 4 * M * group[0])
-            else:
-                tanh = held([P, len(group), M], F32, f"anc{group[0]}")
-            engine.tensor_scalar(tanh[:], sig[group][:], 2.0, -1.0, ALU.mult, ALU.add)
-            for i, k in enumerate(group):
-                anc[k] = tanh[:, i, :]
+        def to_tanh(b):
+            nc.vector.tensor_scalar(anc[b][:], sig[b][:], 2.0, -1.0, ALU.mult, ALU.add)
 
         def weigh(k, m0=0, m1=M):
             b, t = tiles[k]
             picked = x2[k][:].indirect(p2[:, m0 // LIST : m1 // LIST])
-            nc.vector.tensor_tensor(weighed[b][:, t, m0:m1], picked, anc[k][:, m0:m1], ALU.mult)
+            nc.vector.tensor_tensor(weighed[b][:, t, m0:m1], picked, anc[b][:, t, m0:m1], ALU.mult)
 
         def borrow(k, m0, m1):
             b, t = tiles[k]
@@ -249,7 +222,7 @@ def tile_list_sound_change_dating_kernel(
 
         def score(m0, m1):
             y = held([P, N // P, m1 - m0], F32, f"y{m0}")
-            accs = [bank(3 * CHUNKS.index((m0, m1)) + c)[:, : m1 - m0] for c in range(N // P)]
+            accs = [free_bank()[:, : m1 - m0] for c in range(N // P)]
             for b, start in enumerate((0, m0)):
                 part = slice(m0 - start, m1 - start)
                 for c, acc in enumerate(accs):
@@ -271,75 +244,78 @@ def tile_list_sound_change_dating_kernel(
 
         by_scalar, by_vector = nc.scalar.copy, nc.vector.tensor_copy
 
-        rounded_shape = [P, PACK, P, PACK]
-
-        for q in range(2):
-            for k in range(SHIFT):
-                features(k, QUARTER * q, QUARTER * (q + 1), SHIFT * q + k, by_scalar)
-        for k in range(2):
-            features(k, BANK, S, 2 * SHIFT + k, by_scalar)
-        sigmoid(0)
-        sigmoid(1)
-        round_w2(0, 0, held(rounded_shape, BF16, "w2_bf00"))
-        order_w1(1, w1_late)
-        feature_half(2, 1, by_vector)
         for q in range(4):
             nc.sync.dma_start(
                 w1_late[32 * q : 32 * q + 4, :, :N].bitcast(I32),
                 w3_scales[:, 4 * q : 4 * q + 4, :].rearrange("a r c -> r a c").bitcast(I32),
             )
-        quantize_w2(0, 0)
-        sigmoid(2)
-        feature_half(3, 0, by_scalar)
-        feature_half(3, 1, by_scalar)
-        feature_half(4, 0, by_vector)
-        round_w2(0, 1, reused(rounded_shape, BF16, "w2_bf01", ANCESTORS + PIECE // 2))
-        w3_w = reused([P, 2, N], I32, "w3_w", W1_LATE + 2 * H)
+        first_half = reused([P, 2, PACK, P, PACK], BF16, "w2_bf0", ROUNDED)
+        for a in range(2):
+            round_by_gpsimd(w2_raw[0, a], first_half[:, a])
+        w3_w = reused([P, 2, N], I32, "w3_w", 0)
         nc.sync.dma_start(w3_w[:], w3_words.rearrange("a p c i -> p a (c i)").bitcast(I32))
-        prior = reused([P, N // P], F32, "prior", W1_LATE + 2 * H + 8 * N)
+        prior = reused([P, N // P], F32, "prior", 4 * KB)
         with nc.allow_non_contiguous_dma(reason="one value of period to a partition"):
             nc.sync.dma_start(prior[:], period.rearrange("(c p) -> p c", p=P))
-        feature_half(4, 1, by_vector)
-        quantize_w2(0, 1)
-        to_tanh(groups[0], nc.gpsimd)
-        sigmoid(3)
-        to_tanh(groups[1], nc.gpsimd)
-        for k in range(PACK + 1, 2 * PACK):
-            feature_half(k, 0, by_vector)
-            feature_half(k, 1, by_vector)
-            sigmoid(k - 1)
+
+        for q in range(2):
+            for k in range(EARLY):
+                features(k, QUARTER * q, QUARTER * (q + 1), by_scalar)
+        features(0, BANK, S, by_scalar)
+        for k in range(1, EARLY):
+            features(k, BANK, S, by_vector)
+        for k in range(EARLY, 7):
+            features(k, 0, BANK, by_vector)
+            features(k, BANK, S, by_vector)
+        nc.vector.quantize_mx(
+            w2_w[0][:].rearrange("p a c -> p (a c)").bitcast(FP8X4), w2_s[0][:].rearrange("p a c -> p (a c)"),
+            first_half[:].rearrange("p a t m j -> p (a t m j)"),
+        )
+        features(7, 0, BANK, by_vector)
+        features(7, BANK, S, by_vector)
+        for k in range(8):
+            sigmoid(k)
+        third = reused([P, PACK, P, PACK], BF16, "w2_bf10", ROUNDED + 4 * KB)
+        round_by_gpsimd(w2_raw[1, 0], third[:])
         reflex(0, 0, by_vector)
         reflex(0, 1, by_vector)
-        sigmoid(7)
-        round_w2(1, 0, reused(rounded_shape, BF16, "w2_bf10", FIFTH))
-        round_w2(1, 1, reused(rounded_shape, BF16, "w2_bf11", FIFTH + PIECE // 2))
-        quantize_w2(1, 0)
-        quantize_w2(1, 1)
-        to_tanh(groups[2], nc.vector)
+        fourth = reused([P, PACK, P, PACK], BF16, "w2_bf11", W2_RAW[1, 0])
+        round_by_vector(w2_raw[1, 1], fourth[:])
+        nc.vector.quantize_mx(w2_w[1][:, 0].bitcast(FP8X4), w2_s[1][:, 0], third[:].rearrange("p t m j -> p (t m j)"))
+        to_tanh(0)
+        nc.vector.quantize_mx(w2_w[1][:, 1].bitcast(FP8X4), w2_s[1][:, 1], fourth[:].rearrange("p t m j -> p (t m j)"))
 
-        for k in range(1, PACK + 1):
+        def reflexes(k):
+            for h in range(2):
+                reflex(k, h, by_scalar)
+
+        for k in range(1, PACK):
             reflexes(k)
-            weigh(k - 1)
-            borrow(k - 1, 0, M)
-        reflexes(5)
+        weigh(0)
+        weigh(1)
+        to_tanh(1)
+        weigh(2)
+        weigh(3)
+        for k in range(PACK):
+            borrow(k, 0, M)
+        for k in range(PACK, 2 * PACK):
+            reflexes(k)
         weigh(4)
         sum_z(0, 0, M)
-        reflexes(6)
         weigh(5)
         quantize_z(0, 0, M)
-        reflexes(7)
         weigh(6)
         weigh(7, 0, HALF)
         weigh(7, HALF, M)
         for m0, m1 in CHUNKS:
             for k in range(PACK, 2 * PACK):
                 borrow(k, m0, m1)
-        first, second, third = CHUNKS
-        sum_z(1, *first)
-        sum_z(1, *second)
-        quantize_z(1, *first)
-        sum_z(1, *third)
-        quantize_z(1, *second)
-        quantize_z(1, *third)
+        wide, middle, last = CHUNKS
+        sum_z(1, *wide)
+        sum_z(1, *middle)
+        quantize_z(1, *wide)
+        sum_z(1, *last)
+        quantize_z(1, *middle)
+        quantize_z(1, *last)
         for m0, m1 in CHUNKS:
             score(m0, m1)

@@ -33,7 +33,10 @@ TABLE = (0, 20 * KB)
 W2_RAW = {(0, 0): 0, (0, 1): 11 * KB, (1, 0): 20 * KB, (1, 1): 28 * KB}
 W1_LATE = 8 * KB
 W1_SECOND = 10 * KB
-ROUNDED = 36 * KB
+ROUNDED = {(0, 0): 36 * KB, (0, 1): 40 * KB, (1, 0): 40 * KB, (1, 1): 44 * KB}
+SIGMOIDS = 44 * KB
+ANCESTORS = (20 * KB, 28 * KB)
+X1_AT = {2: 52 * KB, 4: 52 * KB, 5: 36 * KB, 6: 11 * KB, 7: 15 * KB}
 
 
 def tile_list_sound_change_dating_kernel(
@@ -115,7 +118,7 @@ def tile_list_sound_change_dating_kernel(
                 picked = tab_w[a][:].bitcast(U32).indirect(idx[:, j0 // LIST : j1 // LIST])
                 nc.vector.tensor_copy(v_w[a, h][:, j0 - BANK * h : j1 - BANK * h].bitcast(U32), picked)
 
-        w1_w = [held([P, 2, PACK, 2 * P], U8, f"w1_w{b}") for b in range(2)]
+        w1_w = [held([P, 2, PACK, 2 * P], U8, "w1_w0"), reused([P, 2, PACK, 2 * P], U8, "w1_w1", 0)]
 
         def order_first(a, copy):
             copy(w1_w[0][:, a].bitcast(U16), w1_raw[a][:].bitcast(U16).rearrange("p (m t) -> p t m", t=PACK))
@@ -126,33 +129,45 @@ def tile_list_sound_change_dating_kernel(
         nc.sync.dma_start(w1_raw[1][:].bitcast(I32), w1_halves[0][:, 1, :].bitcast(I32))
         order_first(1, nc.scalar.copy)
 
+        w2_raw = {key: reused([P, PACK, PASS], F32, f"w2_raw{key[0]}{key[1]}", at) for key, at in W2_RAW.items()}
+        rounded = {key: reused([P, PACK, P, PACK], BF16, f"w2_bf{key[0]}{key[1]}", at) for key, at in ROUNDED.items()}
+
+        def load_w2(b, a, c0=0, c1=PASS):
+            rows = w2[PASS * a : PASS * (a + 1), PASS * b + c0 : PASS * b + c1]
+            nc.sync.dma_start(w2_raw[b, a][:, :, c0:c1], rows.rearrange("(p j) c -> p j c", j=PACK))
+
+        load_w2(0, 0, 0, PASS // 2)
+        load_w2(0, 0, PASS // 2, PASS)
         w1_late = reused([P, 2, H], U8, "w1_late", W1_LATE)
         nc.sync.dma_start(w1_late[:].bitcast(I32), w1_halves[1].bitcast(I32))
-        w2_raw = {}
-        for (b, a), offset in W2_RAW.items():
-            w2_raw[b, a] = reused([P, PACK, PASS], F32, f"w2_raw{b}{a}", offset)
-            rows = w2[PASS * a : PASS * (a + 1), PASS * b : PASS * (b + 1)]
-            nc.sync.dma_start(w2_raw[b, a][:], rows.rearrange("(p j) c -> p j c", j=PACK))
-        nc.vector.tensor_copy(
-            w1_w[1][:].bitcast(U16), w1_late[:].bitcast(U16).rearrange("p a (m t) -> p a t m", t=PACK)
-        )
+        load_w2(0, 1)
+        load_w2(1, 0)
+        load_w2(1, 1)
 
-        def round_by_gpsimd(raw, rounded):
+        def round_by_gpsimd(b, a):
             for ms in (slice(0, P // 2), slice(P // 2, P)):
                 nc.gpsimd.tensor_scalar(
-                    rounded[:, :, ms].rearrange("p t m j -> p m t j"),
-                    raw[:].rearrange("p j (m t) -> p m t j", t=PACK)[:, ms],
+                    rounded[b, a][:, :, ms].rearrange("p t m j -> p m t j"),
+                    w2_raw[b, a][:].rearrange("p j (m t) -> p m t j", t=PACK)[:, ms],
                     1.0, 0.0, ALU.mult, ALU.add,
                 )
 
-        def round_by_vector(raw, rounded):
+        def round_by_vector(b, a):
             nc.vector.tensor_copy(
-                rounded.rearrange("p (u t) m j -> p u m j t", u=2),
-                raw[:].rearrange("p j (m u t) -> p u m j t", u=2, t=2),
+                rounded[b, a][:].rearrange("p (u t) m j -> p u m j t", u=2),
+                w2_raw[b, a][:].rearrange("p j (m u t) -> p u m j t", u=2, t=2),
             )
 
-        w2_w = [held([P, 2, PASS], I32, f"w2_w{b}") for b in range(2)]
-        w2_s = [held([P, 2, PASS], U8, f"w2_s{b}") for b in range(2)]
+        w2_w = {(0, a): held([P, PASS], I32, f"w2_w0{a}") for a in range(2)}
+        for a in range(2):
+            w2_w[1, a] = reused([P, PASS], I32, f"w2_w1{a}", SIGMOIDS + (4 + 2 * a) * KB)
+        w2_s = {key: held([P, PASS], U8, f"w2_s{key[0]}{key[1]}") for key in W2_RAW}
+
+        def quantize_w2(b, a):
+            nc.vector.quantize_mx(
+                w2_w[b, a][:].bitcast(FP8X4), w2_s[b, a][:], rounded[b, a][:].rearrange("p t m j -> p (t m j)")
+            )
+
         tiles = [(b, t) for b in range(2) for t in range(PACK)]
 
         def first_stage(x, j0, j1, words, scales, copy):
@@ -166,7 +181,7 @@ def tile_list_sound_change_dating_kernel(
                 )
             copy(x[:, j0:j1], acc)
 
-        x1 = [held([P, S], F32, f"x1_{k}") for k in range(7)] + [reused([P, S], F32, "x1_7", ROUNDED)]
+        x1 = [reused([P, S], F32, f"x1_{k}", X1_AT[k]) if k in X1_AT else held([P, S], F32, f"x1_{k}") for k in range(8)]
         x2 = [held([P, S], F32, f"x2_{k}") for k in range(8)]
 
         def features(k, j0, j1, copy):
@@ -178,21 +193,21 @@ def tile_list_sound_change_dating_kernel(
         def reflex(k, h, copy):
             b, t = tiles[k]
             cols = slice(P * t, P * (t + 1))
-            words = [w2_w[b][:, a, cols].bitcast(FP8X4) for a in range(2)]
-            scales = [w2_s[b][:, a, cols] for a in range(2)]
+            words = [w2_w[b, a][:, cols].bitcast(FP8X4) for a in range(2)]
+            scales = [w2_s[b, a][:, cols] for a in range(2)]
             first_stage(x2[k], BANK * h, BANK * (h + 1), words, scales, copy)
 
-        sig = [held([P, PACK, M], F32, f"sig{b}") for b in range(2)]
-        anc = [reused([P, PACK, M], F32, f"anc{b}", (24 + 8 * b) * KB) for b in range(2)]
+        sig = [reused([P, PACK, M], F32, "sig0", SIGMOIDS), held([P, PACK, M], F32, "sig1")]
+        anc = [reused([P, PACK, M], F32, f"anc{b}", ANCESTORS[b]) for b in range(2)]
         weighed = [held([P, PACK, M], F32, f"weighed{b}") for b in range(2)]
-        loan = [held([P, PACK, M], F32, f"loan{b}") for b in range(2)]
+        loan = [reused([P, PACK, M], F32, "loan0", ROUNDED[1, 0]), held([P, PACK, M], F32, "loan1")]
 
         def sigmoid(k):
             b, t = tiles[k]
             nc.scalar.activation(sig[b][:, t, :], x1[k][:].indirect(p1[:]), ACT.Sigmoid, scale=2.0)
 
-        def to_tanh(b):
-            nc.vector.tensor_scalar(anc[b][:], sig[b][:], 2.0, -1.0, ALU.mult, ALU.add)
+        def to_tanh(b, engine):
+            engine.tensor_scalar(anc[b][:], sig[b][:], 2.0, -1.0, ALU.mult, ALU.add)
 
         def weigh(k, m0=0, m1=M):
             b, t = tiles[k]
@@ -244,67 +259,73 @@ def tile_list_sound_change_dating_kernel(
 
         by_scalar, by_vector = nc.scalar.copy, nc.vector.tensor_copy
 
+        def whole(stage, k, copy):
+            for h in range(2):
+                stage(k, h, copy)
+
+        def feature(k, h, copy):
+            features(k, BANK * h, BANK * (h + 1), copy)
+
+        round_by_gpsimd(0, 0)
+        for k in range(EARLY):
+            features(k, 0, QUARTER, by_scalar)
+        for k in range(EARLY):
+            features(k, QUARTER, BANK, by_vector if k else by_scalar)
+        for k in range(EARLY):
+            feature(k, 1, by_vector if k else by_scalar)
+        feature(3, 0, by_scalar)
+        sigmoid(0)
+        sigmoid(1)
+        feature(3, 1, by_scalar)
+        sigmoid(2)
+        sigmoid(3)
+        nc.vector.tensor_copy(
+            w1_w[1][:].bitcast(U16), w1_late[:].bitcast(U16).rearrange("p a (m t) -> p a t m", t=PACK)
+        )
         for q in range(4):
             nc.sync.dma_start(
                 w1_late[32 * q : 32 * q + 4, :, :N].bitcast(I32),
                 w3_scales[:, 4 * q : 4 * q + 4, :].rearrange("a r c -> r a c").bitcast(I32),
             )
-        first_half = reused([P, 2, PACK, P, PACK], BF16, "w2_bf0", ROUNDED)
-        for a in range(2):
-            round_by_gpsimd(w2_raw[0, a], first_half[:, a])
-        w3_w = reused([P, 2, N], I32, "w3_w", 0)
+        w3_w = reused([P, 2, N], I32, "w3_w", 2 * KB)
         nc.sync.dma_start(w3_w[:], w3_words.rearrange("a p c i -> p a (c i)").bitcast(I32))
-        prior = reused([P, N // P], F32, "prior", 4 * KB)
+        prior = reused([P, N // P], F32, "prior", 5 * KB)
         with nc.allow_non_contiguous_dma(reason="one value of period to a partition"):
             nc.sync.dma_start(prior[:], period.rearrange("(c p) -> p c", p=P))
-
-        for q in range(2):
-            for k in range(EARLY):
-                features(k, QUARTER * q, QUARTER * (q + 1), by_scalar)
-        features(0, BANK, S, by_scalar)
-        for k in range(1, EARLY):
-            features(k, BANK, S, by_vector)
-        for k in range(EARLY, 7):
-            features(k, 0, BANK, by_vector)
-            features(k, BANK, S, by_vector)
-        nc.vector.quantize_mx(
-            w2_w[0][:].rearrange("p a c -> p (a c)").bitcast(FP8X4), w2_s[0][:].rearrange("p a c -> p (a c)"),
-            first_half[:].rearrange("p a t m j -> p (a t m j)"),
-        )
-        features(7, 0, BANK, by_vector)
-        features(7, BANK, S, by_vector)
-        for k in range(8):
+        round_by_vector(0, 1)
+        quantize_w2(0, 0)
+        quantize_w2(0, 1)
+        round_by_gpsimd(1, 0)
+        to_tanh(0, nc.gpsimd)
+        whole(feature, 4, by_scalar)
+        for k in range(5, 8):
+            whole(feature, k, by_vector)
+        for k in (5, 4, 6, 7):
             sigmoid(k)
-        third = reused([P, PACK, P, PACK], BF16, "w2_bf10", ROUNDED + 4 * KB)
-        round_by_gpsimd(w2_raw[1, 0], third[:])
-        reflex(0, 0, by_vector)
-        reflex(0, 1, by_vector)
-        fourth = reused([P, PACK, P, PACK], BF16, "w2_bf11", W2_RAW[1, 0])
-        round_by_vector(w2_raw[1, 1], fourth[:])
-        nc.vector.quantize_mx(w2_w[1][:, 0].bitcast(FP8X4), w2_s[1][:, 0], third[:].rearrange("p t m j -> p (t m j)"))
-        to_tanh(0)
-        nc.vector.quantize_mx(w2_w[1][:, 1].bitcast(FP8X4), w2_s[1][:, 1], fourth[:].rearrange("p t m j -> p (t m j)"))
-
-        def reflexes(k):
-            for h in range(2):
-                reflex(k, h, by_scalar)
-
-        for k in range(1, PACK):
-            reflexes(k)
+        for k in range(2):
+            whole(reflex, k, by_vector)
+        reflex(2, 0, by_vector)
+        round_by_vector(1, 1)
+        quantize_w2(1, 0)
+        quantize_w2(1, 1)
+        reflex(2, 1, by_scalar)
+        whole(reflex, 3, by_scalar)
         weigh(0)
         weigh(1)
-        to_tanh(1)
+        to_tanh(1, nc.vector)
         weigh(2)
         weigh(3)
+        for k in (4, 5):
+            whole(reflex, k, by_scalar)
         for k in range(PACK):
             borrow(k, 0, M)
-        for k in range(PACK, 2 * PACK):
-            reflexes(k)
+        for k in (6, 7):
+            whole(reflex, k, by_scalar)
         weigh(4)
-        sum_z(0, 0, M)
         weigh(5)
-        quantize_z(0, 0, M)
+        sum_z(0, 0, M)
         weigh(6)
+        quantize_z(0, 0, M)
         weigh(7, 0, HALF)
         weigh(7, HALF, M)
         for m0, m1 in CHUNKS:

@@ -26,7 +26,7 @@ SCALE_ROWS = 32
 HALF = M // 2
 QUARTER = S // 4
 KB = 1024
-EARLY = 3
+EARLY = 4
 CHUNKS = [(0, HALF), (HALF, HALF + P), (HALF + P, M)]
 
 TABLE = (0, 20 * KB)
@@ -158,9 +158,7 @@ def tile_list_sound_change_dating_kernel(
                 w2_raw[b, a][:].rearrange("p j (m u t) -> p u m j t", u=2, t=2),
             )
 
-        w2_w = {(0, a): held([P, PASS], I32, f"w2_w0{a}") for a in range(2)}
-        for a in range(2):
-            w2_w[1, a] = reused([P, PASS], I32, f"w2_w1{a}", SIGMOIDS + (4 + 2 * a) * KB)
+        w2_w = {key: held([P, PASS], I32, f"w2_w{key[0]}{key[1]}") for key in W2_RAW}
         w2_s = {key: held([P, PASS], U8, f"w2_s{key[0]}{key[1]}") for key in W2_RAW}
 
         def quantize_w2(b, a):
@@ -270,15 +268,11 @@ def tile_list_sound_change_dating_kernel(
         for k in range(EARLY):
             features(k, 0, QUARTER, by_scalar)
         for k in range(EARLY):
-            features(k, QUARTER, BANK, by_vector if k else by_scalar)
+            features(k, QUARTER, BANK, by_vector if k in (1, 2) else by_scalar)
         for k in range(EARLY):
             feature(k, 1, by_vector if k else by_scalar)
-        feature(3, 0, by_scalar)
-        sigmoid(0)
-        sigmoid(1)
-        feature(3, 1, by_scalar)
-        sigmoid(2)
-        sigmoid(3)
+        for k in (1, 0, 2, 3):
+            sigmoid(k)
         nc.vector.tensor_copy(
             w1_w[1][:].bitcast(U16), w1_late[:].bitcast(U16).rearrange("p a (m t) -> p a t m", t=PACK)
         )
@@ -296,21 +290,21 @@ def tile_list_sound_change_dating_kernel(
         quantize_w2(0, 0)
         quantize_w2(0, 1)
         round_by_gpsimd(1, 0)
-        to_tanh(0, nc.gpsimd)
         whole(feature, 4, by_scalar)
         for k in range(5, 8):
             whole(feature, k, by_vector)
         for k in (5, 4, 6, 7):
             sigmoid(k)
-        for k in range(2):
-            whole(reflex, k, by_vector)
-        reflex(2, 0, by_vector)
-        round_by_vector(1, 1)
+        whole(reflex, 0, by_vector)
+        reflex(1, 0, by_vector)
+        reflex(1, 1, by_scalar)
+        for k in (2, 3):
+            whole(reflex, k, by_scalar)
+        to_tanh(0, nc.vector)
         quantize_w2(1, 0)
-        quantize_w2(1, 1)
-        reflex(2, 1, by_scalar)
-        whole(reflex, 3, by_scalar)
+        round_by_vector(1, 1)
         weigh(0)
+        quantize_w2(1, 1)
         weigh(1)
         to_tanh(1, nc.vector)
         weigh(2)

@@ -118,7 +118,7 @@ def tile_list_sound_change_dating_kernel(
                 picked = tab_w[a][:].bitcast(U32).indirect(idx[:, j0 // LIST : j1 // LIST])
                 nc.vector.tensor_copy(v_w[a, h][:, j0 - BANK * h : j1 - BANK * h].bitcast(U32), picked)
 
-        w1_w = [held([P, 2, PACK, 2 * P], U8, "w1_w0"), reused([P, 2, PACK, 2 * P], U8, "w1_w1", 0)]
+        w1_w = [held([P, 2, PACK, 2 * P], U8, "w1_w0"), held([P, 2, PACK, 2 * P], U8, "w1_w1")]
 
         def order_first(a, copy):
             copy(w1_w[0][:, a].bitcast(U16), w1_raw[a][:].bitcast(U16).rearrange("p (m t) -> p t m", t=PACK))
@@ -132,12 +132,11 @@ def tile_list_sound_change_dating_kernel(
         w2_raw = {key: reused([P, PACK, PASS], F32, f"w2_raw{key[0]}{key[1]}", at) for key, at in W2_RAW.items()}
         rounded = {key: reused([P, PACK, P, PACK], BF16, f"w2_bf{key[0]}{key[1]}", at) for key, at in ROUNDED.items()}
 
-        def load_w2(b, a, c0=0, c1=PASS):
-            rows = w2[PASS * a : PASS * (a + 1), PASS * b + c0 : PASS * b + c1]
-            nc.sync.dma_start(w2_raw[b, a][:, :, c0:c1], rows.rearrange("(p j) c -> p j c", j=PACK))
+        def load_w2(b, a):
+            rows = w2[PASS * a : PASS * (a + 1), PASS * b : PASS * (b + 1)]
+            nc.sync.dma_start(w2_raw[b, a][:], rows.rearrange("(p j) c -> p j c", j=PACK))
 
-        load_w2(0, 0, 0, PASS // 2)
-        load_w2(0, 0, PASS // 2, PASS)
+        load_w2(0, 0)
         w1_late = reused([P, 2, H], U8, "w1_late", W1_LATE)
         nc.sync.dma_start(w1_late[:].bitcast(I32), w1_halves[1].bitcast(I32))
         load_w2(0, 1)
@@ -264,18 +263,18 @@ def tile_list_sound_change_dating_kernel(
         def feature(k, h, copy):
             features(k, BANK * h, BANK * (h + 1), copy)
 
-        round_by_gpsimd(0, 0)
         for k in range(EARLY):
             features(k, 0, QUARTER, by_scalar)
         for k in range(EARLY):
             features(k, QUARTER, BANK, by_vector if k in (1, 2) else by_scalar)
-        for k in range(EARLY):
-            feature(k, 1, by_vector if k else by_scalar)
-        for k in (1, 0, 2, 3):
-            sigmoid(k)
+        round_by_vector(0, 0)
         nc.vector.tensor_copy(
             w1_w[1][:].bitcast(U16), w1_late[:].bitcast(U16).rearrange("p a (m t) -> p a t m", t=PACK)
         )
+        for k in range(EARLY):
+            feature(k, 1, by_vector if k >= 2 else by_scalar)
+        for k in range(EARLY):
+            sigmoid(k)
         for q in range(4):
             nc.sync.dma_start(
                 w1_late[32 * q : 32 * q + 4, :, :N].bitcast(I32),

@@ -33,10 +33,10 @@ TABLE = (0, 20 * KB)
 W2_RAW = {(0, 0): 0, (0, 1): 11 * KB, (1, 0): 20 * KB, (1, 1): 28 * KB}
 W1_LATE = 8 * KB
 W1_SECOND = 10 * KB
-ROUNDED = {(0, 0): 36 * KB, (0, 1): 40 * KB, (1, 0): 40 * KB, (1, 1): 44 * KB}
-SIGMOIDS = 44 * KB
-ANCESTORS = (20 * KB, 28 * KB)
-X1_AT = {2: 52 * KB, 4: 52 * KB, 5: 36 * KB, 6: 11 * KB, 7: 15 * KB}
+ROUNDED = {(0, 0): 36 * KB, (0, 1): 42 * KB, (1, 0): 42 * KB, (1, 1): 20 * KB}
+LOANS = 18 * KB
+ANCESTORS = (26 * KB, 34 * KB)
+X1_AT = {5: 36 * KB, 6: 11 * KB, 7: 15 * KB}
 
 
 def tile_list_sound_change_dating_kernel(
@@ -194,10 +194,10 @@ def tile_list_sound_change_dating_kernel(
             scales = [w2_s[b, a][:, cols] for a in range(2)]
             first_stage(x2[k], BANK * h, BANK * (h + 1), words, scales, copy)
 
-        sig = [reused([P, PACK, M], F32, "sig0", SIGMOIDS), held([P, PACK, M], F32, "sig1")]
+        sig = [held([P, PACK, M], F32, f"sig{b}") for b in range(2)]
         anc = [reused([P, PACK, M], F32, f"anc{b}", ANCESTORS[b]) for b in range(2)]
         weighed = [held([P, PACK, M], F32, f"weighed{b}") for b in range(2)]
-        loan = [reused([P, PACK, M], F32, "loan0", ROUNDED[1, 0]), held([P, PACK, M], F32, "loan1")]
+        loan = [reused([P, PACK, M], F32, "loan0", LOANS), held([P, PACK, M], F32, "loan1")]
 
         def sigmoid(k):
             b, t = tiles[k]
@@ -273,8 +273,10 @@ def tile_list_sound_change_dating_kernel(
         )
         for k in range(EARLY):
             feature(k, 1, by_vector if k >= 2 else by_scalar)
-        for k in range(EARLY):
+        for k in range(EARLY - 1):
             sigmoid(k)
+        whole(feature, 4, by_scalar)
+        sigmoid(3)
         for q in range(4):
             nc.sync.dma_start(
                 w1_late[32 * q : 32 * q + 4, :, :N].bitcast(I32),
@@ -289,25 +291,22 @@ def tile_list_sound_change_dating_kernel(
         quantize_w2(0, 0)
         quantize_w2(0, 1)
         round_by_gpsimd(1, 0)
-        whole(feature, 4, by_scalar)
         for k in range(5, 8):
             whole(feature, k, by_vector)
-        for k in (5, 4, 6, 7):
+        for k in range(PACK, 2 * PACK):
             sigmoid(k)
         whole(reflex, 0, by_vector)
         reflex(1, 0, by_vector)
         reflex(1, 1, by_scalar)
         for k in (2, 3):
             whole(reflex, k, by_scalar)
-        to_tanh(0, nc.vector)
-        quantize_w2(1, 0)
         round_by_vector(1, 1)
-        weigh(0)
+        quantize_w2(1, 0)
         quantize_w2(1, 1)
-        weigh(1)
+        to_tanh(0, nc.vector)
         to_tanh(1, nc.vector)
-        weigh(2)
-        weigh(3)
+        for k in range(PACK):
+            weigh(k)
         for k in (4, 5):
             whole(reflex, k, by_scalar)
         for k in range(PACK):

@@ -29,14 +29,15 @@ KB = 1024
 EARLY = 4
 CHUNKS = [(0, HALF), (HALF, HALF + P), (HALF + P, M)]
 
-TABLE = (0, 20 * KB)
-W2_RAW = {(0, 0): 0, (0, 1): 11 * KB, (1, 0): 20 * KB, (1, 1): 28 * KB}
+TABLE = (0, 22 * KB)
+W2_RAW = {(0, 0): 0, (0, 1): 13 * KB, (1, 0): 22 * KB, (1, 1): 30 * KB}
 W1_LATE = 8 * KB
 W1_SECOND = 10 * KB
-ROUNDED = {(0, 0): 36 * KB, (0, 1): 42 * KB, (1, 0): 42 * KB, (1, 1): 20 * KB}
-LOANS = 18 * KB
-ANCESTORS = (26 * KB, 34 * KB)
-X1_AT = {5: 36 * KB, 6: 11 * KB, 7: 15 * KB}
+W1_ORDERED = 11 * KB
+ROUNDED = {(0, 0): 38 * KB, (0, 1): 44 * KB, (1, 0): 44 * KB, (1, 1): 22 * KB}
+LOANS = 20 * KB
+ANCESTORS = (28 * KB, 36 * KB)
+X1_AT = {5: 38 * KB, 6: 13 * KB, 7: 17 * KB}
 
 
 def tile_list_sound_change_dating_kernel(
@@ -118,13 +119,13 @@ def tile_list_sound_change_dating_kernel(
                 picked = tab_w[a][:].bitcast(U32).indirect(idx[:, j0 // LIST : j1 // LIST])
                 nc.vector.tensor_copy(v_w[a, h][:, j0 - BANK * h : j1 - BANK * h].bitcast(U32), picked)
 
-        w1_w = [held([P, 2, PACK, 2 * P], U8, "w1_w0"), held([P, 2, PACK, 2 * P], U8, "w1_w1")]
+        w1_w = [reused([P, 2, PACK, 2 * P], U8, "w1_w0", W1_ORDERED), held([P, 2, PACK, 2 * P], U8, "w1_w1")]
 
         def order_first(a, copy):
             copy(w1_w[0][:, a].bitcast(U16), w1_raw[a][:].bitcast(U16).rearrange("p (m t) -> p t m", t=PACK))
 
-        order_first(0, nc.vector.tensor_copy)
         gather_table(0, (0, BANK, S))
+        order_first(0, nc.vector.tensor_copy)
         gather_table(1, (0, QUARTER, BANK, S))
         nc.sync.dma_start(w1_raw[1][:].bitcast(I32), w1_halves[0][:, 1, :].bitcast(I32))
         order_first(1, nc.scalar.copy)

@@ -233,25 +233,37 @@ def tile_list_sound_change_dating_kernel(
             z_s[b, m0] = held([P, m1 - m0], U8, f"z_s{b}{m0}")
             nc.vector.quantize_mx(z_w[b, m0][:].bitcast(FP8X4), z_s[b, m0][:], z_bf[b, m0][:].rearrange("p m t -> p (m t)"))
 
+        sums = {}
+
+        def score_pass(b, m0, m1):
+            shared = m0 == HALF
+            if b == 0 and shared:
+                bank = free_bank()
+                sums[m0] = [bank[:, P * c : P * (c + 1)] for c in range(N // P)]
+            elif b == 0:
+                sums[m0] = [free_bank()[:, : m1 - m0] for c in range(N // P)]
+            origin = m0 if b else 0
+            part = slice(m0 - origin, m1 - origin)
+            for c, acc in enumerate(sums[m0]):
+                cols = slice(P * c, P * (c + 1))
+                nc.tensor.matmul_mx(
+                    acc, lhsT=w3_w[:, b, cols].bitcast(FP8X4), lhsT_scale=w1_late[:, b, cols],
+                    rhs=z_w[b, origin][:, part].bitcast(FP8X4), rhs_scale=z_s[b, origin][:, part],
+                    start=b == 0 and (c == 0 or not shared), stop=b == 1 and (c == N // P - 1 or not shared),
+                )
+
         def score(m0, m1):
+            score_pass(1, m0, m1)
+            accs = sums[m0]
             y = held([P, N // P, m1 - m0], F32, f"y{m0}")
-            accs = [free_bank()[:, : m1 - m0] for c in range(N // P)]
-            for b, start in enumerate((0, m0)):
-                part = slice(m0 - start, m1 - start)
-                for c, acc in enumerate(accs):
-                    cols = slice(P * c, P * (c + 1))
-                    nc.tensor.matmul_mx(
-                        acc, lhsT=w3_w[:, b, cols].bitcast(FP8X4), lhsT_scale=w1_late[:, b, cols],
-                        rhs=z_w[b, start][:, part].bitcast(FP8X4), rhs_scale=z_s[b, start][:, part],
-                        start=b == 0, stop=b == 1,
-                    )
             for c, acc in enumerate(accs):
-                if c == 1 and m1 == M:
+                if m0 == HALF or (c == 1 and m1 == M):
                     nc.vector.tensor_scalar(y[:, c, :], acc, prior[:, c : c + 1], None, ALU.add)
                 else:
                     nc.scalar.activation(y[:, c, :], acc, ACT.Identity, bias=prior[:, c : c + 1])
                 if m0 != HALF:
-                    nc.sync.dma_start(out[P * c : P * (c + 1), m0:m1], y[:, c, :])
+                    queue = nc.scalar if c == 2 and m1 == M else nc.sync
+                    queue.dma_start(out[P * c : P * (c + 1), m0:m1], y[:, c, :])
             if m0 == HALF:
                 nc.sync.dma_start(out.rearrange("(c p) m -> p c m", p=P)[:, :, m0:m1], y[:])
 
@@ -314,20 +326,22 @@ def tile_list_sound_change_dating_kernel(
             borrow(k, 0, M)
         for k in (6, 7):
             whole(reflex, k, by_scalar)
-        weigh(4)
-        weigh(5)
-        sum_z(0, 0, M)
-        weigh(6)
-        quantize_z(0, 0, M)
-        weigh(7, 0, HALF)
-        weigh(7, HALF, M)
         for m0, m1 in CHUNKS:
             for k in range(PACK, 2 * PACK):
                 borrow(k, m0, m1)
         wide, middle, last = CHUNKS
+        weigh(4)
+        weigh(5)
+        sum_z(0, 0, M)
+        weigh(6)
+        weigh(7, 0, HALF)
+        quantize_z(0, 0, M)
+        for m0, m1 in CHUNKS:
+            score_pass(0, m0, m1)
         sum_z(1, *wide)
-        sum_z(1, *middle)
+        weigh(7, HALF, M)
         quantize_z(1, *wide)
+        sum_z(1, *middle)
         sum_z(1, *last)
         quantize_z(1, *middle)
         quantize_z(1, *last)

@@ -125,7 +125,7 @@ def tile_list_sound_change_dating_kernel(
             copy(w1_w[0][:, a].bitcast(U16), w1_raw[a][:].bitcast(U16).rearrange("p (m t) -> p t m", t=PACK))
 
         gather_table(0, (0, BANK, S))
-        order_first(0, nc.vector.tensor_copy)
+        order_first(0, nc.scalar.copy)
         gather_table(1, (0, QUARTER, BANK, S))
         nc.sync.dma_start(w1_raw[1][:].bitcast(I32), w1_halves[0][:, 1, :].bitcast(I32))
         order_first(1, nc.scalar.copy)
@@ -300,11 +300,13 @@ def tile_list_sound_change_dating_kernel(
         prior = reused([P, N // P], F32, "prior", 5 * KB)
         with nc.allow_non_contiguous_dma(reason="one value of period to a partition"):
             nc.sync.dma_start(prior[:], period.rearrange("(c p) -> p c", p=P))
-        round_by_vector(0, 1)
         quantize_w2(0, 0)
+        round_by_vector(0, 1)
+        feature(5, 0, by_vector)
         quantize_w2(0, 1)
         round_by_gpsimd(1, 0)
-        for k in range(5, 8):
+        feature(5, 1, by_vector)
+        for k in (6, 7):
             whole(feature, k, by_vector)
         for k in range(PACK, 2 * PACK):
             sigmoid(k)

@@ -284,10 +284,12 @@ def tile_list_sound_change_dating_kernel(
         nc.vector.tensor_copy(
             w1_w[1][:].bitcast(U16), w1_late[:].bitcast(U16).rearrange("p a (m t) -> p a t m", t=PACK)
         )
-        for k in range(EARLY):
-            feature(k, 1, by_vector if k >= 2 else by_scalar)
         for k in range(EARLY - 1):
-            sigmoid(k)
+            feature(k, 1, by_vector if k == 2 else by_scalar)
+        sigmoid(0)
+        sigmoid(1)
+        feature(3, 1, by_scalar)
+        sigmoid(2)
         whole(feature, 4, by_scalar)
         sigmoid(3)
         for q in range(4):

@@ -34,8 +34,8 @@ W2_RAW = {(0, 0): 0, (0, 1): 13 * KB, (1, 0): 22 * KB, (1, 1): 30 * KB}
 W1_LATE = 8 * KB
 W1_SECOND = 10 * KB
 W1_ORDERED = 11 * KB
-ROUNDED = {(0, 0): 38 * KB, (0, 1): 44 * KB, (1, 0): 44 * KB, (1, 1): 22 * KB}
-LOANS = 20 * KB
+ROUNDED = {(0, 0): 38 * KB, (0, 1): 44 * KB, (1, 0): 44 * KB, (1, 1): 48 * KB}
+LOANS = 46 * KB
 ANCESTORS = (28 * KB, 36 * KB)
 X1_AT = {5: 38 * KB, 6: 13 * KB, 7: 17 * KB}
 
@@ -144,18 +144,19 @@ def tile_list_sound_change_dating_kernel(
         load_w2(1, 0)
         load_w2(1, 1)
 
-        def round_by_gpsimd(b, a):
-            for ms in (slice(0, P // 2), slice(P // 2, P)):
-                nc.gpsimd.tensor_scalar(
-                    rounded[b, a][:, :, ms].rearrange("p t m j -> p m t j"),
-                    w2_raw[b, a][:].rearrange("p j (m t) -> p m t j", t=PACK)[:, ms],
-                    1.0, 0.0, ALU.mult, ALU.add,
-                )
+        low, high = slice(0, P // 2), slice(P // 2, P)
 
-        def round_by_vector(b, a):
+        def round_by_gpsimd(b, a, ms):
+            nc.gpsimd.tensor_scalar(
+                rounded[b, a][:, :, ms].rearrange("p t m j -> p m t j"),
+                w2_raw[b, a][:].rearrange("p j (m t) -> p m t j", t=PACK)[:, ms],
+                1.0, 0.0, ALU.mult, ALU.add,
+            )
+
+        def round_by_vector(b, a, ms=slice(0, P)):
             nc.vector.tensor_copy(
-                rounded[b, a][:].rearrange("p (u t) m j -> p u m j t", u=2),
-                w2_raw[b, a][:].rearrange("p j (m u t) -> p u m j t", u=2, t=2),
+                rounded[b, a][:].rearrange("p (u t) m j -> p u m j t", u=2)[:, :, ms],
+                w2_raw[b, a][:].rearrange("p j (m u t) -> p u m j t", u=2, t=2)[:, :, ms],
             )
 
         w2_w = {key: held([P, PASS], I32, f"w2_w{key[0]}{key[1]}") for key in W2_RAW}
@@ -306,18 +307,19 @@ def tile_list_sound_change_dating_kernel(
         round_by_vector(0, 1)
         feature(5, 0, by_vector)
         quantize_w2(0, 1)
-        round_by_gpsimd(1, 0)
+        round_by_gpsimd(1, 0, low)
+        round_by_gpsimd(1, 0, high)
+        round_by_gpsimd(1, 1, low)
         feature(5, 1, by_vector)
         for k in (6, 7):
             whole(feature, k, by_vector)
         for k in range(PACK, 2 * PACK):
             sigmoid(k)
-        whole(reflex, 0, by_vector)
-        reflex(1, 0, by_vector)
-        reflex(1, 1, by_scalar)
+        for k in (0, 1):
+            whole(reflex, k, by_vector)
         for k in (2, 3):
             whole(reflex, k, by_scalar)
-        round_by_vector(1, 1)
+        round_by_vector(1, 1, high)
         quantize_w2(1, 0)
         quantize_w2(1, 1)
         to_tanh(0, nc.vector)

@@ -87,8 +87,6 @@ def tile_list_sound_change_dating_kernel(
         nc.sync.dma_start(w1_raw[0][:].bitcast(I32), w1_halves[0][:, 0, :].bitcast(I32))
         nc.sync.dma_start(w1_s_raw[:SCALE_ROWS, :].bitcast(I32), w1_scales.rearrange("a q c -> (a q) c").bitcast(I32))
         nc.sync.dma_start(p1[:], pos1)
-        nc.sync.dma_start(p2[:], pos2)
-        nc.sync.dma_start(p3[:], pos3)
         nc.sync.dma_start(tab_w[0][:], tab_words[0].rearrange("p t i -> p (t i)").bitcast(I32))
         for cols in (slice(0, T // 2), slice(T // 2, T)):
             nc.sync.dma_start(tab_w[1][:, cols], tab_words[1].rearrange("p t i -> p (t i)").bitcast(I32)[:, cols])
@@ -143,6 +141,8 @@ def tile_list_sound_change_dating_kernel(
         load_w2(0, 1)
         load_w2(1, 0)
         load_w2(1, 1)
+        nc.sync.dma_start(p2[:], pos2)
+        nc.sync.dma_start(p3[:], pos3)
 
         low, high = slice(0, P // 2), slice(P // 2, P)
 

@@ -35,8 +35,9 @@ W1_LATE = 8 * KB
 W1_SECOND = 10 * KB
 W1_ORDERED = 11 * KB
 ROUNDED = {(0, 0): 38 * KB, (0, 1): 44 * KB, (1, 0): 44 * KB, (1, 1): 48 * KB}
-LOANS = 46 * KB
-ANCESTORS = (28 * KB, 36 * KB)
+WEIGHED = 44 * KB
+WIDE_Z = 48 * KB
+WIDE_AT = {4: 22 * KB, 5: 30 * KB}
 X1_AT = {5: 38 * KB, 6: 13 * KB, 7: 17 * KB}
 
 
@@ -144,19 +145,17 @@ def tile_list_sound_change_dating_kernel(
         nc.sync.dma_start(p2[:], pos2)
         nc.sync.dma_start(p3[:], pos3)
 
-        low, high = slice(0, P // 2), slice(P // 2, P)
-
-        def round_by_gpsimd(b, a, ms):
+        def round_by_gpsimd(b, a):
             nc.gpsimd.tensor_scalar(
-                rounded[b, a][:, :, ms].rearrange("p t m j -> p m t j"),
-                w2_raw[b, a][:].rearrange("p j (m t) -> p m t j", t=PACK)[:, ms],
+                rounded[b, a][:].rearrange("p t m j -> p m t j"),
+                w2_raw[b, a][:].rearrange("p j (m t) -> p m t j", t=PACK),
                 1.0, 0.0, ALU.mult, ALU.add,
             )
 
-        def round_by_vector(b, a, ms=slice(0, P)):
+        def round_by_vector(b, a):
             nc.vector.tensor_copy(
-                rounded[b, a][:].rearrange("p (u t) m j -> p u m j t", u=2)[:, :, ms],
-                w2_raw[b, a][:].rearrange("p j (m u t) -> p u m j t", u=2, t=2)[:, :, ms],
+                rounded[b, a][:].rearrange("p (u t) m j -> p u m j t", u=2),
+                w2_raw[b, a][:].rearrange("p j (m u t) -> p u m j t", u=2, t=2),
             )
 
         w2_w = {key: held([P, PASS], I32, f"w2_w{key[0]}{key[1]}") for key in W2_RAW}
@@ -181,7 +180,9 @@ def tile_list_sound_change_dating_kernel(
             copy(x[:, j0:j1], acc)
 
         x1 = [reused([P, S], F32, f"x1_{k}", X1_AT[k]) if k in X1_AT else held([P, S], F32, f"x1_{k}") for k in range(8)]
-        x2 = [held([P, S], F32, f"x2_{k}") for k in range(8)]
+        wide_x2 = {k: reused([P, 2 * S], F32, f"x2_{k}", at) for k, at in WIDE_AT.items()}
+        wide_x2.update({k: held([P, 2 * S], F32, f"x2_{k}") for k in (6, 7)})
+        x2 = [wide_x2[k] if k in wide_x2 else held([P, S], F32, f"x2_{k}") for k in range(8)]
 
         def features(k, j0, j1, copy):
             b, t = tiles[k]
@@ -196,22 +197,34 @@ def tile_list_sound_change_dating_kernel(
             scales = [w2_s[b, a][:, cols] for a in range(2)]
             first_stage(x2[k], BANK * h, BANK * (h + 1), words, scales, copy)
 
-        sig = [held([P, PACK, M], F32, f"sig{b}") for b in range(2)]
-        anc = [reused([P, PACK, M], F32, f"anc{b}", ANCESTORS[b]) for b in range(2)]
-        weighed = [held([P, PACK, M], F32, f"weighed{b}") for b in range(2)]
-        loan = [reused([P, PACK, M], F32, "loan0", LOANS), held([P, PACK, M], F32, "loan1")]
+        sig_pairs = [wide_x2[k][:, S:] for k in (6, 7)]
+        anc_pairs = [wide_x2[k][:, S:] for k in WIDE_AT]
+        sig1 = held([P, PACK, M], F32, "sig1")
+        twice = held([P, PACK, M], F32, "twice")
+        weighed0 = reused([P, PACK, M], F32, "weighed0", WEIGHED)
+        weighed1 = {0: held([P, PACK, HALF], F32, "weighed10"), HALF: reused([P, PACK, HALF], F32, "weighed11", WEIGHED)}
+        loan = [held([P, PACK, M], F32, f"loan{b}") for b in range(2)]
+
+        def in_pair(pairs, t):
+            return pairs[t // 2][:, M * (t % 2) : M * (t % 2 + 1)]
 
         def sigmoid(k):
             b, t = tiles[k]
-            nc.scalar.activation(sig[b][:, t, :], x1[k][:].indirect(p1[:]), ACT.Sigmoid, scale=2.0)
+            nc.scalar.activation(sig1[:, t, :] if b else in_pair(sig_pairs, t), x1[k][:].indirect(p1[:]), ACT.Sigmoid, scale=2.0)
 
-        def to_tanh(b, engine):
-            engine.tensor_scalar(anc[b][:], sig[b][:], 2.0, -1.0, ALU.mult, ALU.add)
+        def to_tanh(u):
+            nc.vector.tensor_scalar(anc_pairs[u], sig_pairs[u], 2.0, -1.0, ALU.mult, ALU.add)
 
-        def weigh(k, m0=0, m1=M):
-            b, t = tiles[k]
-            picked = x2[k][:].indirect(p2[:, m0 // LIST : m1 // LIST])
-            nc.vector.tensor_tensor(weighed[b][:, t, m0:m1], picked, anc[b][:, t, m0:m1], ALU.mult)
+        def weigh(k):
+            nc.vector.tensor_tensor(weighed0[:, k, :], x2[k][:].indirect(p2[:]), in_pair(anc_pairs, k), ALU.mult)
+
+        def daughter(k):
+            nc.vector.tensor_scalar(twice[:, k - PACK, :], x2[k][:].indirect(p2[:]), 2.0, 0.0, ALU.mult, ALU.add)
+
+        def weigh_late(m0, m1):
+            nc.vector.scalar_tensor_tensor(
+                weighed1[m0][:], sig1[:, :, m0:m1], -0.5, twice[:, :, m0:m1], ALU.add, ALU.mult
+            )
 
         def borrow(k, m0, m1):
             b, t = tiles[k]
@@ -221,12 +234,20 @@ def tile_list_sound_change_dating_kernel(
         z_bf, z_w, z_s = {}, {}, {}
 
         def sum_z(b, m0, m1):
-            z_bf[b, m0] = held([P, m1 - m0, PACK], BF16, f"z_bf{b}{m0}")
+            name, origin = f"z_bf{b}{m0}", m0 // HALF * HALF
+            shape = [P, m1 - m0, PACK]
+            z_bf[b, m0] = held(shape, BF16, name) if m0 else reused(shape, BF16, name, WIDE_Z)
             nc.vector.tensor_tensor(
                 z_bf[b, m0][:].rearrange("p (c i) t -> p c t i", i=2),
-                weighed[b][:, :, m0:m1].rearrange("p t (c i) -> p c t i", i=2),
+                weighed1[origin][:, :, m0 - origin : m1 - origin].rearrange("p t (c i) -> p c t i", i=2),
                 loan[b][:, :, m0:m1].rearrange("p t (c i) -> p c t i", i=2),
                 ALU.add,
+            )
+
+        def sum_z_by_gpsimd():
+            z_bf[0, 0] = held([P, M, PACK], BF16, "z_bf00")
+            nc.gpsimd.tensor_tensor(
+                z_bf[0, 0][:], weighed0[:].rearrange("p t m -> p m t"), loan[0][:].rearrange("p t m -> p m t"), ALU.add
             )
 
         def quantize_z(b, m0, m1):
@@ -307,45 +328,40 @@ def tile_list_sound_change_dating_kernel(
         round_by_vector(0, 1)
         feature(5, 0, by_vector)
         quantize_w2(0, 1)
-        round_by_gpsimd(1, 0, low)
-        round_by_gpsimd(1, 0, high)
-        round_by_gpsimd(1, 1, low)
+        round_by_gpsimd(1, 0)
+        round_by_gpsimd(1, 1)
         feature(5, 1, by_vector)
         for k in (6, 7):
             whole(feature, k, by_vector)
         for k in range(PACK, 2 * PACK):
             sigmoid(k)
-        for k in (0, 1):
+        for k in (0, 1, 2):
             whole(reflex, k, by_vector)
-        for k in (2, 3):
-            whole(reflex, k, by_scalar)
-        round_by_vector(1, 1, high)
+        reflex(3, 0, by_vector)
+        reflex(3, 1, by_scalar)
         quantize_w2(1, 0)
         quantize_w2(1, 1)
-        to_tanh(0, nc.vector)
-        to_tanh(1, nc.vector)
+        to_tanh(0)
+        to_tanh(1)
         for k in range(PACK):
             weigh(k)
-        for k in (4, 5):
-            whole(reflex, k, by_scalar)
         for k in range(PACK):
             borrow(k, 0, M)
-        for k in (6, 7):
+        sum_z_by_gpsimd()
+        for k in range(PACK, 2 * PACK):
             whole(reflex, k, by_scalar)
+        for k in range(PACK, 2 * PACK):
+            daughter(k)
         for m0, m1 in CHUNKS:
             for k in range(PACK, 2 * PACK):
                 borrow(k, m0, m1)
         wide, middle, last = CHUNKS
-        weigh(4)
-        weigh(5)
-        sum_z(0, 0, M)
-        weigh(6)
-        weigh(7, 0, HALF)
+        weigh_late(0, HALF)
         quantize_z(0, 0, M)
         for m0, m1 in CHUNKS:
             score_pass(0, m0, m1)
         sum_z(1, *wide)
-        weigh(7, HALF, M)
+        weigh_late(HALF, M)
         quantize_z(1, *wide)
         sum_z(1, *middle)
         sum_z(1, *last)

@@ -247,7 +247,10 @@ def tile_list_sound_change_dating_kernel(
         def sum_z_by_gpsimd():
             z_bf[0, 0] = held([P, M, PACK], BF16, "z_bf00")
             nc.gpsimd.tensor_tensor(
-                z_bf[0, 0][:], weighed0[:].rearrange("p t m -> p m t"), loan[0][:].rearrange("p t m -> p m t"), ALU.add
+                z_bf[0, 0][:].rearrange("p (c i) t -> p c t i", i=2),
+                weighed0[:].rearrange("p t (c i) -> p c t i", i=2),
+                loan[0][:].rearrange("p t (c i) -> p c t i", i=2),
+                ALU.add,
             )
 
         def quantize_z(b, m0, m1):

@@ -36,9 +36,11 @@ W1_SECOND = 10 * KB
 W1_ORDERED = 11 * KB
 ROUNDED = {(0, 0): 38 * KB, (0, 1): 44 * KB, (1, 0): 44 * KB, (1, 1): 48 * KB}
 WEIGHED = 44 * KB
-WIDE_Z = 48 * KB
+LAST_CODES = 52 * KB
+GPSIMD_SHARE = 64
 WIDE_AT = {4: 22 * KB, 5: 30 * KB}
-X1_AT = {5: 38 * KB, 6: 13 * KB, 7: 17 * KB}
+LATE_LOANS = 60 * KB
+X1_AT = {4: LATE_LOANS, 5: 38 * KB, 6: 13 * KB, 7: 17 * KB}
 
 
 def tile_list_sound_change_dating_kernel(
@@ -145,20 +147,21 @@ def tile_list_sound_change_dating_kernel(
         nc.sync.dma_start(p2[:], pos2)
         nc.sync.dma_start(p3[:], pos3)
 
-        def round_by_gpsimd(b, a):
+        def round_by_gpsimd(b, a, ms=slice(0, P)):
             nc.gpsimd.tensor_scalar(
-                rounded[b, a][:].rearrange("p t m j -> p m t j"),
-                w2_raw[b, a][:].rearrange("p j (m t) -> p m t j", t=PACK),
+                rounded[b, a][:, :, ms].rearrange("p t m j -> p m t j"),
+                w2_raw[b, a][:].rearrange("p j (m t) -> p m t j", t=PACK)[:, ms],
                 1.0, 0.0, ALU.mult, ALU.add,
             )
 
-        def round_by_vector(b, a):
+        def round_by_vector(b, a, ms=slice(0, P)):
             nc.vector.tensor_copy(
-                rounded[b, a][:].rearrange("p (u t) m j -> p u m j t", u=2),
-                w2_raw[b, a][:].rearrange("p j (m u t) -> p u m j t", u=2, t=2),
+                rounded[b, a][:].rearrange("p (u t) m j -> p u m j t", u=2)[:, :, ms],
+                w2_raw[b, a][:].rearrange("p j (m u t) -> p u m j t", u=2, t=2)[:, :, ms],
             )
 
-        w2_w = {key: held([P, PASS], I32, f"w2_w{key[0]}{key[1]}") for key in W2_RAW}
+        w2_w = {key: held([P, PASS], I32, f"w2_w{key[0]}{key[1]}") for key in W2_RAW if key != (1, 1)}
+        w2_w[1, 1] = reused([P, PASS], I32, "w2_w11", LAST_CODES)
         w2_s = {key: held([P, PASS], U8, f"w2_s{key[0]}{key[1]}") for key in W2_RAW}
 
         def quantize_w2(b, a):
@@ -199,18 +202,18 @@ def tile_list_sound_change_dating_kernel(
 
         sig_pairs = [wide_x2[k][:, S:] for k in (6, 7)]
         anc_pairs = [wide_x2[k][:, S:] for k in WIDE_AT]
-        sig1 = held([P, PACK, M], F32, "sig1")
+        sig1 = [reused([P, 2, M], F32, "sig10", LAST_CODES), held([P, 2, M], F32, "sig11")]
         twice = held([P, PACK, M], F32, "twice")
         weighed0 = reused([P, PACK, M], F32, "weighed0", WEIGHED)
-        weighed1 = {0: held([P, PACK, HALF], F32, "weighed10"), HALF: reused([P, PACK, HALF], F32, "weighed11", WEIGHED)}
-        loan = [held([P, PACK, M], F32, f"loan{b}") for b in range(2)]
+        weighed1 = held([P, PACK, M], F32, "weighed1")
+        loan = [held([P, PACK, M], F32, "loan0"), reused([P, PACK, M], F32, "loan1", LATE_LOANS)]
 
         def in_pair(pairs, t):
             return pairs[t // 2][:, M * (t % 2) : M * (t % 2 + 1)]
 
         def sigmoid(k):
             b, t = tiles[k]
-            nc.scalar.activation(sig1[:, t, :] if b else in_pair(sig_pairs, t), x1[k][:].indirect(p1[:]), ACT.Sigmoid, scale=2.0)
+            nc.scalar.activation(sig1[t // 2][:, t % 2, :] if b else in_pair(sig_pairs, t), x1[k][:].indirect(p1[:]), ACT.Sigmoid, scale=2.0)
 
         def to_tanh(u):
             nc.vector.tensor_scalar(anc_pairs[u], sig_pairs[u], 2.0, -1.0, ALU.mult, ALU.add)
@@ -221,10 +224,9 @@ def tile_list_sound_change_dating_kernel(
         def daughter(k):
             nc.vector.tensor_scalar(twice[:, k - PACK, :], x2[k][:].indirect(p2[:]), 2.0, 0.0, ALU.mult, ALU.add)
 
-        def weigh_late(m0, m1):
-            nc.vector.scalar_tensor_tensor(
-                weighed1[m0][:], sig1[:, :, m0:m1], -0.5, twice[:, :, m0:m1], ALU.add, ALU.mult
-            )
+        def weigh_late(u):
+            pair = slice(2 * u, 2 * u + 2)
+            nc.vector.scalar_tensor_tensor(weighed1[:, pair], sig1[u][:], -0.5, twice[:, pair], ALU.add, ALU.mult)
 
         def borrow(k, m0, m1):
             b, t = tiles[k]
@@ -234,12 +236,10 @@ def tile_list_sound_change_dating_kernel(
         z_bf, z_w, z_s = {}, {}, {}
 
         def sum_z(b, m0, m1):
-            name, origin = f"z_bf{b}{m0}", m0 // HALF * HALF
-            shape = [P, m1 - m0, PACK]
-            z_bf[b, m0] = held(shape, BF16, name) if m0 else reused(shape, BF16, name, WIDE_Z)
+            z_bf[b, m0] = reused([P, m1 - m0, PACK], BF16, f"z_bf{b}{m0}", WEIGHED + 2 * PACK * m0)
             nc.vector.tensor_tensor(
                 z_bf[b, m0][:].rearrange("p (c i) t -> p c t i", i=2),
-                weighed1[origin][:, :, m0 - origin : m1 - origin].rearrange("p t (c i) -> p c t i", i=2),
+                weighed1[:, :, m0:m1].rearrange("p t (c i) -> p c t i", i=2),
                 loan[b][:, :, m0:m1].rearrange("p t (c i) -> p c t i", i=2),
                 ALU.add,
             )
@@ -332,16 +332,17 @@ def tile_list_sound_change_dating_kernel(
         feature(5, 0, by_vector)
         quantize_w2(0, 1)
         round_by_gpsimd(1, 0)
-        round_by_gpsimd(1, 1)
+        round_by_gpsimd(1, 1, slice(0, GPSIMD_SHARE))
         feature(5, 1, by_vector)
         for k in (6, 7):
             whole(feature, k, by_vector)
-        for k in range(PACK, 2 * PACK):
-            sigmoid(k)
-        for k in (0, 1, 2):
+        sigmoid(6)
+        sigmoid(7)
+        for k in (0, 1):
             whole(reflex, k, by_vector)
-        reflex(3, 0, by_vector)
-        reflex(3, 1, by_scalar)
+        for k in (2, 3):
+            whole(reflex, k, by_scalar)
+        round_by_vector(1, 1, slice(GPSIMD_SHARE, P))
         quantize_w2(1, 0)
         quantize_w2(1, 1)
         to_tanh(0)
@@ -352,21 +353,24 @@ def tile_list_sound_change_dating_kernel(
             borrow(k, 0, M)
         sum_z_by_gpsimd()
         for k in range(PACK, 2 * PACK):
-            whole(reflex, k, by_scalar)
+            reflex(k, 0, by_vector if k == PACK else by_scalar)
+            reflex(k, 1, by_scalar)
+        sigmoid(4)
+        sigmoid(5)
         for k in range(PACK, 2 * PACK):
             daughter(k)
         for m0, m1 in CHUNKS:
             for k in range(PACK, 2 * PACK):
                 borrow(k, m0, m1)
         wide, middle, last = CHUNKS
-        weigh_late(0, HALF)
+        weigh_late(1)
+        weigh_late(0)
         quantize_z(0, 0, M)
         for m0, m1 in CHUNKS:
             score_pass(0, m0, m1)
         sum_z(1, *wide)
-        weigh_late(HALF, M)
-        quantize_z(1, *wide)
         sum_z(1, *middle)
+        quantize_z(1, *wide)
         sum_z(1, *last)
         quantize_z(1, *middle)
         quantize_z(1, *last)

@@ -247,9 +247,9 @@ def tile_list_sound_change_dating_kernel(
         def sum_z_by_gpsimd():
             z_bf[0, 0] = held([P, M, PACK], BF16, "z_bf00")
             nc.gpsimd.tensor_tensor(
-                z_bf[0, 0][:].rearrange("p (c i) t -> p c t i", i=2),
-                weighed0[:].rearrange("p t (c i) -> p c t i", i=2),
-                loan[0][:].rearrange("p t (c i) -> p c t i", i=2),
+                z_bf[0, 0][:].rearrange("p (c i) t -> p c t i", i=4),
+                weighed0[:].rearrange("p t (c i) -> p c t i", i=4),
+                loan[0][:].rearrange("p t (c i) -> p c t i", i=4),
                 ALU.add,
             )
 

@@ -35,6 +35,7 @@ W1_LATE = 8 * KB
 W1_SECOND = 10 * KB
 W1_ORDERED = 11 * KB
 ROUNDED = {(0, 0): 38 * KB, (0, 1): 44 * KB, (1, 0): 44 * KB, (1, 1): 48 * KB}
+LOAN_CUTS = {4: (0, HALF + P, M), 5: (0, HALF + P, M), 6: (0, HALF, HALF + P, M), 7: (0, HALF, HALF + P, M)}
 WEIGHED = 44 * KB
 LAST_CODES = 52 * KB
 GPSIMD_SHARE = 64
@@ -265,6 +266,7 @@ def tile_list_sound_change_dating_kernel(
             if b == 0 and shared:
                 bank = free_bank()
                 sums[m0] = [bank[:, P * c : P * (c + 1)] for c in range(N // P)]
+                sums["shared"] = bank[:, :N].rearrange("p (c m) -> p c m", m=P)
             elif b == 0:
                 sums[m0] = [free_bank()[:, : m1 - m0] for c in range(N // P)]
             origin = m0 if b else 0
@@ -281,16 +283,17 @@ def tile_list_sound_change_dating_kernel(
             score_pass(1, m0, m1)
             accs = sums[m0]
             y = held([P, N // P, m1 - m0], F32, f"y{m0}")
+            if m0 == HALF:
+                nc.vector.tensor_tensor(y[:], sums["shared"], prior[:].unsqueeze(2).to_broadcast([P, N // P, P]), ALU.add)
+                nc.sync.dma_start(out.rearrange("(c p) m -> p c m", p=P)[:, :, m0:m1], y[:])
+                return
             for c, acc in enumerate(accs):
-                if m0 == HALF or (c == 1 and m1 == M):
+                if c == 1 and m1 == M:
                     nc.vector.tensor_scalar(y[:, c, :], acc, prior[:, c : c + 1], None, ALU.add)
                 else:
                     nc.scalar.activation(y[:, c, :], acc, ACT.Identity, bias=prior[:, c : c + 1])
-                if m0 != HALF:
-                    queue = nc.scalar if c == 2 and m1 == M else nc.sync
-                    queue.dma_start(out[P * c : P * (c + 1), m0:m1], y[:, c, :])
-            if m0 == HALF:
-                nc.sync.dma_start(out.rearrange("(c p) m -> p c m", p=P)[:, :, m0:m1], y[:])
+                queue = nc.scalar if c == 2 and m1 == M else nc.sync
+                queue.dma_start(out[P * c : P * (c + 1), m0:m1], y[:, c, :])
 
         by_scalar, by_vector = nc.scalar.copy, nc.vector.tensor_copy
 
@@ -304,7 +307,7 @@ def tile_list_sound_change_dating_kernel(
         for k in range(EARLY):
             features(k, 0, QUARTER, by_scalar)
         for k in range(EARLY):
-            features(k, QUARTER, BANK, by_vector if k in (1, 2) else by_scalar)
+            features(k, QUARTER, BANK, by_vector if k == 2 else by_scalar)
         round_by_vector(0, 0)
         nc.vector.tensor_copy(
             w1_w[1][:].bitcast(U16), w1_late[:].bitcast(U16).rearrange("p a (m t) -> p a t m", t=PACK)
@@ -353,15 +356,17 @@ def tile_list_sound_change_dating_kernel(
             borrow(k, 0, M)
         sum_z_by_gpsimd()
         for k in range(PACK, 2 * PACK):
-            reflex(k, 0, by_vector if k == PACK else by_scalar)
+            reflex(k, 0, by_vector if k == PACK + 1 else by_scalar)
             reflex(k, 1, by_scalar)
         sigmoid(4)
         sigmoid(5)
         for k in range(PACK, 2 * PACK):
             daughter(k)
-        for m0, m1 in CHUNKS:
-            for k in range(PACK, 2 * PACK):
-                borrow(k, m0, m1)
+        for start in (0, HALF, HALF + P):
+            for k, cuts in LOAN_CUTS.items():
+                for m0, m1 in zip(cuts, cuts[1:]):
+                    if m0 == start:
+                        borrow(k, m0, m1)
         wide, middle, last = CHUNKS
         weigh_late(1)
         weigh_late(0)

@@ -157,8 +157,8 @@ def tile_list_sound_change_dating_kernel(
 
         def round_by_vector(b, a, ms=slice(0, P)):
             nc.vector.tensor_copy(
-                rounded[b, a][:].rearrange("p (u t) m j -> p u m j t", u=2)[:, :, ms],
-                w2_raw[b, a][:].rearrange("p j (m u t) -> p u m j t", u=2, t=2)[:, :, ms],
+                rounded[b, a][:, :, ms].rearrange("p t m j -> p m j t"),
+                w2_raw[b, a][:].rearrange("p j (m t) -> p m j t", t=PACK)[:, ms],
             )
 
         w2_w = {key: held([P, PASS], I32, f"w2_w{key[0]}{key[1]}") for key in W2_RAW if key != (1, 1)}
@@ -239,9 +239,9 @@ def tile_list_sound_change_dating_kernel(
         def sum_z(b, m0, m1):
             z_bf[b, m0] = reused([P, m1 - m0, PACK], BF16, f"z_bf{b}{m0}", WEIGHED + 2 * PACK * m0)
             nc.vector.tensor_tensor(
-                z_bf[b, m0][:].rearrange("p (c i) t -> p c t i", i=2),
-                weighed1[:, :, m0:m1].rearrange("p t (c i) -> p c t i", i=2),
-                loan[b][:, :, m0:m1].rearrange("p t (c i) -> p c t i", i=2),
+                z_bf[b, m0][:].rearrange("p (c i) t -> p c t i", i=4),
+                weighed1[:, :, m0:m1].rearrange("p t (c i) -> p c t i", i=4),
+                loan[b][:, :, m0:m1].rearrange("p t (c i) -> p c t i", i=4),
                 ALU.add,
             )
 

from contextlib import ExitStack

import concourse.mybir as mybir

K, H, N, T, S, M = 1024, 1024, 384, 4096, 1024, 512
FLOPS = 2 * (2 * K * H * S + H * N * M)

F32 = mybir.dt.float32
BF16 = mybir.dt.bfloat16
I32 = mybir.dt.int32
U32 = mybir.dt.uint32
U16 = mybir.dt.uint16
U8 = mybir.dt.uint8
FP8X4 = mybir.dt.float8_e4m3fn_x4
FP4X4 = mybir.dt.float4_e2m1fn_x4
ACT = mybir.ActivationFunctionType
ALU = mybir.AluOpType

P = 128
PACK = 4
PASS = P * PACK
BANK = 512
BANKS = 8
LIST = 16
SCALE_ROWS = 32
HALF = M // 2
QUARTER = S // 4
KB = 1024
EARLY = 4
CHUNKS = [(0, HALF), (HALF, HALF + P), (HALF + P, M)]

TABLE = (0, 22 * KB)
W2_RAW = {(0, 0): 0, (0, 1): 13 * KB, (1, 0): 22 * KB, (1, 1): 30 * KB}
W1_LATE = 8 * KB
W1_SECOND = 10 * KB
W1_ORDERED = 11 * KB
ROUNDED = {(0, 0): 38 * KB, (0, 1): 44 * KB, (1, 0): 44 * KB, (1, 1): 48 * KB}
LOAN_CUTS = {4: (0, HALF + P, M), 5: (0, HALF + P, M), 6: (0, HALF, HALF + P, M), 7: (0, HALF, HALF + P, M)}
WEIGHED = 44 * KB
LAST_CODES = 52 * KB
GPSIMD_SHARE = 64
WIDE_AT = {4: 22 * KB, 5: 30 * KB}
LATE_LOANS = 60 * KB
X1_AT = {4: LATE_LOANS, 5: 38 * KB, 6: 13 * KB, 7: 17 * KB}


def tile_list_sound_change_dating_kernel(
    tc, tab_words, tab_scales, offs, pos1, pos2, pos3, w1_words, w1_scales, w2, w3_words, w3_scales, period, out
):
    nc = tc.nc
    with ExitStack() as ctx:
        keep = ctx.enter_context(tc.tile_pool(name="keep", bufs=1))
        reuse = ctx.enter_context(tc.tile_pool(name="reuse", bufs=1))
        psum = ctx.enter_context(tc.psum_pool(name="psum", bufs=1))

        def held(shape, dtype, name):
            return keep.tile(shape, dtype, name=name, align_bytes=64)

        def reused(shape, dtype, name, offset):
            return reuse.tile(shape, dtype, name=name, offset=offset, align_bytes=64)

        filled = []

        def free_bank():
            filled.append(psum.tile([P, BANK], F32, name=f"bank{len(filled) % BANKS}"))
            return filled[-1]

        idx = keep.tile([P, S // LIST], U16, name="idx")
        p1 = keep.tile([P, M // LIST], U16, name="p1")
        p2 = keep.tile([P, M // LIST], U16, name="p2")
        p3 = keep.tile([P, M // LIST], U16, name="p3")

        tab_s = held([P, T], U8, "tab_s")
        w1_s_raw = held([P, H], U8, "w1_s_raw")
        planes = [held([P, S + H], U8, f"plane{a}") for a in range(2)]
        v_cols, w1_cols = slice(0, S), slice(S, S + H)
        for raw, engine in ((tab_s, nc.vector), (w1_s_raw, nc.gpsimd)):
            for rows in (slice(32, 64), slice(64, P)):
                engine.memset(raw[rows, :].bitcast(I32), 0)
        nc.gpsimd.memset(planes[1][:].bitcast(I32), 0)

        warm = held([P, 2], F32, "warm")
        nc.gpsimd.memset(warm[:, 0:1], 0.0)
        nc.scalar.activation(warm[:, 1:2], warm[:, 0:1], ACT.Sigmoid)

        tab_w = [reused([P, T], I32, f"tab_w{a}", TABLE[a]) for a in range(2)]
        w1_halves = w1_words.rearrange("a p (b c) -> b p a c", b=2)
        w1_raw = [held([P, H], U8, "w1_raw0"), reused([P, H], U8, "w1_raw1", W1_SECOND)]
        nc.sync.dma_start(tab_s[:SCALE_ROWS, :].bitcast(I32), tab_scales.rearrange("a q c -> (a q) c").bitcast(I32))
        nc.sync.dma_start(idx[:], offs)
        nc.sync.dma_start(w1_raw[0][:].bitcast(I32), w1_halves[0][:, 0, :].bitcast(I32))
        nc.sync.dma_start(w1_s_raw[:SCALE_ROWS, :].bitcast(I32), w1_scales.rearrange("a q c -> (a q) c").bitcast(I32))
        nc.sync.dma_start(p1[:], pos1)
        nc.sync.dma_start(tab_w[0][:], tab_words[0].rearrange("p t i -> p (t i)").bitcast(I32))
        for cols in (slice(0, T // 2), slice(T // 2, T)):
            nc.sync.dma_start(tab_w[1][:, cols], tab_words[1].rearrange("p t i -> p (t i)").bitcast(I32)[:, cols])

        v_s_raw = held([P, S], U8, "v_s_raw")
        nc.vector.tensor_copy(v_s_raw[:], tab_s[:].indirect(idx[:]))
        nc.vector.tensor_copy(
            planes[0][:, w1_cols].rearrange("p (b t m) -> p b t m", b=2, t=PACK),
            w1_s_raw[:].rearrange("p (b m t) -> p b t m", b=2, t=PACK),
        )
        nc.vector.tensor_copy(planes[0][:, v_cols].bitcast(I32), v_s_raw[:].bitcast(I32))
        for a in range(2):
            for q in range(4):
                if (a, q) != (0, 0):
                    row = 16 * a + 4 * q
                    queue = nc.gpsimd if (a, q) == (1, 3) else nc.scalar
                    queue.dma_start(
                        planes[a][32 * q : 32 * q + 4, :].bitcast(I32), planes[0][row : row + 4, :].bitcast(I32)
                    )

        v_w = {}

        def gather_table(a, cuts):
            for j0, j1 in zip(cuts, cuts[1:]):
                h = j0 // BANK
                if j0 % BANK == 0:
                    v_w[a, h] = held([P, BANK], I32, f"v_w{a}{h}")
                picked = tab_w[a][:].bitcast(U32).indirect(idx[:, j0 // LIST : j1 // LIST])
                nc.vector.tensor_copy(v_w[a, h][:, j0 - BANK * h : j1 - BANK * h].bitcast(U32), picked)

        w1_w = [reused([P, 2, PACK, 2 * P], U8, "w1_w0", W1_ORDERED), held([P, 2, PACK, 2 * P], U8, "w1_w1")]

        def order_first(a, copy):
            copy(w1_w[0][:, a].bitcast(U16), w1_raw[a][:].bitcast(U16).rearrange("p (m t) -> p t m", t=PACK))

        gather_table(0, (0, BANK, S))
        order_first(0, nc.scalar.copy)
        gather_table(1, (0, QUARTER, BANK, S))
        nc.sync.dma_start(w1_raw[1][:].bitcast(I32), w1_halves[0][:, 1, :].bitcast(I32))
        order_first(1, nc.scalar.copy)

        w2_raw = {key: reused([P, PACK, PASS], F32, f"w2_raw{key[0]}{key[1]}", at) for key, at in W2_RAW.items()}
        rounded = {key: reused([P, PACK, P, PACK], BF16, f"w2_bf{key[0]}{key[1]}", at) for key, at in ROUNDED.items()}

        def load_w2(b, a):
            rows = w2[PASS * a : PASS * (a + 1), PASS * b : PASS * (b + 1)]
            nc.sync.dma_start(w2_raw[b, a][:], rows.rearrange("(p j) c -> p j c", j=PACK))

        load_w2(0, 0)
        w1_late = reused([P, 2, H], U8, "w1_late", W1_LATE)
        nc.sync.dma_start(w1_late[:].bitcast(I32), w1_halves[1].bitcast(I32))
        load_w2(0, 1)
        load_w2(1, 0)
        load_w2(1, 1)
        nc.sync.dma_start(p2[:], pos2)
        nc.sync.dma_start(p3[:], pos3)

        def round_by_gpsimd(b, a, ms=slice(0, P)):
            nc.gpsimd.tensor_scalar(
                rounded[b, a][:, :, ms].rearrange("p t m j -> p m t j"),
                w2_raw[b, a][:].rearrange("p j (m t) -> p m t j", t=PACK)[:, ms],
                1.0, 0.0, ALU.mult, ALU.add,
            )

        def round_by_vector(b, a, ms=slice(0, P)):
            nc.vector.tensor_copy(
                rounded[b, a][:, :, ms].rearrange("p t m j -> p m j t"),
                w2_raw[b, a][:].rearrange("p j (m t) -> p m j t", t=PACK)[:, ms],
            )

        w2_w = {key: held([P, PASS], I32, f"w2_w{key[0]}{key[1]}") for key in W2_RAW if key != (1, 1)}
        w2_w[1, 1] = reused([P, PASS], I32, "w2_w11", LAST_CODES)
        w2_s = {key: held([P, PASS], U8, f"w2_s{key[0]}{key[1]}") for key in W2_RAW}

        def quantize_w2(b, a):
            nc.vector.quantize_mx(
                w2_w[b, a][:].bitcast(FP8X4), w2_s[b, a][:], rounded[b, a][:].rearrange("p t m j -> p (t m j)")
            )

        tiles = [(b, t) for b in range(2) for t in range(PACK)]

        def first_stage(x, j0, j1, words, scales, copy):
            h = j0 // BANK
            acc = free_bank()[:, : j1 - j0]
            for a in range(2):
                nc.tensor.matmul_mx(
                    acc, lhsT=words[a], lhsT_scale=scales[a],
                    rhs=v_w[a, h][:, j0 - BANK * h : j1 - BANK * h].bitcast(FP8X4), rhs_scale=planes[a][:, j0:j1],
                    start=a == 0, stop=a == 1,
                )
            copy(x[:, j0:j1], acc)

        x1 = [reused([P, S], F32, f"x1_{k}", X1_AT[k]) if k in X1_AT else held([P, S], F32, f"x1_{k}") for k in range(8)]
        wide_x2 = {k: reused([P, 2 * S], F32, f"x2_{k}", at) for k, at in WIDE_AT.items()}
        wide_x2.update({k: held([P, 2 * S], F32, f"x2_{k}") for k in (6, 7)})
        x2 = [wide_x2[k] if k in wide_x2 else held([P, S], F32, f"x2_{k}") for k in range(8)]

        def features(k, j0, j1, copy):
            b, t = tiles[k]
            first = S + PASS * b + P * t
            words = [w1_w[b][:, a, t, :].bitcast(FP4X4) for a in range(2)]
            first_stage(x1[k], j0, j1, words, [planes[a][:, first : first + P] for a in range(2)], copy)

        def reflex(k, h, copy):
            b, t = tiles[k]
            cols = slice(P * t, P * (t + 1))
            words = [w2_w[b, a][:, cols].bitcast(FP8X4) for a in range(2)]
            scales = [w2_s[b, a][:, cols] for a in range(2)]
            first_stage(x2[k], BANK * h, BANK * (h + 1), words, scales, copy)

        sig_pairs = [wide_x2[k][:, S:] for k in (6, 7)]
        anc_pairs = [wide_x2[k][:, S:] for k in WIDE_AT]
        sig1 = [reused([P, 2, M], F32, "sig10", LAST_CODES), held([P, 2, M], F32, "sig11")]
        twice = held([P, PACK, M], F32, "twice")
        weighed0 = reused([P, PACK, M], F32, "weighed0", WEIGHED)
        weighed1 = held([P, PACK, M], F32, "weighed1")
        loan = [held([P, PACK, M], F32, "loan0"), reused([P, PACK, M], F32, "loan1", LATE_LOANS)]

        def in_pair(pairs, t):
            return pairs[t // 2][:, M * (t % 2) : M * (t % 2 + 1)]

        def sigmoid(k):
            b, t = tiles[k]
            nc.scalar.activation(sig1[t // 2][:, t % 2, :] if b else in_pair(sig_pairs, t), x1[k][:].indirect(p1[:]), ACT.Sigmoid, scale=2.0)

        def to_tanh(u):
            nc.vector.tensor_scalar(anc_pairs[u], sig_pairs[u], 2.0, -1.0, ALU.mult, ALU.add)

        def weigh(k):
            nc.vector.tensor_tensor(weighed0[:, k, :], x2[k][:].indirect(p2[:]), in_pair(anc_pairs, k), ALU.mult)

        def daughter(k):
            nc.vector.tensor_scalar(twice[:, k - PACK, :], x2[k][:].indirect(p2[:]), 2.0, 0.0, ALU.mult, ALU.add)

        def weigh_late(u):
            pair = slice(2 * u, 2 * u + 2)
            nc.vector.scalar_tensor_tensor(weighed1[:, pair], sig1[u][:], -0.5, twice[:, pair], ALU.add, ALU.mult)

        def borrow(k, m0, m1):
            b, t = tiles[k]
            picked = x2[k][:].indirect(p3[:, m0 // LIST : m1 // LIST])
            nc.scalar.activation(loan[b][:, t, m0:m1], picked, ACT.Copy)

        z_bf, z_w, z_s = {}, {}, {}

        def sum_z(b, m0, m1):
            z_bf[b, m0] = reused([P, m1 - m0, PACK], BF16, f"z_bf{b}{m0}", WEIGHED + 2 * PACK * m0)
            nc.vector.tensor_tensor(
                z_bf[b, m0][:].rearrange("p (c i) t -> p c t i", i=4),
                weighed1[:, :, m0:m1].rearrange("p t (c i) -> p c t i", i=4),
                loan[b][:, :, m0:m1].rearrange("p t (c i) -> p c t i", i=4),
                ALU.add,
            )

        def sum_z_by_gpsimd():
            z_bf[0, 0] = held([P, M, PACK], BF16, "z_bf00")
            nc.gpsimd.tensor_tensor(
                z_bf[0, 0][:].rearrange("p (c i) t -> p c t i", i=4),
                weighed0[:].rearrange("p t (c i) -> p c t i", i=4),
                loan[0][:].rearrange("p t (c i) -> p c t i", i=4),
                ALU.add,
            )

        def quantize_z(b, m0, m1):
            z_w[b, m0] = held([P, m1 - m0], I32, f"z_w{b}{m0}")
            z_s[b, m0] = held([P, m1 - m0], U8, f"z_s{b}{m0}")
            nc.vector.quantize_mx(z_w[b, m0][:].bitcast(FP8X4), z_s[b, m0][:], z_bf[b, m0][:].rearrange("p m t -> p (m t)"))

        sums = {}

        def score_pass(b, m0, m1):
            shared = m0 == HALF
            if b == 0 and shared:
                bank = free_bank()
                sums[m0] = [bank[:, P * c : P * (c + 1)] for c in range(N // P)]
                sums["shared"] = bank[:, :N].rearrange("p (c m) -> p c m", m=P)
            elif b == 0:
                sums[m0] = [free_bank()[:, : m1 - m0] for c in range(N // P)]
            origin = m0 if b else 0
            part = slice(m0 - origin, m1 - origin)
            for c, acc in enumerate(sums[m0]):
                cols = slice(P * c, P * (c + 1))
                nc.tensor.matmul_mx(
                    acc, lhsT=w3_w[:, b, cols].bitcast(FP8X4), lhsT_scale=w1_late[:, b, cols],
                    rhs=z_w[b, origin][:, part].bitcast(FP8X4), rhs_scale=z_s[b, origin][:, part],
                    start=b == 0 and (c == 0 or not shared), stop=b == 1 and (c == N // P - 1 or not shared),
                )

        def score(m0, m1):
            score_pass(1, m0, m1)
            accs = sums[m0]
            y = held([P, N // P, m1 - m0], F32, f"y{m0}")
            if m0 == HALF:
                nc.vector.tensor_tensor(y[:], sums["shared"], prior[:].unsqueeze(2).to_broadcast([P, N // P, P]), ALU.add)
                nc.sync.dma_start(out.rearrange("(c p) m -> p c m", p=P)[:, :, m0:m1], y[:])
                return
            for c, acc in enumerate(accs):
                if c == 1 and m1 == M:
                    nc.vector.tensor_scalar(y[:, c, :], acc, prior[:, c : c + 1], None, ALU.add)
                else:
                    nc.scalar.activation(y[:, c, :], acc, ACT.Identity, bias=prior[:, c : c + 1])
                queue = nc.scalar if c == 2 and m1 == M else nc.sync
                queue.dma_start(out[P * c : P * (c + 1), m0:m1], y[:, c, :])

        by_scalar, by_vector = nc.scalar.copy, nc.vector.tensor_copy

        def whole(stage, k, copy):
            for h in range(2):
                stage(k, h, copy)

        def feature(k, h, copy):
            features(k, BANK * h, BANK * (h + 1), copy)

        for k in range(EARLY):
            features(k, 0, QUARTER, by_scalar)
        for k in range(EARLY):
            features(k, QUARTER, BANK, by_vector if k == 2 else by_scalar)
        round_by_vector(0, 0)
        nc.vector.tensor_copy(
            w1_w[1][:].bitcast(U16), w1_late[:].bitcast(U16).rearrange("p a (m t) -> p a t m", t=PACK)
        )
        for k in range(EARLY - 1):
            feature(k, 1, by_vector if k == 2 else by_scalar)
        sigmoid(0)
        sigmoid(1)
        feature(3, 1, by_scalar)
        sigmoid(2)
        whole(feature, 4, by_scalar)
        sigmoid(3)
        for q in range(4):
            nc.sync.dma_start(
                w1_late[32 * q : 32 * q + 4, :, :N].bitcast(I32),
                w3_scales[:, 4 * q : 4 * q + 4, :].rearrange("a r c -> r a c").bitcast(I32),
            )
        w3_w = reused([P, 2, N], I32, "w3_w", 2 * KB)
        nc.sync.dma_start(w3_w[:], w3_words.rearrange("a p c i -> p a (c i)").bitcast(I32))
        prior = reused([P, N // P], F32, "prior", 5 * KB)
        with nc.allow_non_contiguous_dma(reason="one value of period to a partition"):
            nc.sync.dma_start(prior[:], period.rearrange("(c p) -> p c", p=P))
        quantize_w2(0, 0)
        round_by_vector(0, 1)
        feature(5, 0, by_vector)
        quantize_w2(0, 1)
        round_by_gpsimd(1, 0)
        round_by_gpsimd(1, 1, slice(0, GPSIMD_SHARE))
        feature(5, 1, by_vector)
        for k in (6, 7):
            whole(feature, k, by_vector)
        sigmoid(6)
        sigmoid(7)
        for k in (0, 1):
            whole(reflex, k, by_vector)
        for k in (2, 3):
            whole(reflex, k, by_scalar)
        round_by_vector(1, 1, slice(GPSIMD_SHARE, P))
        quantize_w2(1, 0)
        quantize_w2(1, 1)
        to_tanh(0)
        to_tanh(1)
        for k in range(PACK):
            weigh(k)
        for k in range(PACK):
            borrow(k, 0, M)
        sum_z_by_gpsimd()
        for k in range(PACK, 2 * PACK):
            reflex(k, 0, by_vector if k == PACK + 1 else by_scalar)
            reflex(k, 1, by_scalar)
        sigmoid(4)
        sigmoid(5)
        for k in range(PACK, 2 * PACK):
            daughter(k)
        for start in (0, HALF, HALF + P):
            for k, cuts in LOAN_CUTS.items():
                for m0, m1 in zip(cuts, cuts[1:]):
                    if m0 == start:
                        borrow(k, m0, m1)
        wide, middle, last = CHUNKS
        weigh_late(1)
        weigh_late(0)
        quantize_z(0, 0, M)
        for m0, m1 in CHUNKS:
            score_pass(0, m0, m1)
        sum_z(1, *wide)
        sum_z(1, *middle)
        quantize_z(1, *wide)
        sum_z(1, *last)
        quantize_z(1, *middle)
        quantize_z(1, *last)
        for m0, m1 in CHUNKS:
            score(m0, m1)
